import numpy as np, ml_dtypes
CORES = [16,18,20,22]
N = 4
import mx_ref
BF = ml_dtypes.bfloat16
def entries(a):
    return np.ascontiguousarray(a.T).reshape(-1)
def table(e):
    return np.ascontiguousarray(np.reshape(e, (-1, 16)).T).astype(np.int32)
def pick(q, e):
    c = np.concatenate([q[0].reshape(128, -1, 4), np.zeros((128, 1, 4), np.uint8)], axis=1); s = np.concatenate([q[1], np.ones((16, 1), np.uint8)], axis=1)
    return (np.ascontiguousarray(c[:, e].reshape(128, -1)), np.ascontiguousarray(s[:, e]))
def join(*qs):
    return (np.concatenate([q[0] for q in qs], axis=1), np.concatenate([q[1] for q in qs], axis=1))
def put(q, e, v):
    c, s = q[0].reshape(128, -1, 4).copy(), q[1].copy(); c[:, e] = v[0].reshape(128, -1, 4); s[:, e] = v[1]
    return (c.reshape(128, -1), s)
def pk(c, s):
    return (np.ascontiguousarray(c), mx_ref.live(s))
def emit(q):
    return q[0], q[1]
def cols(t, e):
    v = np.concatenate([t.reshape(128, -1, 4), np.zeros((128, 1, 4), BF)], axis=1)
    return np.ascontiguousarray(v[:, e]).reshape(128, -1)
def cut(t, i, w=512):
    return t[:, w * i:w * i + w]
def f(rng, *shape):
    return mx_ref.flush((rng.standard_normal(shape, dtype=np.float32) * np.exp2(rng.integers(-2, 3, shape[:-1] + (1,)))).astype(BF))
def wide(rng, *shape, cols=0):
    v = rng.standard_normal(shape, dtype=np.float32) * np.exp2(rng.integers(-12, 13, shape)).astype(np.float32)
    if cols: v *= np.repeat(np.exp2(rng.integers(-cols, cols + 1, shape[:-2] + (1, shape[-1] // 4))) * (rng.random(shape[:-2] + (1, shape[-1] // 4)) > 0.0625), 4, axis=-1).astype(np.float32)
    return mx_ref.flush(v.astype(BF))
P, CAPP, LC = 256, 64, 192
def choose(e, g, d):
    c = e[np.arange(P), np.argmax(g[e], axis=1)]
    for s in range(N):
        if s != d:
            late = np.flatnonzero(c // P == s)[CAPP:]
            c[late] = e[late, 0]
    return c
def play(e0, e1, e2, p1, p2, u, a):
    k = [mx_ref.quantize(u[d]) for d in range(N)]
    A = [[mx_ref.quantize(np.ascontiguousarray(cut(a[d], i))) for i in range(4)] for d in range(N)]
    H = [mx_ref.quantize(e0[d]) for d in range(N)]
    g = np.stack([mx_ref.matmul(k[d], H[d])[0] for d in range(N)]) + np.float32(0)
    chosen, tiles, scores = [], [], [g]
    for e, p in ((e1, p1), (e2, p2)):
        every, before = join(*H), g.reshape(-1)
        H, g = [], np.zeros((N, P), np.float32)
        for d in range(N):
            c = choose(entries(p[d]).reshape(P, 4), before, d)
            x = pick(every, c)
            R = np.stack([mx_ref.matmul(A[d][i], x) for i in range(4)], axis=2).reshape(128, 4 * P)
            h = (R * np.float32(0.05) + e[d].astype(np.float32)).astype(BF)
            q = mx_ref.quantize(h)
            g[d] = before[c] + mx_ref.matmul(k[d], q)[0]
            H.append(q)
            chosen.append(c)
            tiles.append(h)
        scores.append(g)
    return np.stack(chosen).reshape(2, N, P), tiles, scores, H
def large(v):
    v = v.astype(np.float32)
    v[np.abs(v) < np.float32(0.03125)] = 0
    return v.astype(BF)
def lean(v, u, s):
    t = np.abs(v.astype(np.float32)).reshape(128, -1, 4) * np.sign(u[:, None, :4].astype(np.float32)) * np.asarray(s, np.float32)[None, :, None]
    return t.reshape(128, -1).astype(BF)
def near(t, u, score):
    size = np.concatenate([[0.0], np.exp2(np.arange(-26, -7))])[:, None] * np.array([1, 1.25, 1.5, 1.75])
    v = np.repeat(t.astype(np.float32).reshape(128, 1, 4), 80, axis=1)
    v[:8] = np.sign(u[:8, None, :4].astype(np.float32)) * size.reshape(1, 80, 1)
    v = np.ascontiguousarray(v.reshape(128, 320).astype(BF))
    s = score(v)
    i = int(np.argmin(np.abs(s - s[0] - np.float32(2.5) * np.spacing(np.abs(s[0])))))
    return cols(v, [0, i])
def strong(u):
    return (u.astype(np.float32) * np.float32(2.0 ** 24)).astype(BF)
def lists(rng):
    out = []
    for d in range(N):
        others = np.delete(np.arange(N), d)
        rank = others[np.argsort(rng.random((P, N - 1)), axis=1)[:, :3]]
        pool = np.stack([rng.permutation(P)[:LC] for s in range(N)])
        e = np.zeros((P, 4), int)
        e[:, 0] = d * P + rng.integers(0, P, P)
        e[:, 1:] = rank * P + pool[rank, rng.integers(0, LC, (P, 3))]
        out.append(table(e.reshape(-1)))
    return np.stack(out)
def crowd(rng, s):
    out, half = [], LC // 2
    for d in range(N):
        x = rng.permutation(np.delete(np.arange(N), d))
        hi = np.stack([rng.permutation(np.flatnonzero(s[r]))[:half] for r in range(N)])
        lo = np.stack([rng.permutation(np.flatnonzero(~s[r]))[:half] for r in range(N)])
        j = rng.permutation(P)
        one, two, home = j[:P // 2], j[P // 2:P // 2 + CAPP], j[P // 2 + CAPP:]
        rank = np.stack([np.full(P, x[0]), np.full(P, x[1]), x[rng.integers(2, N - 1, P)]], axis=1)
        n = rng.integers(0, half, (P, 3))
        n[j, 0] = np.arange(P) % (P // 2) % half
        n[two, 1] = rng.permutation(half)[:CAPP]
        at = lo[rank, n]
        at[one, 0] = hi[x[0], n[one, 0]]
        at[two, 1] = hi[x[1], n[two, 1]]
        e = np.zeros((P, 4), int)
        e[:, 0] = d * P + np.flatnonzero(~s[d])[rng.integers(0, P // 2, P)]
        e[home, 0] = d * P + np.flatnonzero(s[d])[rng.integers(0, P // 2, home.size)]
        e[:, 1:] = rng.permuted(rank * P + at, axis=1)
        out.append(table(e.reshape(-1)))
    return np.stack(out)
def plain(rng):
    u = np.array(f(rng, 128, 512))
    u[:, 4:] = 0
    return {"e0": np.array(f(rng, N, 128, 4 * P)), "e1": large(f(rng, N, 128, 4 * P)), "e2": large(f(rng, N, 128, 4 * P)), "p1": lists(rng), "p2": lists(rng),
            "u": np.stack([u] * N), "a": f(rng, N, 128, 2048), "w": f(rng, N, 128, 512)}
def setup_inputs(rng):
    return plain(rng)
def setup_inputs_full(rng):
    d = plain(rng)
    for e, p, size in (("e0", "p1", 1), ("e1", "p2", 64)):
        s = np.stack([rng.permutation(P) < P // 2 for r in range(N)])
        for r in range(N): d[e][r] = lean(d[e][r], d["u"][r], size * np.where(s[r], 1, -1))
        d[p] = crowd(rng, s)
    return d
def setup_inputs_ties(rng):
    d = plain(rng)
    u, a = np.ascontiguousarray(d["u"][0]), np.array(d["a"][0])
    a.reshape(128, 4, 512)[:, :, :32] = 0
    k = mx_ref.quantize(u)
    def row(t): return mx_ref.matmul(k, mx_ref.quantize(t))[0]
    x = np.concatenate([f(rng, 128, 16), near(lean(f(rng, 128, 4), u, [1]), u, row)], axis=1)
    best = cols(x, [5] * 4)
    top, q = row(best)[0], mx_ref.quantize(best)
    R = np.stack([mx_ref.matmul(mx_ref.quantize(np.ascontiguousarray(cut(a, i))), q)[:, 0] for i in range(4)], axis=1)
    def later(t): return top + row((np.tile(R, 80) * np.float32(0.05) + t.astype(np.float32)).astype(BF))
    z = near(lean(large(f(rng, 128, 4)), u, [8]), u, later)
    d["e0"] = np.stack([cols(x, rng.integers(0, 6, P)) for r in range(N)])
    d["e1"] = np.stack([cols(z, rng.integers(0, 2, P)) for r in range(N)])
    d["a"] = np.stack([a] * N)
    return d
def setup_inputs_own(rng):
    d = plain(rng)
    d["u"] = strong(d["u"])
    best, worst = rng.permutation(N)[:2]
    for r, s in ((best, 1), (worst, -1)):
        d["e0"][r] = lean(d["e0"][r], d["u"][r], np.full(P, 8 * s))
        d["e1"][r] = lean(d["e1"][r], d["u"][r], np.full(P, 256 * s))
    return d
def setup_inputs_flip(rng):
    d = plain(rng)
    d["u"] = strong(d["u"])
    for r in range(N):
        s = rng.permutation(P) % 2 * 2 - 1
        d["e0"][r] = lean(d["e0"][r], d["u"][r], 1024 * s)
        d["e1"][r] = lean(d["e1"][r], d["u"][r], -16384 * s)
    return d
def setup_inputs_spread(rng):
    d = plain(rng)
    d["e0"] = wide(rng, N, 128, 4 * P, cols=4)
    d["e1"] = large(wide(rng, N, 128, 4 * P, cols=4))
    d["e2"] = large(wide(rng, N, 128, 4 * P, cols=4))
    return d
def check_inputs(d):
    b = []
    for k in ("e0", "e1", "e2", "u", "a", "w"):
        v = np.abs(d[k].astype(np.float32))
        if not (np.isfinite(v).all() and ((v == 0) | (v >= 2.0 ** -30) & (v <= 2.0 ** 30)).all()): b.append("a value of " + k)
    u = d["u"].astype(np.float32)
    if (u[:, :, 4:] != 0).any(): b.append("u has numbers behind its column 0")
    if (u != u[:1]).any(): b.append("u isn't the same on all ranks")
    for k in ("p1", "p2"):
        for r in range(N):
            e = entries(d[k][r]).reshape(P, 4)
            if e.min() < 0 or e.max() >= N * P:
                b.append(k + " out of range")
                continue
            o = np.sort(e[:, 1:] // P, axis=1)
            if (e[:, 0] // P != r).any(): b.append(k + ": predecessor 0")
            if (o == r).any() or (o[:, 1:] == o[:, :-1]).any(): b.append(k + ": predecessors 1 to 3")
            if np.bincount(np.unique(e[:, 1:]) // P, minlength=N).max() > LC: b.append(k + ": too many columns of one rank")
    if not b:
        chosen, tiles, scores, H = play(*[d[k] for k in ("e0", "e1", "e2", "p1", "p2", "u", "a")])
        v = np.abs(np.stack(tiles).astype(np.float32))
        if not (np.isfinite(v).all() and ((v == 0) | (v >= 2.0 ** -30) & (v <= 2.0 ** 30)).all()): b.append("a value of h_1 or h_2")
        if not np.isfinite(np.stack(scores)).all(): b.append("a score")
    return b
def reference(e0, e1, e2, p1, p2, u, a, w):
    chosen, tiles, scores, H = play(e0, e1, e2, p1, p2, u, a)
    ch, g = np.zeros((N, 2, P), np.float32), np.zeros((N, 1, P), np.float32)
    oc, osc, y = np.zeros((N, 128, 4 * P), np.uint8), np.zeros((N, 16, P), np.uint8), np.zeros((N, 128, P), np.float32)
    for r in range(N):
        ch[r] = chosen[:, r]
        g[r, 0] = scores[2][r]
        oc[r], osc[r] = emit(H[r])
        y[r] = mx_ref.matmul(mx_ref.quantize(w[r]), H[r])
    return {"ch": ch, "g": g, "oc": oc, "osc": osc, "y": y}

@@ -1,0 +1,509 @@
+from concourse.bass import DstId, RemoteDMATransfer
+from concourse.mybir import dt, AluOpType as A, ActivationFunctionType as AF
+
+P, CAPP = 256, 64
+TINY = 2.0 ** -100
+F, B, I, H, C, S8 = "float32", "bfloat16", "int32", "uint16", "float8_e4m3fn_x4", "uint8"
+SCRATCH = {"PS": ("psum", [128, 4096], F)}
+PLACE = {"PS": ("PS", 0, 4096)}
+
+
+def _buf(dtype, **names):
+    for k, n in names.items():
+        SCRATCH[k] = ("sbuf", [128, n], dtype)
+        PLACE[k] = (k, 0, n)
+
+
+def _area(dtype, **names):
+    k = "W" + dtype
+    for name, n in names.items():
+        at = SCRATCH[k][1][1] if k in SCRATCH else 0
+        PLACE[name] = (k, at, n)
+        SCRATCH[k] = ("sbuf", [128, at + (n + 15) // 16 * 16], dtype)
+
+
+def _each(**names):
+    return {n + str(t): w for t in (1, 2) for n, w in names.items()}
+
+
+_buf(B, UT=512, E0=1024, AT=2048, WT=512, E1=1024, E2=1024, HT1=1024, HT2=1024)
+_buf(C, UQ=128, AQ=512, WQ=128, QO0=256, QO1=256, QO2=256, QW0=448, QW1=448, SQ1=192, SQ2=192, XQ1=256, XQ2=256)
+_buf(S8, UP=128, AP=512, WP=128, QS0=256, QS1=256, QS2=256, QP0=448, QP1=448, SS1=192, SS2=192, XS1=256, XS2=256)
+_buf(H, MSG1=4, MSG2=2, MSG3=6, LM1=12, LM2=6, LM3=18)
+_buf(F, U1=32, U2=32, Z1=1024, Z2=1024, YB=256, S0=256, S1=256, S2=256, PR1=256, PR2=256, PB1=256, PB2=256)
+_buf(I, RAW1=64, RAW2=64)
+_area(H, DUP=8)
+_area(I, PI=1, PJ=4, DUPI=8, TRI=8)
+_area(F, ZERO=64, NEG=8, KCOL=4, P15F=4, P15E=4, XEO=8, GCOL=4, BC=4, TR=8, ZB=368)
+_area(F, **_each(RL=64, RN=64, T2=64, TN=64, M1=32, MN=32, PKA=4, KFN=8, KSC=8, LCN=8, CG=8, LF=8, RB=128, VR=128, KF=32, KL=24,
+                 TK=24, KK=32, G=128, TG=128, V3=24, D=24, D2=24, X1=8, X2=8, LO=8, TB=32, EC=32, LT=8, AA=8, W=640, WD=128,
+                 TW=128, LS=4, M16=16, MM=8, EQ=32, KEY=32, K16=16, KM=8, TB2=32, EC2=32, SV=8, KP=8, VAL=24, BK=72, SA=24,
+                 SB=24, NK=8, OO=16, XC=16, A2=32, TA=32, XT=16, KQ=32, PP=32, P16=16, PA=8))
+_area(I, **_each(TI=64, TJ=64, LW=8, LC=8, WN=8, KN=8, LOC=4, CL=4, LI=8, KC=8, KD=32, LN=8))
+_area(H, **_each(LU=8, OF=8, PO=12, XO=16))
+NDMA = 36
+SEMAPHORES = ["qv", "qa", "qt", "qg", "m3", "lm3"] + ["d%d" % i for i in range(NDMA)] + [
+    x + str(t) for t in (1, 2) for x in ("m", "lm", "v", "lv", "c", "lc", "s", "ls")]
+
+
+def rank_program(g, core, T, topo):
+    me = T.rank_of(core)
+    if me is None:
+        return
+    others = [(me + 1 + i) % 4 for i in range(3)]
+    slot_at = [(me - d) % 4 - 1 for d in others]
+    qs = {"v": g.vector, "a": g.scalar, "t": g.tensor, "g": g, "s": g.sync}
+    hist, know, cnt, total = {}, {q: {} for q in qs}, {}, {}
+
+    def V(name, c0=0, c1=None, st=1, p0=0, p1=128):
+        return (name, p0, p1, c0, PLACE[name][2] if c1 is None else c1, st)
+
+    def blk(k, name, c0=0, c1=None, st=1):
+        return V(name, c0, c1, st, 32 * k, 32 * k + 32)
+
+    def ap(v):
+        name, o, _ = PLACE[v[0]]
+        return T[name][v[1]:v[2], o + v[3]:o + v[4]] if v[5] == 1 else T[name][v[1]:v[2], o + v[3]:o + v[4]:v[5]]
+
+    def clash(a, b):
+        if a[2] <= b[1] or b[2] <= a[1] or a[4] <= b[3] or b[4] <= a[3]:
+            return False
+        return not (a[5] == b[5] and a[5] > 1 and (a[3] - b[3]) % a[5])
+
+    def bank(v):
+        return (v[0], 0, 128, v[3] // 512 * 512, v[3] // 512 * 512 + 512, 1) if v[0] == "PS" else v
+
+    def wait(q, evs):
+        need = {}
+        for sem, val, clock in evs:
+            if know[q].get(sem, 0) < val and need.get(sem, (0, 0))[0] < val:
+                need[sem] = (val, clock)
+        for sem in sorted(need):
+            val, clock = need[sem]
+            if know[q].get(sem, 0) >= val or any(o != sem and need[o][1].get(sem, 0) >= val for o in need):
+                continue
+            qs[q].wait_ge(T.sem[sem], val)
+        for sem in need:
+            for k, n in list(need[sem][1].items()) + [(sem, need[sem][0])]:
+                know[q][k] = max(know[q].get(k, 0), n)
+
+    def use(q, reads, writes):
+        evs = []
+        for r, w in [(bank(v), False) for v in reads] + [(bank(v), True) for v in writes]:
+            evs += [ev for (o, ow, ev) in hist.get(r[0], []) if (w or ow) and clash(r, o)]
+        wait(q, evs)
+
+    def note(q, sem, val, reads, writes):
+        clock = dict(know[q])
+        clock[sem] = val
+        total[sem] = max(total.get(sem, 0), val)
+        for r, w in [(bank(v), False) for v in reads] + [(bank(v), True) for v in writes]:
+            hist.setdefault(r[0], []).append((r, w, (sem, val, clock)))
+        return (sem, val, clock)
+
+    def op(q, call, reads, writes):
+        use(q, reads, writes)
+        cnt[q] = cnt.get(q, 0) + 1
+        call().then_inc(T.sem["q" + q], 1)
+        return note(q, "q" + q, cnt[q], reads, writes)
+
+    def sv(s):
+        return ap(s) if isinstance(s, tuple) else s
+
+    def tc(o, a):
+        op("v", lambda: g.vector.tensor_copy(ap(o), ap(a)), [a], [o])
+
+    def tt(o, a, b, f):
+        op("v", lambda: g.vector.tensor_tensor(ap(o), ap(a), ap(b), f), [a, b], [o])
+
+    def ts(o, a, s1, f1, s2=None, f2=None):
+        rd = [a] + [s for s in (s1, s2) if isinstance(s, tuple)]
+        if f2 is None:
+            op("v", lambda: g.vector.tensor_scalar(ap(o), ap(a), sv(s1), None, f1), rd, [o])
+        else:
+            op("v", lambda: g.vector.tensor_scalar(ap(o), ap(a), sv(s1), sv(s2), f1, f2), rd, [o])
+
+    def scan(o, a, b):
+        op("v", lambda: g.vector.tensor_tensor_scan(ap(o), ap(a), ap(b), 0.0, A.add, A.add), [a, b], [o])
+
+    def tr(o, a):
+        op("v", lambda: g.vector.transpose(ap(o), ap(a)), [a], [o])
+
+    def ms(o, c):
+        op("v", lambda: g.vector.memset(ap(o), c), [], [o])
+
+    def gat(o, w, off):
+        op("v", lambda: g.vector.tensor_copy(ap(o), ap(w).indirect(ap(off))), [w, off], [o])
+
+    def pick(qo, so, qw, sw, off):
+        op("v", lambda: g.vector.tensor_copy(ap(qo).bitcast(dt.uint32), ap(qw).bitcast(dt.uint32).indirect(ap(off))), [qw, off], [qo])
+        op("a", lambda: g.scalar.activation(ap(so), ap(sw).indirect(ap(off)), AF.Copy), [sw, off], [so])
+
+    def qz(q, s, a):
+        op("v", lambda: g.vector.quantize_mx(ap(q), ap(s), ap(a)), [a], [q, s])
+
+    def act(o, a, scale=1.0):
+        op("a", lambda: g.scalar.activation(ap(o), ap(a), AF.Copy, scale=scale), [a], [o])
+
+    def plus(o, a, bias):
+        op("a", lambda: g.scalar.activation(ap(o), ap(a), AF.Identity, bias=ap(bias)), [a, bias], [o])
+
+    def mm(b, n, wq, ws, xq, xs):
+        o = V("PS", 512 * b, 512 * b + n)
+        op("t", lambda: g.tensor.matmul_mx(ap(o), ap(wq), ap(ws), ap(xq), ap(xs), True, True), [wq, ws, xq, xs], [o])
+        return o
+
+    def dma(q, out, in_, reads, writes):
+        use(q, reads, writes)
+        n = cnt.get("dma", 0)
+        cnt["dma"] = n + 1
+        qs[q].dma_start(out, in_).then_inc(T.sem["d%d" % n], 16)
+        return note(q, "d%d" % n, 16, reads, writes)
+
+    def load(q, v, src):
+        return dma(q, ap(v), src, [], [v])
+
+    def mask_of(engines):
+        return sum(1 << e for e in engines)
+
+    def dst(d):
+        rid, pid, _ = topo.addr(T.cores[d])
+        return DstId(rid=rid, pnc=pid)
+
+    def spread(src, land, sem, lsem):
+        use("g", [src], [])
+        e = topo.engines(core, T.cores[others[0]])[:16]
+        g.remote_dma_fused([RemoteDMATransfer(
+            dst_ids=[dst(d) for d in others], dma_engine_mask=mask_of(e), remote_sem=T.sem[sem], srcs=[ap(src)],
+            dsts=[ap(land(s)) for s in slot_at])], local_sem=T.sem[lsem])
+        return note("g", lsem, len(e), [src], [])
+
+    def arrive(sem, n, writes):
+        total[sem] = n
+        for v in writes:
+            hist.setdefault(v[0], []).append((v, True, (sem, n, {sem: n})))
+
+    n16 = len(topo.engines(core, T.cores[others[0]])[:16]) * 3
+    for i in (1, 2, 3):
+        arrive("m%d" % i, n16, [V("LM%d" % i)])
+    for t in (1, 2):
+        arrive("v%d" % t, n16, [V("U%d" % t, 8, 32)])
+        arrive("c%d" % t, 12, [V("QW%d" % (t - 1), 256, 448)])
+        arrive("s%d" % t, 12, [V("QP%d" % (t - 1), 256, 448)])
+
+    def zb(t, o, n):
+        return V("ZB", 184 * (t - 1) + o, 184 * (t - 1) + o + n)
+
+    def sub(v, a, b, k=None):
+        return (v[0], v[1] if k is None else 32 * k, v[2] if k is None else 32 * k + 32, v[3] + a, v[3] + b, 1)
+
+    def bufs(t):
+        return lambda name, *a: V(name + str(t), *a)
+
+    load("s", V("RAW1", p0=0, p1=16), T.p1[:])
+    load("a", V("RAW1", p0=16, p1=32), T.p1[:])
+    load("s", V("E0", 0, 512), T.e0[:, 0:512])
+    load("a", V("UT", 0, 4), T.u[:, 0:4])
+    load("a", V("E0", 512, 1024), T.e0[:, 512:1024])
+    load("s", V("RAW2", p0=0, p1=16), T.p2[:])
+    load("a", V("RAW2", p0=16, p1=32), T.p2[:])
+    op("g", lambda: g.iota(ap(V("PI")), [[0, 1]], 0, 1), [], [V("PI")])
+    op("g", lambda: g.iota(ap(V("DUPI")), [[16, 4], [0, 2]], 0, 0), [], [V("DUPI")])
+    op("g", lambda: g.iota(ap(V("TRI")), [[1, 8]], 257, 0), [], [V("TRI")])
+    ms(V("ZERO"), 0.0)
+    for j, m in enumerate((3, 15, 1, 96)):
+        ts(V("PJ", j, j + 1), V("PI"), m, A.bitwise_and)
+    kcol, p15 = V("KCOL", 0, 1), V("P15F", 0, 1)
+    tc(kcol, V("PJ", 0, 1))
+    tc(p15, V("PJ", 1, 2))
+    ts(V("P15E", 0, 1), p15, 8.0, A.mult)
+    tc(V("XEO", 4, 5), V("PJ", 2, 3))
+    ts(V("XEO", 0, 1), V("XEO", 4, 5), -1.0, A.mult, 1.0, A.add)
+    ts(V("GCOL", 0, 1), V("PJ", 3, 4), 8.0, A.mult)
+    ts(V("DUP"), V("DUPI"), p15, A.add)
+    ts(V("TR"), V("TRI"), V("P15E", 0, 1), A.add)
+    ms(V("NEG"), -1.0)
+    for k in range(4):
+        ms(blk(k, "BC", 0, 1), float(255 + 64 * others.index(k)) if k != me else 0.0)
+    ms(V("ZB"), 0.0)
+    for t in (1, 2):
+        ms(V("W%d" % t, 0, 64), 0.0)
+
+    def prep_lists(t, pk):
+        b = bufs(t)
+        for s in range(4):
+            ts(blk(s, "TI%d" % t), V("RAW%d" % t, p0=0, p1=32), 1024 - 256 * s, A.add)
+        ts(b("TJ"), b("TI"), 1023, A.bitwise_and)
+        for gg in range(2):
+            for h in range(2):
+                ts(b("RL", 32 * gg + 16 * h, 32 * gg + 16 * h + 16), b("TJ", 32 * gg + h, 32 * gg + 32, 2), 4.0, A.mult, kcol, A.add)
+        tr(b("T2"), b("RL"))
+        tt(b("M1"), b("T2", 0, 64, 2), b("T2", 1, 64, 2), A.min)
+        for gg in range(2):
+            tt(b("LW", gg, 8, 2), b("M1", 16 * gg, 16 * gg + 8, 2), b("M1", 16 * gg + 1, 16 * gg + 8, 2), A.min)
+        ts(b("LC"), b("LW"), 2, A.logical_shift_right)
+        ts(b("PKA"), b("LC", 4, 8), 256.0, A.mult)
+        tt(b("LOC"), b("PKA"), b("LC", 0, 4), A.add)
+        tc(pk, b("LOC"))
+
+    def prep_nodes(t, kcols):
+        b = bufs(t)
+        for h in range(2):
+            ts(b("RN", 32 * h, 32 * h + 32), b("TJ", h, 64, 2), 4.0, A.mult, kcol, A.add)
+        tr(b("TN"), b("RN"))
+        tt(b("MN"), b("TN", 0, 64, 2), b("TN", 1, 64, 2), A.min)
+        for h in range(2):
+            tt(b("WN", 4 * h, 4 * h + 4), b("MN", 16 * h, 16 * h + 8, 2), b("MN", 16 * h + 1, 16 * h + 8, 2), A.min)
+        ts(b("KN"), b("WN"), 3, A.bitwise_and)
+        ts(b("KSC", 0, 2), b("KN", 0, 8, 4), 4.0, A.mult)
+        for i in (1, 2, 3):
+            tt(b("KFN", 2 * i, 2 * i + 2), b("KSC", 2 * i - 2, 2 * i), b("KN", i, 8, 4), A.add)
+            if i < 3:
+                ts(b("KSC", 2 * i, 2 * i + 2), b("KFN", 2 * i, 2 * i + 2), 4.0, A.mult)
+        tc(kcols, b("KFN", 6, 8))
+
+    def own_columns(t):
+        b = bufs(t)
+        ts(b("LN"), b("WN"), 2, A.logical_shift_right)
+        tc(b("LCN"), b("LN"))
+        plus(b("CG"), b("LCN"), V("GCOL", 0, 1))
+
+    def packed(t, d):
+        if d == me:
+            return blk(me, "MSG1") if t == 1 else blk(me, "MSG3", 0, 4)
+        i = others.index(d)
+        return blk(me, "LM1", 4 * i, 4 * i + 4) if t == 1 else blk(me, "LM3", 6 * i, 6 * i + 4)
+
+    def ties(t, d):
+        if d == me:
+            return V("MSG2") if t == 1 else V("MSG3", 4, 6)
+        i = others.index(d)
+        return V("LM2", 2 * i, 2 * i + 2) if t == 1 else V("LM3", 6 * i + 4, 6 * i + 6)
+
+    def decode_lists(t):
+        b = bufs(t)
+        for d in range(4):
+            tc(blk(d, "CL%d" % t), packed(t, d))
+        ts(b("LI", 0, 4), b("CL"), 255, A.bitwise_and)
+        ts(b("LI", 4, 8), b("CL"), 8, A.logical_shift_right)
+        tc(b("LU"), b("LI"))
+
+    def value_rows(t):
+        b = bufs(t)
+        tc(b("LF"), b("LI"))
+        for c in range(8):
+            plus(b("RB", 16 * c, 16 * c + 16), V("ZERO", 0, 16), b("LF", c, c + 1))
+        for i in range(3):
+            act(b("V3", 8 * i, 8 * i + 8), b("U", 0, 8))
+
+    def decode_ties(t):
+        b = bufs(t)
+        for d in range(4):
+            tc(b("KC", 2 * d, 2 * d + 2), ties(t, d))
+        for i in range(4):
+            ts(b("KD", i, 32, 4), b("KC"), 2 * (3 - i), A.logical_shift_right, 3, A.bitwise_and)
+        tc(b("KF"), b("KD"))
+        ka = zb(t, 144, 32)
+        for d in range(4):
+            for s in range(4):
+                if s != d:
+                    i = (s - me) % 4
+                    act(sub(ka, 8 * i, 8 * i + 8, d), blk(s, "KF%d" % t, 8 * d, 8 * d + 8))
+        tr(b("VR"), b("RB"))
+        for i in range(3):
+            tt(b("KL", 8 * i, 8 * i + 8), sub(ka, 8 * i + 8, 8 * i + 16), sub(ka, 0, 8), A.is_lt)
+        act(b("TK"), b("KL"), TINY)
+        ts(b("KK"), ka, -1.0, A.mult, 4.0, A.add)
+
+    def scores_out(t):
+        b = bufs(t)
+        gat(b("G"), V("S%d" % (t - 1)), b("LU"))
+        tr(b("TG"), b("G"))
+        tc(b("U", 0, 4), b("TG", 0, 128, 32))
+        tc(b("U", 4, 8), b("TG", 16, 128, 32))
+        return spread(b("U", 0, 8), lambda s: b("U", 8 + 8 * s, 16 + 8 * s), "v%d" % t, "lv%d" % t)
+
+    def prefix(x, add, ni, eb, tb, ec):
+        scan(sub(ni, 0, 8), x, add)
+        tr(tb, ni)
+        scan(sub(eb, 1, 33), tb, V("ZERO", 0, 32))
+        tr(ec, sub(eb, 0, 32))
+
+    def choose_and_send(t):
+        b = bufs(t)
+        tt(b("D"), b("U", 8, 32), b("V3"), A.subtract)
+        tt(b("D2"), b("D"), b("TK"), A.add)
+        tt(b("X1"), b("D2", 0, 8), b("D2", 8, 16), A.max)
+        tt(b("X2"), b("X1"), b("D2", 16, 24), A.max)
+        ts(b("LO"), b("X2"), 0.0, A.is_gt)
+        ni = zb(t, 0, 32)
+        prefix(b("LO"), V("NEG"), ni, zb(t, 64, 40), b("TB"), b("EC"))
+        tt(b("LT"), b("LO"), V("TR"), A.mult)
+        tt(b("AA"), b("LT"), sub(ni, 0, 8), A.subtract)
+        for h in range(2):
+            ts(b("OF", h, 8, 2), b("AA", 4 * h, 4 * h + 4), b("EC", 7, 8), A.subtract, -1.0, A.add)
+        op("v", lambda: g.vector.tensor_copy(ap(b("W")).indirect(ap(b("OF"))), ap(b("VR"))), [b("VR"), b("OF")], [b("W")])
+        gat(b("WD"), b("W", 0, 64), V("DUP"))
+        tr(b("TW"), b("WD"))
+        tt(b("LS"), b("TW", 0, 128, 32), b("TW", 16, 128, 32), A.add)
+        cols = {d: (4 * i, 4 * i + 4) for i, d in enumerate(others)}
+        for d in others:
+            for k in (d // 2 * 2, d // 2 * 2 + 1):
+                tc(blk(k, "PO%d" % t, *cols[d]), blk(d, "LS%d" % t))
+        for half in range(2):
+            runs = sorted(cols[d] for d in others if d // 2 == half)
+            if len(runs) == 2 and runs[0][1] == runs[1][0]:
+                runs = [(runs[0][0], runs[1][1])]
+            for lo, hi in runs:
+                tc(V("PO%d" % t, lo, hi, 1, 64 - 64 * half, 128 - 64 * half), V("PO%d" % t, lo, hi, 1, 64 * half, 64 * half + 64))
+        pick(b("SQ"), b("SS"), V("QO%d" % (t - 1)), V("QS%d" % (t - 1)), b("PO"))
+        ev = None
+        for src, land, sem, turn in (("SQ", "QW", "c", 0), ("SS", "QP", "s", 3)):
+            use("g", [b(src)], [])
+            trs = []
+            for i, d in enumerate(others):
+                e = topo.engines(core, T.cores[d])
+                j = 4 * ((i + turn) % 4)
+                a, z = b(src, 64 * i, 64 * i + 64), V(land + str(t - 1), 256 + 64 * slot_at[i], 320 + 64 * slot_at[i])
+                trs.append(RemoteDMATransfer(
+                    dst_ids=[dst(d)], dma_engine_mask=mask_of(e[j:j + 4]), remote_sem=T.sem[sem + str(t)],
+                    srcs=[ap(a).bitcast(dt.uint8) if src == "SQ" else ap(a)], dsts=[ap(z).bitcast(dt.uint8) if src == "SQ" else ap(z)]))
+            g.remote_dma_fused(trs, local_sem=T.sem["l" + sem + str(t)])
+            ev = note("g", "l" + sem + str(t), 12, [b(src)], [])
+        return ev
+
+    def own_list(t):
+        b = bufs(t)
+        mk = lambda name, *a: blk(me, name + str(t), *a)
+        tt(b("M16"), b("U", 0, 16), b("U", 16, 32), A.max)
+        tt(b("MM"), b("M16", 0, 8), b("M16", 8, 16), A.max)
+        for i in range(4):
+            tt(b("EQ", 8 * i, 8 * i + 8), b("U", 8 * i, 8 * i + 8), b("MM"), A.is_equal)
+        tt(b("KEY"), b("EQ"), b("KK"), A.mult)
+        tt(b("K16"), b("KEY", 0, 16), b("KEY", 16, 32), A.max)
+        tt(b("KM"), b("K16", 0, 8), b("K16", 8, 16), A.max)
+        wb, i2 = zb(t, 176, 8), zb(t, 32, 32)
+        for i, s in enumerate(others):
+            tt(sub(wb, 0, 8, s), mk("KEY", 8 * i + 8, 8 * i + 16), mk("KM"), A.is_equal)
+        prefix(wb, V("ZERO", 0, 8), i2, zb(t, 104, 40), b("TB2"), b("EC2"))
+        ts(b("KP"), sub(i2, 0, 8), b("EC2", 7, 8), A.add, float(CAPP), A.is_le)
+        ts(b("SV"), sub(i2, 0, 8), b("EC2", 7, 8), A.add, V("BC", 0, 1), A.add)
+        keep = b("VAL", 16, 24)
+        tt(keep, b("KP"), wb, A.mult)
+        tt(b("VAL", 0, 8), keep, b("SV"), A.mult)
+        tt(b("VAL", 8, 16), keep, b("CG"), A.mult)
+        for i, s in enumerate(others):
+            tc(mk("BK", 24 * i, 24 * i + 24), blk(s, "VAL%d" % t))
+            act(mk("KQ", 8 * i + 8, 8 * i + 16), mk("BK", 24 * i + 16, 24 * i + 24))
+        tt(mk("SA"), mk("BK", 0, 24), mk("BK", 24, 48), A.add)
+        tt(mk("SB"), mk("SA"), mk("BK", 48, 72), A.add)
+        ts(mk("KQ", 0, 8), mk("SB", 16, 24), -1.0, A.mult, 1.0, A.add)
+        tt(mk("OO", 0, 8), mk("KQ", 0, 8), mk("LCN"), A.mult)
+        tt(mk("XC", 0, 8), mk("SB", 0, 8), mk("OO", 0, 8), A.add)
+        for j in range(2):
+            ts(mk("A2", 8 * j, 8 * j + 8), mk("XC", 0, 8), blk(me, "XEO", 4 * j, 4 * j + 1), A.mult)
+        tc(mk("A2", 16, 32), mk("A2", 0, 16))
+        tr(mk("TA"), mk("A2"))
+        tt(mk("XT"), mk("TA", 0, 32, 2), mk("TA", 1, 32, 2), A.add)
+        half = me // 2
+        for k in (2 * half, 2 * half + 1):
+            tc(blk(k, "XO%d" % t), mk("XT"))
+        tc(V("XO%d" % t, p0=64 - 64 * half, p1=128 - 64 * half), V("XO%d" % t, p0=64 * half, p1=64 * half + 64))
+        tt(mk("PP"), mk("KQ"), mk("U"), A.mult)
+        tt(mk("P16"), mk("PP", 0, 16), mk("PP", 16, 32), A.add)
+        tt(mk("PA"), mk("P16", 0, 8), mk("P16", 8, 16), A.add)
+        pr = V("PR%d" % t, 0, 256, 1, 0, 1)
+        dma("s", ap(pr), ap(mk("PA")), [mk("PA")], [pr])
+        op("g", lambda: g.partition_broadcast(ap(b("PB")), ap(pr), 128), [pr], [b("PB")])
+
+    def own_numbers(t):
+        mk = lambda name, *a: blk(me, name + str(t), *a)
+        tt(mk("OO", 8, 16), mk("KQ", 0, 8), mk("CG"), A.mult)
+        tt(mk("XC", 8, 16), mk("SB", 8, 16), mk("OO", 8, 16), A.add)
+        dma("s", T.ch[t - 1:t, :], ap(mk("XC", 8, 16)), [mk("XC", 8, 16)], [])
+
+    def new_columns(t, meanwhile):
+        b = bufs(t)
+        for f in range(2):
+            lo, hi = 128 * f, 128 * f + 128
+            pick(b("XQ", lo, hi), b("XS", lo, hi), V("QW%d" % (t - 1)), V("QP%d" % (t - 1)), b("XO", 8 * f, 8 * f + 8))
+        meanwhile()
+        rs = {}
+        for f in range(2):
+            for i in range(4):
+                rs[f, i] = mm(4 * f + i, 128, V("AQ", 128 * i, 128 * i + 128), V("AP", 128 * i, 128 * i + 128),
+                              b("XQ", 128 * f, 128 * f + 128), b("XS", 128 * f, 128 * f + 128))
+        for f in range(2):
+            for i in range(4):
+                act(b("Z", 512 * f + 128 * i, 512 * f + 128 * i + 128), rs[f, i], 0.05)
+        for f in range(2):
+            lo, hi = 128 * f, 128 * f + 128
+            for i in range(4):
+                tt(b("HT", 512 * f + i, 512 * f + 512, 4), b("Z", 512 * f + 128 * i, 512 * f + 128 * i + 128),
+                   V("E%d" % t, 512 * f + i, 512 * f + 512, 4), A.add)
+            qz(V("QO%d" % t, lo, hi), V("QS%d" % t, lo, hi), b("HT", 512 * f, 512 * f + 512))
+            rs[f] = mm(f, 128, V("UQ"), V("UP"), V("QO%d" % t, lo, hi), V("QS%d" % t, lo, hi))
+            if t == 2:
+                yp = mm(2 + f, 128, V("WQ"), V("WP"), V("QO2", lo, hi), V("QS2", lo, hi))
+                dma("s", T.oc[:, 4 * lo:4 * hi], ap(V("QO2", lo, hi)).bitcast(dt.uint8), [V("QO2", lo, hi)], [])
+                for k in range(4):
+                    sc = V("QS2", lo, hi, 1, 32 * k, 32 * k + 4)
+                    dma("s" if f == 0 or k < 2 else "a", T.osc[4 * k:4 * k + 4, lo:hi], ap(sc), [sc], [])
+                act(V("YB", lo, hi), yp)
+                dma("a", T.y[:, lo:hi], ap(V("YB", lo, hi)), [V("YB", lo, hi)], [])
+        for f in range(2):
+            tt(V("S%d" % t, 128 * f, 128 * f + 128), rs[f], b("PB", 128 * f, 128 * f + 128), A.add)
+        if t == 2:
+            row = V("S2", 0, 256, 1, 0, 1)
+            dma("s", T.g[:], ap(row), [row], [])
+
+    def quantise_a(i):
+        qz(V("AQ", 128 * i, 128 * i + 128), V("AP", 128 * i, 128 * i + 128), V("AT", 512 * i, 512 * i + 512))
+
+    prep_lists(1, V("MSG1"))
+    ev = spread(V("MSG1"), lambda s: V("LM1", 4 * s, 4 * s + 4), "m1", "lm1")
+    wait("s", [ev])
+    for i in (0, 1):
+        load("s", V("AT", 1024 * i, 1024 * i + 1024), T.a[:, 1024 * i:1024 * i + 1024])
+    w = 4
+    while w < 512:
+        act(V("UT", w, 2 * w), V("UT", 0, w))
+        w *= 2
+    qz(V("UQ"), V("UP"), V("UT"))
+    qz(V("QO0"), V("QS0"), V("E0"))
+    ps = mm(0, 256, V("UQ"), V("UP"), V("QO0"), V("QS0"))
+    act(V("S0"), ps)
+    prep_nodes(1, V("MSG2"))
+    spread(V("MSG2"), lambda s: V("LM2", 2 * s, 2 * s + 2), "m2", "lm2")
+    prep_lists(2, V("MSG3", 0, 4))
+    decode_lists(1)
+    ev = scores_out(1)
+    wait("s", [ev])
+    load("s", V("E1"), T.e1[:])
+    prep_nodes(2, V("MSG3", 4, 6))
+    spread(V("MSG3"), lambda s: V("LM3", 6 * s, 6 * s + 6), "m3", "lm3")
+    value_rows(1)
+    decode_ties(1)
+    own_columns(1)
+    qz(V("QW0", 0, 256), V("QP0", 0, 256), V("E0"))
+    quantise_a(0)
+    quantise_a(1)
+    ev = choose_and_send(1)
+    wait("s", [ev])
+    load("s", V("E2"), T.e2[:])
+    load("s", V("WT"), T.w[:])
+    own_list(1)
+    quantise_a(2)
+    quantise_a(3)
+    new_columns(1, lambda: (own_numbers(1), decode_lists(2)))
+    scores_out(2)
+    value_rows(2)
+    decode_ties(2)
+    own_columns(2)
+    qz(V("QW1", 0, 256), V("QP1", 0, 256), V("HT1"))
+    qz(V("WQ"), V("WP"), V("WT"))
+    choose_and_send(2)
+    own_list(2)
+    new_columns(2, lambda: own_numbers(2))
+    for sem in sorted(total):
+        wait("s", [(sem, total[sem], {})])

@@ -3,6 +3,7 @@ from concourse.mybir import dt, AluOpType as A, ActivationFunctionType as AF
 
 P, CAPP = 256, 64
 TINY = 2.0 ** -100
+STEP = 2.0 ** -24 * (1 + 2.0 ** -10)
 F, B, I, H, C, S8 = "float32", "bfloat16", "int32", "uint16", "float8_e4m3fn_x4", "uint8"
 SCRATCH = {"PS": ("psum", [128, 4096], F)}
 PLACE = {"PS": ("PS", 0, 4096)}
@@ -34,12 +35,13 @@ _buf(F, U1=32, U2=32, Z1=1024, Z2=1024, YB=256, S0=256, S1=256, S2=256, PR1=256,
 _buf(I, RAW1=64, RAW2=64)
 _area(H, DUP=8)
 _area(I, PI=1, PJ=4, DUPI=8, TRI=8)
-_area(F, ZERO=64, NEG=8, KCOL=4, P15F=4, P15E=4, XEO=8, GCOL=4, BC=4, TR=8, ZB=368)
-_area(F, **_each(RL=64, RN=64, T2=64, TN=64, M1=32, MN=32, PKA=4, KFN=8, KSC=8, LCN=8, CG=8, LF=8, RB=128, VR=128, KF=32, KL=24,
-                 TK=24, KK=32, G=128, TG=128, V3=24, D=24, D2=24, X1=8, X2=8, LO=8, TB=32, EC=32, LT=8, AA=8, W=640, WD=128,
-                 TW=128, LS=4, M16=16, MM=8, EQ=32, KEY=32, K16=16, KM=8, TB2=32, EC2=32, SV=8, KP=8, VAL=24, BK=72, SA=24,
-                 SB=24, NK=8, OO=16, XC=16, A2=32, TA=32, XT=16, KQ=32, PP=32, P16=16, PA=8))
-_area(I, **_each(TI=64, TJ=64, LW=8, LC=8, WN=8, KN=8, LOC=4, CL=4, LI=8, KC=8, KD=32, LN=8))
+_area(F, ZERO=64, NEG=8, KCOL=4, P15F=4, P15E=4, XEO=8, GCOL=4, BC=4, TR=8, ZB=368, HI=4, HJ=4)
+_area(F, **_each(RL=64, RN=64, T2=64, TN=64, M1=32, MN=32, LW=8, LOC=4, KFN=8, KSC=8, LCN=8, OL=8, OB=8, CD=8, CG=8, LF=8, RB=128,
+                 VR=128, KF=32, KL=24, KK=32, G=128, TG=128, V3=24, AB=24, AC=24, DE=24, VA=24, L3=24, X1=8, LO=8, TB=32, EC=32,
+                 LT=8, AA=8, W=640, WD=128, TW=128, LS=4, M16=16, MM=8, EQ=32, KEY=32, K16=16, KM=8, TB2=32, EC2=32, SV=8, NW=8,
+                 NP=8, BP=8, VAL=24, BK=72, SA=24, SB=8, KS=8, CA=8, CO=8, CH=8, XC=8, A2=32, TA=32, XT=16, KQ=32, PP=32, P16=16,
+                 PA=8))
+_area(I, **_each(TI=64, TJ=64, WN=8, KN=8, CL=4, LI=8, KC=8, KD=32, LN=8))
 _area(H, **_each(LU=8, OF=8, PO=12, XO=16))
 NDMA = 36
 SEMAPHORES = ["qv", "qa", "qt", "qg", "m3", "lm3"] + ["d%d" % i for i in range(NDMA)] + [
@@ -211,15 +213,17 @@ def rank_program(g, core, T, topo):
     op("g", lambda: g.iota(ap(V("DUPI")), [[16, 4], [0, 2]], 0, 0), [], [V("DUPI")])
     op("g", lambda: g.iota(ap(V("TRI")), [[1, 8]], 257, 0), [], [V("TRI")])
     ms(V("ZERO"), 0.0)
-    for j, m in enumerate((3, 15, 1, 96)):
+    for j, m in enumerate((15, 3, 1, 96)):
         ts(V("PJ", j, j + 1), V("PI"), m, A.bitwise_and)
-    kcol, p15 = V("KCOL", 0, 1), V("P15F", 0, 1)
-    tc(kcol, V("PJ", 0, 1))
-    tc(p15, V("PJ", 1, 2))
-    ts(V("P15E", 0, 1), p15, 8.0, A.mult)
+    p15, kcol = V("P15F", 0, 1), V("KCOL", 0, 1)
+    tc(p15, V("PJ", 0, 1))
+    tc(kcol, V("PJ", 1, 2))
+    ts(V("HJ", 0, 1), p15, 8.0, A.is_ge, 255.0, A.mult)
     tc(V("XEO", 4, 5), V("PJ", 2, 3))
-    ts(V("XEO", 0, 1), V("XEO", 4, 5), -1.0, A.mult, 1.0, A.add)
     ts(V("GCOL", 0, 1), V("PJ", 3, 4), 8.0, A.mult)
+    ts(V("HI", 0, 1), V("HJ", 0, 1), 1.0, A.add)
+    ts(V("P15E", 0, 1), p15, 8.0, A.mult)
+    ts(V("XEO", 0, 1), V("XEO", 4, 5), -1.0, A.mult, 1.0, A.add)
     ts(V("DUP"), V("DUPI"), p15, A.add)
     ts(V("TR"), V("TRI"), V("P15E", 0, 1), A.add)
     ms(V("NEG"), -1.0)
@@ -236,14 +240,12 @@ def rank_program(g, core, T, topo):
         ts(b("TJ"), b("TI"), 1023, A.bitwise_and)
         for gg in range(2):
             for h in range(2):
-                ts(b("RL", 32 * gg + 16 * h, 32 * gg + 16 * h + 16), b("TJ", 32 * gg + h, 32 * gg + 32, 2), 4.0, A.mult, kcol, A.add)
+                ts(b("RL", 32 * gg + 16 * h, 32 * gg + 16 * h + 16), b("TJ", 32 * gg + h, 32 * gg + 32, 2), V("HI", 0, 1), A.mult)
         tr(b("T2"), b("RL"))
         tt(b("M1"), b("T2", 0, 64, 2), b("T2", 1, 64, 2), A.min)
         for gg in range(2):
             tt(b("LW", gg, 8, 2), b("M1", 16 * gg, 16 * gg + 8, 2), b("M1", 16 * gg + 1, 16 * gg + 8, 2), A.min)
-        ts(b("LC"), b("LW"), 2, A.logical_shift_right)
-        ts(b("PKA"), b("LC", 4, 8), 256.0, A.mult)
-        tt(b("LOC"), b("PKA"), b("LC", 0, 4), A.add)
+        tt(b("LOC"), b("LW", 0, 4), b("LW", 4, 8), A.add)
         tc(pk, b("LOC"))
 
     def prep_nodes(t, kcols):
@@ -266,7 +268,12 @@ def rank_program(g, core, T, topo):
         b = bufs(t)
         ts(b("LN"), b("WN"), 2, A.logical_shift_right)
         tc(b("LCN"), b("LN"))
-        plus(b("CG"), b("LCN"), V("GCOL", 0, 1))
+        for k in [me] + others:
+            act(blk(k, "OL%d" % t), blk(me, "LCN%d" % t))
+        ts(blk(me, "CO%d" % t), blk(me, "LCN%d" % t), float(P * me), A.add)
+        ts(b("OB"), b("OL"), -1.0, A.mult, V("BC", 0, 1), A.add)
+        tt(b("CD"), b("LCN"), b("OL"), A.subtract)
+        ts(b("CG"), b("CD"), V("GCOL", 0, 1), A.add, float(-P * me), A.add)
 
     def packed(t, d):
         if d == me:
@@ -282,7 +289,7 @@ def rank_program(g, core, T, topo):
 
     def decode_lists(t):
         b = bufs(t)
-        for d in range(4):
+        for d in [me] + others:
             tc(blk(d, "CL%d" % t), packed(t, d))
         ts(b("LI", 0, 4), b("CL"), 255, A.bitwise_and)
         ts(b("LI", 4, 8), b("CL"), 8, A.logical_shift_right)
@@ -291,10 +298,11 @@ def rank_program(g, core, T, topo):
     def value_rows(t):
         b = bufs(t)
         tc(b("LF"), b("LI"))
-        for c in range(8):
-            plus(b("RB", 16 * c, 16 * c + 16), V("ZERO", 0, 16), b("LF", c, c + 1))
         for i in range(3):
             act(b("V3", 8 * i, 8 * i + 8), b("U", 0, 8))
+        op("a", lambda: g.scalar.activation(ap(b("AB")), ap(b("V3")), AF.Abs, scale=STEP), [b("V3")], [b("AB")])
+        for c in range(8):
+            plus(b("RB", 16 * c, 16 * c + 16), V("ZERO", 0, 16), b("LF", c, c + 1))
 
     def decode_ties(t):
         b = bufs(t)
@@ -309,11 +317,17 @@ def rank_program(g, core, T, topo):
                 if s != d:
                     i = (s - me) % 4
                     act(sub(ka, 8 * i, 8 * i + 8, d), blk(s, "KF%d" % t, 8 * d, 8 * d + 8))
+        ts(b("AC"), b("AB"), TINY, A.add)
         tr(b("VR"), b("RB"))
+
+    def ties_end(t):
+        b = bufs(t)
+        ka = zb(t, 144, 32)
         for i in range(3):
             tt(b("KL", 8 * i, 8 * i + 8), sub(ka, 8 * i + 8, 8 * i + 16), sub(ka, 0, 8), A.is_lt)
-        act(b("TK"), b("KL"), TINY)
         ts(b("KK"), ka, -1.0, A.mult, 4.0, A.add)
+        tt(b("DE"), b("AC"), b("KL"), A.mult)
+        tt(b("VA"), b("V3"), b("DE"), A.subtract)
 
     def scores_out(t):
         b = bufs(t)
@@ -323,23 +337,22 @@ def rank_program(g, core, T, topo):
         tc(b("U", 4, 8), b("TG", 16, 128, 32))
         return spread(b("U", 0, 8), lambda s: b("U", 8 + 8 * s, 16 + 8 * s), "v%d" % t, "lv%d" % t)
 
-    def prefix(x, add, ni, eb, tb, ec):
+    def prefix(x, add, ni, eb, tb, ec, one, two):
         scan(sub(ni, 0, 8), x, add)
+        one()
         tr(tb, ni)
+        two()
         scan(sub(eb, 1, 33), tb, V("ZERO", 0, 32))
         tr(ec, sub(eb, 0, 32))
 
     def choose_and_send(t):
         b = bufs(t)
-        tt(b("D"), b("U", 8, 32), b("V3"), A.subtract)
-        tt(b("D2"), b("D"), b("TK"), A.add)
-        tt(b("X1"), b("D2", 0, 8), b("D2", 8, 16), A.max)
-        tt(b("X2"), b("X1"), b("D2", 16, 24), A.max)
-        ts(b("LO"), b("X2"), 0.0, A.is_gt)
+        tt(b("L3"), b("U", 8, 32), b("VA"), A.is_gt)
+        tt(b("X1"), b("L3", 0, 8), b("L3", 8, 16), A.max)
+        tt(b("LO"), b("X1"), b("L3", 16, 24), A.max)
         ni = zb(t, 0, 32)
-        prefix(b("LO"), V("NEG"), ni, zb(t, 64, 40), b("TB"), b("EC"))
-        tt(b("LT"), b("LO"), V("TR"), A.mult)
-        tt(b("AA"), b("LT"), sub(ni, 0, 8), A.subtract)
+        prefix(b("LO"), V("NEG"), ni, zb(t, 64, 40), b("TB"), b("EC"),
+               lambda: tt(b("LT"), b("LO"), V("TR"), A.mult), lambda: tt(b("AA"), b("LT"), sub(ni, 0, 8), A.subtract))
         for h in range(2):
             ts(b("OF", h, 8, 2), b("AA", 4 * h, 4 * h + 4), b("EC", 7, 8), A.subtract, -1.0, A.add)
         op("v", lambda: g.vector.tensor_copy(ap(b("W")).indirect(ap(b("OF"))), ap(b("VR"))), [b("VR"), b("OF")], [b("W")])
@@ -385,42 +398,43 @@ def rank_program(g, core, T, topo):
         wb, i2 = zb(t, 176, 8), zb(t, 32, 32)
         for i, s in enumerate(others):
             tt(sub(wb, 0, 8, s), mk("KEY", 8 * i + 8, 8 * i + 16), mk("KM"), A.is_equal)
-        prefix(wb, V("ZERO", 0, 8), i2, zb(t, 104, 40), b("TB2"), b("EC2"))
-        ts(b("KP"), sub(i2, 0, 8), b("EC2", 7, 8), A.add, float(CAPP), A.is_le)
-        ts(b("SV"), sub(i2, 0, 8), b("EC2", 7, 8), A.add, V("BC", 0, 1), A.add)
+        prefix(wb, V("ZERO", 0, 8), i2, zb(t, 104, 40), b("TB2"), b("EC2"),
+               lambda: ts(b("NW"), wb, -1000.0, A.mult, 1000.0, A.add),
+               lambda: (tt(b("NP"), sub(i2, 0, 8), b("NW"), A.add), tt(b("BP"), sub(i2, 0, 8), b("OB"), A.add)))
         keep = b("VAL", 16, 24)
-        tt(keep, b("KP"), wb, A.mult)
-        tt(b("VAL", 0, 8), keep, b("SV"), A.mult)
+        ts(keep, b("NP"), b("EC2", 7, 8), A.add, float(CAPP), A.is_le)
+        ts(b("SV"), b("BP"), b("EC2", 7, 8), A.add)
         tt(b("VAL", 8, 16), keep, b("CG"), A.mult)
+        tt(b("VAL", 0, 8), keep, b("SV"), A.mult)
         for i, s in enumerate(others):
             tc(mk("BK", 24 * i, 24 * i + 24), blk(s, "VAL%d" % t))
             act(mk("KQ", 8 * i + 8, 8 * i + 16), mk("BK", 24 * i + 16, 24 * i + 24))
         tt(mk("SA"), mk("BK", 0, 24), mk("BK", 24, 48), A.add)
-        tt(mk("SB"), mk("SA"), mk("BK", 48, 72), A.add)
-        ts(mk("KQ", 0, 8), mk("SB", 16, 24), -1.0, A.mult, 1.0, A.add)
-        tt(mk("OO", 0, 8), mk("KQ", 0, 8), mk("LCN"), A.mult)
-        tt(mk("XC", 0, 8), mk("SB", 0, 8), mk("OO", 0, 8), A.add)
+        tt(mk("SB"), mk("BK", 48, 56), mk("LCN"), A.add)
+        tt(mk("KS"), mk("SA", 16, 24), mk("BK", 64, 72), A.add)
+        tt(mk("XC"), mk("SA", 0, 8), mk("SB"), A.add)
+        ts(mk("KQ", 0, 8), mk("KS"), -1.0, A.mult, 1.0, A.add)
         for j in range(2):
-            ts(mk("A2", 8 * j, 8 * j + 8), mk("XC", 0, 8), blk(me, "XEO", 4 * j, 4 * j + 1), A.mult)
+            ts(mk("A2", 8 * j, 8 * j + 8), mk("XC"), blk(me, "XEO", 4 * j, 4 * j + 1), A.mult)
+        tt(mk("PP"), mk("KQ"), mk("U"), A.mult)
         tc(mk("A2", 16, 32), mk("A2", 0, 16))
+        tt(mk("P16"), mk("PP", 0, 16), mk("PP", 16, 32), A.add)
         tr(mk("TA"), mk("A2"))
+        tt(mk("PA"), mk("P16", 0, 8), mk("P16", 8, 16), A.add)
+        pr = V("PR%d" % t, 0, 256, 1, 0, 1)
+        dma("s", ap(pr), ap(mk("PA")), [mk("PA")], [pr])
+        op("g", lambda: g.partition_broadcast(ap(b("PB")), ap(pr), 128), [pr], [b("PB")])
         tt(mk("XT"), mk("TA", 0, 32, 2), mk("TA", 1, 32, 2), A.add)
         half = me // 2
         for k in (2 * half, 2 * half + 1):
             tc(blk(k, "XO%d" % t), mk("XT"))
         tc(V("XO%d" % t, p0=64 - 64 * half, p1=128 - 64 * half), V("XO%d" % t, p0=64 * half, p1=64 * half + 64))
-        tt(mk("PP"), mk("KQ"), mk("U"), A.mult)
-        tt(mk("P16"), mk("PP", 0, 16), mk("PP", 16, 32), A.add)
-        tt(mk("PA"), mk("P16", 0, 8), mk("P16", 8, 16), A.add)
-        pr = V("PR%d" % t, 0, 256, 1, 0, 1)
-        dma("s", ap(pr), ap(mk("PA")), [mk("PA")], [pr])
-        op("g", lambda: g.partition_broadcast(ap(b("PB")), ap(pr), 128), [pr], [b("PB")])
 
     def own_numbers(t):
         mk = lambda name, *a: blk(me, name + str(t), *a)
-        tt(mk("OO", 8, 16), mk("KQ", 0, 8), mk("CG"), A.mult)
-        tt(mk("XC", 8, 16), mk("SB", 8, 16), mk("OO", 8, 16), A.add)
-        dma("s", T.ch[t - 1:t, :], ap(mk("XC", 8, 16)), [mk("XC", 8, 16)], [])
+        tt(mk("CA"), mk("BK", 56, 64), mk("CO"), A.add)
+        tt(mk("CH"), mk("SA", 8, 16), mk("CA"), A.add)
+        dma("s", T.ch[t - 1:t, :], ap(mk("CH")), [mk("CH")], [])
 
     def new_columns(t, meanwhile):
         b = bufs(t)
@@ -480,27 +494,27 @@ def rank_program(g, core, T, topo):
     ev = scores_out(1)
     wait("s", [ev])
     load("s", V("E1"), T.e1[:])
-    prep_nodes(2, V("MSG3", 4, 6))
-    spread(V("MSG3"), lambda s: V("LM3", 6 * s, 6 * s + 6), "m3", "lm3")
     value_rows(1)
     decode_ties(1)
+    prep_nodes(2, V("MSG3", 4, 6))
+    spread(V("MSG3"), lambda s: V("LM3", 6 * s, 6 * s + 6), "m3", "lm3")
+    ties_end(1)
     own_columns(1)
     qz(V("QW0", 0, 256), V("QP0", 0, 256), V("E0"))
-    quantise_a(0)
-    quantise_a(1)
     ev = choose_and_send(1)
     wait("s", [ev])
     load("s", V("E2"), T.e2[:])
     load("s", V("WT"), T.w[:])
     own_list(1)
-    quantise_a(2)
-    quantise_a(3)
+    for i in range(4):
+        quantise_a(i)
     new_columns(1, lambda: (own_numbers(1), decode_lists(2)))
     scores_out(2)
     value_rows(2)
     decode_ties(2)
-    own_columns(2)
     qz(V("QW1", 0, 256), V("QP1", 0, 256), V("HT1"))
+    ties_end(2)
+    own_columns(2)
     qz(V("WQ"), V("WP"), V("WT"))
     choose_and_send(2)
     own_list(2)

@@ -4,6 +4,8 @@ from concourse.mybir import dt, AluOpType as A, ActivationFunctionType as AF
 P, CAPP = 256, 64
 TINY = 2.0 ** -100
 STEP = 2.0 ** -24 * (1 + 2.0 ** -10)
+WAIT, LEAST, ISSUE, WAY = 0.12, 0.08, 0.8, 3.5
+LOCAL, FIRST, LONG = 2.3, 3.8, 5.5
 F, B, I, H, C, S8 = "float32", "bfloat16", "int32", "uint16", "float8_e4m3fn_x4", "uint8"
 SCRATCH = {"PS": ("psum", [128, 4096], F)}
 PLACE = {"PS": ("PS", 0, 4096)}
@@ -35,7 +37,7 @@ _buf(F, U1=32, U2=32, Z1=1024, Z2=1024, YB=256, S0=256, S1=256, S2=256, PR1=256,
 _buf(I, RAW1=64, RAW2=64)
 _area(H, DUP=8)
 _area(I, PI=1, PJ=4, DUPI=8, TRI=8)
-_area(F, ZERO=64, NEG=8, KCOL=4, P15F=4, P15E=4, XEO=8, GCOL=4, BC=4, TR=8, ZB=368, HI=4, HJ=4)
+_area(F, ZERO=64, NEG=8, KCOL=4, P15F=4, P15E=4, XEO=8, GCOL=4, GD=4, BC=4, TR=8, ZB=368, HI=4, HJ=4)
 _area(F, **_each(RL=64, RN=64, T2=64, TN=64, M1=32, MN=32, LW=8, LOC=4, KFN=8, KSC=8, LCN=8, OL=8, OB=8, CD=8, CG=8, LF=8, RB=128,
                  VR=128, KF=32, KL=24, KK=32, G=128, TG=128, V3=24, AB=24, AC=24, DE=24, VA=24, L3=24, X1=8, LO=8, TB=32, EC=32,
                  LT=8, AA=8, W=640, WD=128, TW=128, LS=4, M16=16, MM=8, EQ=32, KEY=32, K16=16, KM=8, TB2=32, EC2=32, SV=8, NW=8,
@@ -56,6 +58,7 @@ def rank_program(g, core, T, topo):
     slot_at = [(me - d) % 4 - 1 for d in others]
     qs = {"v": g.vector, "a": g.scalar, "t": g.tensor, "g": g, "s": g.sync}
     hist, know, cnt, total = {}, {q: {} for q in qs}, {}, {}
+    nodes, past, last = [], {}, {}
 
     def V(name, c0=0, c1=None, st=1, p0=0, p1=128):
         return (name, p0, p1, c0, PLACE[name][2] if c1 is None else c1, st)
@@ -67,6 +70,9 @@ def rank_program(g, core, T, topo):
         name, o, _ = PLACE[v[0]]
         return T[name][v[1]:v[2], o + v[3]:o + v[4]] if v[5] == 1 else T[name][v[1]:v[2], o + v[3]:o + v[4]:v[5]]
 
+    def width(v):
+        return (v[4] - v[3] + v[5] - 1) // v[5]
+
     def clash(a, b):
         if a[2] <= b[1] or b[2] <= a[1] or a[4] <= b[3] or b[4] <= a[3]:
             return False
@@ -74,6 +80,22 @@ def rank_program(g, core, T, topo):
 
     def bank(v):
         return (v[0], 0, 128, v[3] // 512 * 512, v[3] // 512 * 512 + 512, 1) if v[0] == "PS" else v
+
+    def regions(reads, writes):
+        return [(bank(v), False) for v in reads] + [(bank(v), True) for v in writes]
+
+    def push(opts, reads, writes, cost, dur=None, after=()):
+        i, deps = len(nodes), set(after)
+        for r, w in regions(reads, writes):
+            deps |= {j for (o, ow, j) in past.get(r[0], []) if (w or ow) and clash(r, o)}
+        for r, w in regions(reads, writes):
+            past.setdefault(r[0], []).append((r, w, i))
+        prev = last.get("g") if "g" in opts else None
+        if "g" in opts:
+            last["g"] = i
+        nodes.append({"opts": opts, "rd": reads, "wr": writes, "cost": cost, "dur": cost if dur is None else dur,
+                      "deps": deps - {i}, "prev": prev, "gate": [j for j in after]})
+        return i
 
     def wait(q, evs):
         need = {}
@@ -89,81 +111,143 @@ def rank_program(g, core, T, topo):
             for k, n in list(need[sem][1].items()) + [(sem, need[sem][0])]:
                 know[q][k] = max(know[q].get(k, 0), n)
 
-    def use(q, reads, writes):
-        evs = []
-        for r, w in [(bank(v), False) for v in reads] + [(bank(v), True) for v in writes]:
+    def issue(node, q):
+        if q == "x":
+            return
+        evs = [nodes[j]["ev"] for j in node["gate"]]
+        for r, w in regions(node["rd"], node["wr"]):
             evs += [ev for (o, ow, ev) in hist.get(r[0], []) if (w or ow) and clash(r, o)]
         wait(q, evs)
-
-    def note(q, sem, val, reads, writes):
+        kind, call = node["opts"][q]
+        if kind == "op":
+            sem, val = "q" + q, cnt.get(q, 0) + 1
+            cnt[q] = val
+            call().then_inc(T.sem[sem], 1)
+        elif kind == "dma":
+            sem, val = "d%d" % cnt.get("dma", 0), 16
+            cnt["dma"] = cnt.get("dma", 0) + 1
+            call().then_inc(T.sem[sem], 16)
+        else:
+            sem, val = call()
         clock = dict(know[q])
         clock[sem] = val
         total[sem] = max(total.get(sem, 0), val)
-        for r, w in [(bank(v), False) for v in reads] + [(bank(v), True) for v in writes]:
-            hist.setdefault(r[0], []).append((r, w, (sem, val, clock)))
-        return (sem, val, clock)
+        node["ev"] = (sem, val, clock)
+        for r, w in regions(node["rd"], node["wr"]):
+            hist.setdefault(r[0], []).append((r, w, node["ev"]))
 
-    def op(q, call, reads, writes):
-        use(q, reads, writes)
-        cnt[q] = cnt.get(q, 0) + 1
-        call().then_inc(T.sem["q" + q], 1)
-        return note(q, "q" + q, cnt[q], reads, writes)
+    def lay():
+        n = len(nodes)
+        succ = [[] for _ in range(n)]
+        for i, nd in enumerate(nodes):
+            for j in nd["deps"]:
+                succ[j].append(i)
+        high = [0.0] * n
+        for i in range(n - 1, -1, -1):
+            high[i] = nodes[i]["dur"] + max([WAIT + high[j] for j in succ[i]] + [0.0])
+            p = nodes[i]["prev"]
+            if p is not None:
+                high[p] = max(high[p], nodes[p]["cost"] + high[i])
+        left = [len(nd["deps"]) for nd in nodes]
+        ready = {i for i in range(n) if left[i] == 0}
+        free, fin, done = {}, [0.0] * n, set()
+        while ready:
+            cand = []
+            for i in ready:
+                nd = nodes[i]
+                if nd["prev"] is not None and nd["prev"] not in done:
+                    continue
+                s = max([fin[j] + WAIT for j in nd["deps"]] + [0.0])
+                start, q = min((max(s, free.get(q, 0.0)) if q != "x" else s, "vatgsx".index(q)) for q in nd["opts"])
+                cand.append((start, -high[i], i, "vatgsx"[q]))
+            first = min(cand)[0]
+            start, _, i, q = min((c for c in cand if c[0] <= first + 0.05), key=lambda c: c[1:])
+            issue(nodes[i], q)
+            free[q] = start + nodes[i]["cost"]
+            fin[i] = start + nodes[i]["dur"]
+            ready.discard(i)
+            done.add(i)
+            for j in succ[i]:
+                left[j] -= 1
+                if left[j] == 0:
+                    ready.add(j)
+
+    def us(cycles):
+        return max(LEAST, 0.02 + 0.001 * cycles)
+
+    def op(q, call, reads, writes, cycles):
+        return push({q: ("op", call)}, reads, writes, us(cycles))
 
     def sv(s):
         return ap(s) if isinstance(s, tuple) else s
 
+    def cols_of(*ss):
+        return [s for s in ss if isinstance(s, tuple)]
+
     def tc(o, a):
-        op("v", lambda: g.vector.tensor_copy(ap(o), ap(a)), [a], [o])
+        op("v", lambda: g.vector.tensor_copy(ap(o), ap(a)), [a], [o], width(a))
 
     def tt(o, a, b, f):
-        op("v", lambda: g.vector.tensor_tensor(ap(o), ap(a), ap(b), f), [a, b], [o])
+        op("v", lambda: g.vector.tensor_tensor(ap(o), ap(a), ap(b), f), [a, b], [o], width(a) * (1 if a[0] == "PS" else 2))
 
     def ts(o, a, s1, f1, s2=None, f2=None):
-        rd = [a] + [s for s in (s1, s2) if isinstance(s, tuple)]
         if f2 is None:
-            op("v", lambda: g.vector.tensor_scalar(ap(o), ap(a), sv(s1), None, f1), rd, [o])
+            op("v", lambda: g.vector.tensor_scalar(ap(o), ap(a), sv(s1), None, f1), [a] + cols_of(s1), [o], width(a))
         else:
-            op("v", lambda: g.vector.tensor_scalar(ap(o), ap(a), sv(s1), sv(s2), f1, f2), rd, [o])
+            op("v", lambda: g.vector.tensor_scalar(ap(o), ap(a), sv(s1), sv(s2), f1, f2), [a] + cols_of(s1, s2), [o], width(a))
+
+    def lin(o, a, scale=1.0, bias=0.0):
+        def on_v():
+            if scale == 1.0 and bias == 0.0:
+                return g.vector.tensor_copy(ap(o), ap(a))
+            if bias == 0.0:
+                return g.vector.tensor_scalar(ap(o), ap(a), sv(scale), None, A.mult)
+            if scale == 1.0:
+                return g.vector.tensor_scalar(ap(o), ap(a), sv(bias), None, A.add)
+            return g.vector.tensor_scalar(ap(o), ap(a), sv(scale), sv(bias), A.mult, A.add)
+
+        def on_a():
+            if bias == 0.0:
+                return g.scalar.activation(ap(o), ap(a), AF.Copy, scale=sv(scale))
+            return g.scalar.activation(ap(o), ap(a), AF.Identity, scale=sv(scale), bias=sv(bias))
+        push({"v": ("op", on_v), "a": ("op", on_a)}, [a] + cols_of(scale, bias), [o], us(width(a)))
 
     def scan(o, a, b):
-        op("v", lambda: g.vector.tensor_tensor_scan(ap(o), ap(a), ap(b), 0.0, A.add, A.add), [a, b], [o])
+        op("v", lambda: g.vector.tensor_tensor_scan(ap(o), ap(a), ap(b), 0.0, A.add, A.add), [a, b], [o], width(a))
 
     def tr(o, a):
-        op("v", lambda: g.vector.transpose(ap(o), ap(a)), [a], [o])
+        op("v", lambda: g.vector.transpose(ap(o), ap(a)), [a], [o], width(a))
 
     def ms(o, c):
-        op("v", lambda: g.vector.memset(ap(o), c), [], [o])
+        op("v", lambda: g.vector.memset(ap(o), c), [], [o], width(o))
 
     def gat(o, w, off):
-        op("v", lambda: g.vector.tensor_copy(ap(o), ap(w).indirect(ap(off))), [w, off], [o])
+        op("v", lambda: g.vector.tensor_copy(ap(o), ap(w).indirect(ap(off))), [w, off], [o], 50 + 1.5 * width(o))
 
     def pick(qo, so, qw, sw, off):
-        op("v", lambda: g.vector.tensor_copy(ap(qo).bitcast(dt.uint32), ap(qw).bitcast(dt.uint32).indirect(ap(off))), [qw, off], [qo])
-        op("a", lambda: g.scalar.activation(ap(so), ap(sw).indirect(ap(off)), AF.Copy), [sw, off], [so])
+        op("v", lambda: g.vector.tensor_copy(ap(qo).bitcast(dt.uint32), ap(qw).bitcast(dt.uint32).indirect(ap(off))), [qw, off], [qo],
+           50 + 1.5 * width(qo))
+        op("a", lambda: g.scalar.activation(ap(so), ap(sw).indirect(ap(off)), AF.Copy), [sw, off], [so], 70 + 1.5 * width(qo))
 
     def qz(q, s, a):
-        op("v", lambda: g.vector.quantize_mx(ap(q), ap(s), ap(a)), [a], [q, s])
+        op("v", lambda: g.vector.quantize_mx(ap(q), ap(s), ap(a)), [a], [q, s], 0.25 * width(a))
 
     def act(o, a, scale=1.0):
-        op("a", lambda: g.scalar.activation(ap(o), ap(a), AF.Copy, scale=scale), [a], [o])
+        op("a", lambda: g.scalar.activation(ap(o), ap(a), AF.Copy, scale=scale), [a], [o], width(a))
 
     def plus(o, a, bias):
-        op("a", lambda: g.scalar.activation(ap(o), ap(a), AF.Identity, bias=ap(bias)), [a, bias], [o])
+        op("a", lambda: g.scalar.activation(ap(o), ap(a), AF.Identity, bias=ap(bias)), [a, bias], [o], width(a))
 
     def mm(b, n, wq, ws, xq, xs):
         o = V("PS", 512 * b, 512 * b + n)
-        op("t", lambda: g.tensor.matmul_mx(ap(o), ap(wq), ap(ws), ap(xq), ap(xs), True, True), [wq, ws, xq, xs], [o])
+        op("t", lambda: g.tensor.matmul_mx(ap(o), ap(wq), ap(ws), ap(xq), ap(xs), True, True), [wq, ws, xq, xs], [o], n + 16)
         return o
 
-    def dma(q, out, in_, reads, writes):
-        use(q, reads, writes)
-        n = cnt.get("dma", 0)
-        cnt["dma"] = n + 1
-        qs[q].dma_start(out, in_).then_inc(T.sem["d%d" % n], 16)
-        return note(q, "d%d" % n, 16, reads, writes)
+    def dma(q, out, in_, reads, writes, after=(), dur=LOCAL):
+        return push({q: ("dma", lambda: qs[q].dma_start(out, in_))}, reads, writes, 0.08, dur, after)
 
-    def load(q, v, src):
-        return dma(q, ap(v), src, [], [v])
+    def load(q, v, src, dur, after=()):
+        return dma(q, ap(v), src, [], [v], after, dur)
 
     def mask_of(engines):
         return sum(1 << e for e in engines)
@@ -172,26 +256,21 @@ def rank_program(g, core, T, topo):
         rid, pid, _ = topo.addr(T.cores[d])
         return DstId(rid=rid, pnc=pid)
 
-    def spread(src, land, sem, lsem):
-        use("g", [src], [])
+    def remote(transfers, src, lsem, count, sem, arrivals, landing):
+        def call():
+            g.remote_dma_fused(transfers, local_sem=T.sem[lsem])
+            return lsem, count
+        i = push({"g": ("remote", call)}, [src], [], ISSUE, ISSUE + 1.0)
+        push({"x": None}, [], [landing], 0.0, WAY - 1.0, [i])
+        total[sem] = arrivals
+        hist.setdefault(landing[0], []).append((landing, True, (sem, arrivals, {sem: arrivals})))
+        return i
+
+    def spread(src, land, sem, lsem, landing):
         e = topo.engines(core, T.cores[others[0]])[:16]
-        g.remote_dma_fused([RemoteDMATransfer(
+        return remote([RemoteDMATransfer(
             dst_ids=[dst(d) for d in others], dma_engine_mask=mask_of(e), remote_sem=T.sem[sem], srcs=[ap(src)],
-            dsts=[ap(land(s)) for s in slot_at])], local_sem=T.sem[lsem])
-        return note("g", lsem, len(e), [src], [])
-
-    def arrive(sem, n, writes):
-        total[sem] = n
-        for v in writes:
-            hist.setdefault(v[0], []).append((v, True, (sem, n, {sem: n})))
-
-    n16 = len(topo.engines(core, T.cores[others[0]])[:16]) * 3
-    for i in (1, 2, 3):
-        arrive("m%d" % i, n16, [V("LM%d" % i)])
-    for t in (1, 2):
-        arrive("v%d" % t, n16, [V("U%d" % t, 8, 32)])
-        arrive("c%d" % t, 12, [V("QW%d" % (t - 1), 256, 448)])
-        arrive("s%d" % t, 12, [V("QP%d" % (t - 1), 256, 448)])
+            dsts=[ap(land(s)) for s in slot_at])], src, lsem, len(e), sem, 3 * len(e), landing)
 
     def zb(t, o, n):
         return V("ZB", 184 * (t - 1) + o, 184 * (t - 1) + o + n)
@@ -202,16 +281,16 @@ def rank_program(g, core, T, topo):
     def bufs(t):
         return lambda name, *a: V(name + str(t), *a)
 
-    load("s", V("RAW1", p0=0, p1=16), T.p1[:])
-    load("a", V("RAW1", p0=16, p1=32), T.p1[:])
-    load("s", V("E0", 0, 512), T.e0[:, 0:512])
-    load("a", V("UT", 0, 4), T.u[:, 0:4])
-    load("a", V("E0", 512, 1024), T.e0[:, 512:1024])
-    load("s", V("RAW2", p0=0, p1=16), T.p2[:])
-    load("a", V("RAW2", p0=16, p1=32), T.p2[:])
-    op("g", lambda: g.iota(ap(V("PI")), [[0, 1]], 0, 1), [], [V("PI")])
-    op("g", lambda: g.iota(ap(V("DUPI")), [[16, 4], [0, 2]], 0, 0), [], [V("DUPI")])
-    op("g", lambda: g.iota(ap(V("TRI")), [[1, 8]], 257, 0), [], [V("TRI")])
+    load("s", V("RAW1", p0=0, p1=16), T.p1[:], LOCAL)
+    load("a", V("RAW1", p0=16, p1=32), T.p1[:], LOCAL)
+    load("s", V("E0", 0, 512), T.e0[:, 0:512], FIRST)
+    load("a", V("UT", 0, 4), T.u[:, 0:4], FIRST)
+    load("a", V("E0", 512, 1024), T.e0[:, 512:1024], FIRST)
+    load("s", V("RAW2", p0=0, p1=16), T.p2[:], FIRST)
+    load("s", V("RAW2", p0=16, p1=32), T.p2[:], FIRST)
+    op("g", lambda: g.iota(ap(V("PI")), [[0, 1]], 0, 1), [], [V("PI")], 100)
+    op("g", lambda: g.iota(ap(V("DUPI")), [[16, 4], [0, 2]], 0, 0), [], [V("DUPI")], 100)
+    op("g", lambda: g.iota(ap(V("TRI")), [[1, 8]], 257, 0), [], [V("TRI")], 100)
     ms(V("ZERO"), 0.0)
     for j, m in enumerate((15, 3, 1, 96)):
         ts(V("PJ", j, j + 1), V("PI"), m, A.bitwise_and)
@@ -221,9 +300,10 @@ def rank_program(g, core, T, topo):
     ts(V("HJ", 0, 1), p15, 8.0, A.is_ge, 255.0, A.mult)
     tc(V("XEO", 4, 5), V("PJ", 2, 3))
     ts(V("GCOL", 0, 1), V("PJ", 3, 4), 8.0, A.mult)
-    ts(V("HI", 0, 1), V("HJ", 0, 1), 1.0, A.add)
-    ts(V("P15E", 0, 1), p15, 8.0, A.mult)
-    ts(V("XEO", 0, 1), V("XEO", 4, 5), -1.0, A.mult, 1.0, A.add)
+    lin(V("GD", 0, 1), V("GCOL", 0, 1), bias=float(-P * me))
+    lin(V("HI", 0, 1), V("HJ", 0, 1), bias=1.0)
+    lin(V("P15E", 0, 1), p15, scale=8.0)
+    lin(V("XEO", 0, 1), V("XEO", 4, 5), -1.0, 1.0)
     ts(V("DUP"), V("DUPI"), p15, A.add)
     ts(V("TR"), V("TRI"), V("P15E", 0, 1), A.add)
     ms(V("NEG"), -1.0)
@@ -261,7 +341,7 @@ def rank_program(g, core, T, topo):
         for i in (1, 2, 3):
             tt(b("KFN", 2 * i, 2 * i + 2), b("KSC", 2 * i - 2, 2 * i), b("KN", i, 8, 4), A.add)
             if i < 3:
-                ts(b("KSC", 2 * i, 2 * i + 2), b("KFN", 2 * i, 2 * i + 2), 4.0, A.mult)
+                lin(b("KSC", 2 * i, 2 * i + 2), b("KFN", 2 * i, 2 * i + 2), scale=4.0)
         tc(kcols, b("KFN", 6, 8))
 
     def own_columns(t):
@@ -270,10 +350,10 @@ def rank_program(g, core, T, topo):
         tc(b("LCN"), b("LN"))
         for k in [me] + others:
             act(blk(k, "OL%d" % t), blk(me, "LCN%d" % t))
-        ts(blk(me, "CO%d" % t), blk(me, "LCN%d" % t), float(P * me), A.add)
-        ts(b("OB"), b("OL"), -1.0, A.mult, V("BC", 0, 1), A.add)
+        lin(blk(me, "CO%d" % t), blk(me, "LCN%d" % t), bias=float(P * me))
+        lin(b("OB"), b("OL"), -1.0, V("BC", 0, 1))
         tt(b("CD"), b("LCN"), b("OL"), A.subtract)
-        ts(b("CG"), b("CD"), V("GCOL", 0, 1), A.add, float(-P * me), A.add)
+        lin(b("CG"), b("CD"), bias=V("GD", 0, 1))
 
     def packed(t, d):
         if d == me:
@@ -300,9 +380,10 @@ def rank_program(g, core, T, topo):
         tc(b("LF"), b("LI"))
         for i in range(3):
             act(b("V3", 8 * i, 8 * i + 8), b("U", 0, 8))
-        op("a", lambda: g.scalar.activation(ap(b("AB")), ap(b("V3")), AF.Abs, scale=STEP), [b("V3")], [b("AB")])
+        op("a", lambda: g.scalar.activation(ap(b("AB")), ap(b("V3")), AF.Abs, scale=STEP), [b("V3")], [b("AB")], 24)
         for c in range(8):
             plus(b("RB", 16 * c, 16 * c + 16), V("ZERO", 0, 16), b("LF", c, c + 1))
+        tr(b("VR"), b("RB"))
 
     def decode_ties(t):
         b = bufs(t)
@@ -316,16 +397,11 @@ def rank_program(g, core, T, topo):
             for s in range(4):
                 if s != d:
                     i = (s - me) % 4
-                    act(sub(ka, 8 * i, 8 * i + 8, d), blk(s, "KF%d" % t, 8 * d, 8 * d + 8))
-        ts(b("AC"), b("AB"), TINY, A.add)
-        tr(b("VR"), b("RB"))
-
-    def ties_end(t):
-        b = bufs(t)
-        ka = zb(t, 144, 32)
+                    lin(sub(ka, 8 * i, 8 * i + 8, d), blk(s, "KF%d" % t, 8 * d, 8 * d + 8))
         for i in range(3):
             tt(b("KL", 8 * i, 8 * i + 8), sub(ka, 8 * i + 8, 8 * i + 16), sub(ka, 0, 8), A.is_lt)
-        ts(b("KK"), ka, -1.0, A.mult, 4.0, A.add)
+        lin(b("KK"), ka, -1.0, 4.0)
+        ts(b("AC"), b("AB"), TINY, A.add)
         tt(b("DE"), b("AC"), b("KL"), A.mult)
         tt(b("VA"), b("V3"), b("DE"), A.subtract)
 
@@ -333,15 +409,13 @@ def rank_program(g, core, T, topo):
         b = bufs(t)
         gat(b("G"), V("S%d" % (t - 1)), b("LU"))
         tr(b("TG"), b("G"))
-        tc(b("U", 0, 4), b("TG", 0, 128, 32))
-        tc(b("U", 4, 8), b("TG", 16, 128, 32))
-        return spread(b("U", 0, 8), lambda s: b("U", 8 + 8 * s, 16 + 8 * s), "v%d" % t, "lv%d" % t)
+        lin(b("U", 0, 4), b("TG", 0, 128, 32))
+        lin(b("U", 4, 8), b("TG", 16, 128, 32))
+        return spread(b("U", 0, 8), lambda s: b("U", 8 + 8 * s, 16 + 8 * s), "v%d" % t, "lv%d" % t, b("U", 8, 32))
 
-    def prefix(x, add, ni, eb, tb, ec, one, two):
+    def prefix(x, add, ni, eb, tb, ec):
         scan(sub(ni, 0, 8), x, add)
-        one()
         tr(tb, ni)
-        two()
         scan(sub(eb, 1, 33), tb, V("ZERO", 0, 32))
         tr(ec, sub(eb, 0, 32))
 
@@ -351,11 +425,12 @@ def rank_program(g, core, T, topo):
         tt(b("X1"), b("L3", 0, 8), b("L3", 8, 16), A.max)
         tt(b("LO"), b("X1"), b("L3", 16, 24), A.max)
         ni = zb(t, 0, 32)
-        prefix(b("LO"), V("NEG"), ni, zb(t, 64, 40), b("TB"), b("EC"),
-               lambda: tt(b("LT"), b("LO"), V("TR"), A.mult), lambda: tt(b("AA"), b("LT"), sub(ni, 0, 8), A.subtract))
+        prefix(b("LO"), V("NEG"), ni, zb(t, 64, 40), b("TB"), b("EC"))
+        tt(b("LT"), b("LO"), V("TR"), A.mult)
+        tt(b("AA"), b("LT"), sub(ni, 0, 8), A.subtract)
         for h in range(2):
             ts(b("OF", h, 8, 2), b("AA", 4 * h, 4 * h + 4), b("EC", 7, 8), A.subtract, -1.0, A.add)
-        op("v", lambda: g.vector.tensor_copy(ap(b("W")).indirect(ap(b("OF"))), ap(b("VR"))), [b("VR"), b("OF")], [b("W")])
+        op("v", lambda: g.vector.tensor_copy(ap(b("W")).indirect(ap(b("OF"))), ap(b("VR"))), [b("VR"), b("OF")], [b("W")], 450)
         gat(b("WD"), b("W", 0, 64), V("DUP"))
         tr(b("TW"), b("WD"))
         tt(b("LS"), b("TW", 0, 128, 32), b("TW", 16, 128, 32), A.add)
@@ -370,9 +445,7 @@ def rank_program(g, core, T, topo):
             for lo, hi in runs:
                 tc(V("PO%d" % t, lo, hi, 1, 64 - 64 * half, 128 - 64 * half), V("PO%d" % t, lo, hi, 1, 64 * half, 64 * half + 64))
         pick(b("SQ"), b("SS"), V("QO%d" % (t - 1)), V("QS%d" % (t - 1)), b("PO"))
-        ev = None
         for src, land, sem, turn in (("SQ", "QW", "c", 0), ("SS", "QP", "s", 3)):
-            use("g", [b(src)], [])
             trs = []
             for i, d in enumerate(others):
                 e = topo.engines(core, T.cores[d])
@@ -381,9 +454,8 @@ def rank_program(g, core, T, topo):
                 trs.append(RemoteDMATransfer(
                     dst_ids=[dst(d)], dma_engine_mask=mask_of(e[j:j + 4]), remote_sem=T.sem[sem + str(t)],
                     srcs=[ap(a).bitcast(dt.uint8) if src == "SQ" else ap(a)], dsts=[ap(z).bitcast(dt.uint8) if src == "SQ" else ap(z)]))
-            g.remote_dma_fused(trs, local_sem=T.sem["l" + sem + str(t)])
-            ev = note("g", "l" + sem + str(t), 12, [b(src)], [])
-        return ev
+            i = remote(trs, b(src), "l" + sem + str(t), 12, sem + str(t), 12, V(land + str(t - 1), 256, 448))
+        return i
 
     def own_list(t):
         b = bufs(t)
@@ -398,57 +470,52 @@ def rank_program(g, core, T, topo):
         wb, i2 = zb(t, 176, 8), zb(t, 32, 32)
         for i, s in enumerate(others):
             tt(sub(wb, 0, 8, s), mk("KEY", 8 * i + 8, 8 * i + 16), mk("KM"), A.is_equal)
-        prefix(wb, V("ZERO", 0, 8), i2, zb(t, 104, 40), b("TB2"), b("EC2"),
-               lambda: ts(b("NW"), wb, -1000.0, A.mult, 1000.0, A.add),
-               lambda: (tt(b("NP"), sub(i2, 0, 8), b("NW"), A.add), tt(b("BP"), sub(i2, 0, 8), b("OB"), A.add)))
+        prefix(wb, V("ZERO", 0, 8), i2, zb(t, 104, 40), b("TB2"), b("EC2"))
+        lin(b("NW"), wb, -1000.0, 1000.0)
+        tt(b("NP"), sub(i2, 0, 8), b("NW"), A.add)
+        tt(b("BP"), sub(i2, 0, 8), b("OB"), A.add)
         keep = b("VAL", 16, 24)
         ts(keep, b("NP"), b("EC2", 7, 8), A.add, float(CAPP), A.is_le)
         ts(b("SV"), b("BP"), b("EC2", 7, 8), A.add)
         tt(b("VAL", 8, 16), keep, b("CG"), A.mult)
         tt(b("VAL", 0, 8), keep, b("SV"), A.mult)
         for i, s in enumerate(others):
-            tc(mk("BK", 24 * i, 24 * i + 24), blk(s, "VAL%d" % t))
-            act(mk("KQ", 8 * i + 8, 8 * i + 16), mk("BK", 24 * i + 16, 24 * i + 24))
+            lin(mk("BK", 24 * i, 24 * i + 24), blk(s, "VAL%d" % t))
+            lin(mk("KQ", 8 * i + 8, 8 * i + 16), mk("BK", 24 * i + 16, 24 * i + 24))
         tt(mk("SA"), mk("BK", 0, 24), mk("BK", 24, 48), A.add)
         tt(mk("SB"), mk("BK", 48, 56), mk("LCN"), A.add)
         tt(mk("KS"), mk("SA", 16, 24), mk("BK", 64, 72), A.add)
         tt(mk("XC"), mk("SA", 0, 8), mk("SB"), A.add)
-        ts(mk("KQ", 0, 8), mk("KS"), -1.0, A.mult, 1.0, A.add)
+        lin(mk("KQ", 0, 8), mk("KS"), -1.0, 1.0)
         for j in range(2):
-            ts(mk("A2", 8 * j, 8 * j + 8), mk("XC"), blk(me, "XEO", 4 * j, 4 * j + 1), A.mult)
-        tt(mk("PP"), mk("KQ"), mk("U"), A.mult)
-        tc(mk("A2", 16, 32), mk("A2", 0, 16))
-        tt(mk("P16"), mk("PP", 0, 16), mk("PP", 16, 32), A.add)
+            lin(mk("A2", 8 * j, 8 * j + 8), mk("XC"), scale=blk(me, "XEO", 4 * j, 4 * j + 1))
+        lin(mk("A2", 16, 32), mk("A2", 0, 16))
         tr(mk("TA"), mk("A2"))
-        tt(mk("PA"), mk("P16", 0, 8), mk("P16", 8, 16), A.add)
-        pr = V("PR%d" % t, 0, 256, 1, 0, 1)
-        dma("s", ap(pr), ap(mk("PA")), [mk("PA")], [pr])
-        op("g", lambda: g.partition_broadcast(ap(b("PB")), ap(pr), 128), [pr], [b("PB")])
         tt(mk("XT"), mk("TA", 0, 32, 2), mk("TA", 1, 32, 2), A.add)
         half = me // 2
         for k in (2 * half, 2 * half + 1):
             tc(blk(k, "XO%d" % t), mk("XT"))
         tc(V("XO%d" % t, p0=64 - 64 * half, p1=128 - 64 * half), V("XO%d" % t, p0=64 * half, p1=64 * half + 64))
-
-    def own_numbers(t):
-        mk = lambda name, *a: blk(me, name + str(t), *a)
+        tt(mk("PP"), mk("KQ"), mk("U"), A.mult)
+        tt(mk("P16"), mk("PP", 0, 16), mk("PP", 16, 32), A.add)
+        tt(mk("PA"), mk("P16", 0, 8), mk("P16", 8, 16), A.add)
+        pr = V("PR%d" % t, 0, 256, 1, 0, 1)
+        dma("s", ap(pr), ap(mk("PA")), [mk("PA")], [pr])
+        op("g", lambda: g.partition_broadcast(ap(b("PB")), ap(pr), 128), [pr], [b("PB")], 1024)
         tt(mk("CA"), mk("BK", 56, 64), mk("CO"), A.add)
         tt(mk("CH"), mk("SA", 8, 16), mk("CA"), A.add)
         dma("s", T.ch[t - 1:t, :], ap(mk("CH")), [mk("CH")], [])
 
-    def new_columns(t, meanwhile):
+    def new_columns(t):
         b = bufs(t)
         for f in range(2):
             lo, hi = 128 * f, 128 * f + 128
             pick(b("XQ", lo, hi), b("XS", lo, hi), V("QW%d" % (t - 1)), V("QP%d" % (t - 1)), b("XO", 8 * f, 8 * f + 8))
-        meanwhile()
         rs = {}
         for f in range(2):
             for i in range(4):
                 rs[f, i] = mm(4 * f + i, 128, V("AQ", 128 * i, 128 * i + 128), V("AP", 128 * i, 128 * i + 128),
                               b("XQ", 128 * f, 128 * f + 128), b("XS", 128 * f, 128 * f + 128))
-        for f in range(2):
-            for i in range(4):
                 act(b("Z", 512 * f + 128 * i, 512 * f + 128 * i + 128), rs[f, i], 0.05)
         for f in range(2):
             lo, hi = 128 * f, 128 * f + 128
@@ -457,6 +524,7 @@ def rank_program(g, core, T, topo):
                    V("E%d" % t, 512 * f + i, 512 * f + 512, 4), A.add)
             qz(V("QO%d" % t, lo, hi), V("QS%d" % t, lo, hi), b("HT", 512 * f, 512 * f + 512))
             rs[f] = mm(f, 128, V("UQ"), V("UP"), V("QO%d" % t, lo, hi), V("QS%d" % t, lo, hi))
+            tt(V("S%d" % t, lo, hi), rs[f], b("PB", lo, hi), A.add)
             if t == 2:
                 yp = mm(2 + f, 128, V("WQ"), V("WP"), V("QO2", lo, hi), V("QS2", lo, hi))
                 dma("s", T.oc[:, 4 * lo:4 * hi], ap(V("QO2", lo, hi)).bitcast(dt.uint8), [V("QO2", lo, hi)], [])
@@ -465,59 +533,50 @@ def rank_program(g, core, T, topo):
                     dma("s" if f == 0 or k < 2 else "a", T.osc[4 * k:4 * k + 4, lo:hi], ap(sc), [sc], [])
                 act(V("YB", lo, hi), yp)
                 dma("a", T.y[:, lo:hi], ap(V("YB", lo, hi)), [V("YB", lo, hi)], [])
-        for f in range(2):
-            tt(V("S%d" % t, 128 * f, 128 * f + 128), rs[f], b("PB", 128 * f, 128 * f + 128), A.add)
         if t == 2:
             row = V("S2", 0, 256, 1, 0, 1)
             dma("s", T.g[:], ap(row), [row], [])
 
-    def quantise_a(i):
-        qz(V("AQ", 128 * i, 128 * i + 128), V("AP", 128 * i, 128 * i + 128), V("AT", 512 * i, 512 * i + 512))
-
     prep_lists(1, V("MSG1"))
-    ev = spread(V("MSG1"), lambda s: V("LM1", 4 * s, 4 * s + 4), "m1", "lm1")
-    wait("s", [ev])
+    sent = spread(V("MSG1"), lambda s: V("LM1", 4 * s, 4 * s + 4), "m1", "lm1", V("LM1"))
     for i in (0, 1):
-        load("s", V("AT", 1024 * i, 1024 * i + 1024), T.a[:, 1024 * i:1024 * i + 1024])
+        load("s", V("AT", 1024 * i, 1024 * i + 1024), T.a[:, 1024 * i:1024 * i + 1024], LONG, [sent])
     w = 4
     while w < 512:
         act(V("UT", w, 2 * w), V("UT", 0, w))
         w *= 2
     qz(V("UQ"), V("UP"), V("UT"))
     qz(V("QO0"), V("QS0"), V("E0"))
-    ps = mm(0, 256, V("UQ"), V("UP"), V("QO0"), V("QS0"))
-    act(V("S0"), ps)
+    act(V("S0"), mm(0, 256, V("UQ"), V("UP"), V("QO0"), V("QS0")))
     prep_nodes(1, V("MSG2"))
-    spread(V("MSG2"), lambda s: V("LM2", 2 * s, 2 * s + 2), "m2", "lm2")
+    spread(V("MSG2"), lambda s: V("LM2", 2 * s, 2 * s + 2), "m2", "lm2", V("LM2"))
     prep_lists(2, V("MSG3", 0, 4))
     decode_lists(1)
-    ev = scores_out(1)
-    wait("s", [ev])
-    load("s", V("E1"), T.e1[:])
+    sent = scores_out(1)
+    load("s", V("E1"), T.e1[:], LONG, [sent])
+    prep_nodes(2, V("MSG3", 4, 6))
+    spread(V("MSG3"), lambda s: V("LM3", 6 * s, 6 * s + 6), "m3", "lm3", V("LM3"))
     value_rows(1)
     decode_ties(1)
-    prep_nodes(2, V("MSG3", 4, 6))
-    spread(V("MSG3"), lambda s: V("LM3", 6 * s, 6 * s + 6), "m3", "lm3")
-    ties_end(1)
     own_columns(1)
     qz(V("QW0", 0, 256), V("QP0", 0, 256), V("E0"))
-    ev = choose_and_send(1)
-    wait("s", [ev])
-    load("s", V("E2"), T.e2[:])
-    load("s", V("WT"), T.w[:])
-    own_list(1)
     for i in range(4):
-        quantise_a(i)
-    new_columns(1, lambda: (own_numbers(1), decode_lists(2)))
+        qz(V("AQ", 128 * i, 128 * i + 128), V("AP", 128 * i, 128 * i + 128), V("AT", 512 * i, 512 * i + 512))
+    sent = choose_and_send(1)
+    load("s", V("E2"), T.e2[:], LONG, [sent])
+    load("s", V("WT"), T.w[:], LONG, [sent])
+    own_list(1)
+    new_columns(1)
+    decode_lists(2)
     scores_out(2)
     value_rows(2)
     decode_ties(2)
-    qz(V("QW1", 0, 256), V("QP1", 0, 256), V("HT1"))
-    ties_end(2)
     own_columns(2)
+    qz(V("QW1", 0, 256), V("QP1", 0, 256), V("HT1"))
     qz(V("WQ"), V("WP"), V("WT"))
     choose_and_send(2)
     own_list(2)
-    new_columns(2, lambda: own_numbers(2))
+    new_columns(2)
+    lay()
     for sem in sorted(total):
         wait("s", [(sem, total[sem], {})])

@@ -36,16 +36,16 @@ _buf(H, MSG1=4, MSG2=2, MSG3=6, LM1=12, LM2=6, LM3=18)
 _buf(F, U1=32, U2=32, Z1=1024, Z2=1024, YB=256, S0=256, S1=256, S2=256, PR1=256, PR2=256, PB1=256, PB2=256)
 _buf(I, RAW1=64, RAW2=64)
 _area(H, DUP=8)
-_area(I, PI=1, PJ=4, DUPI=8, TRI=8)
-_area(F, ZERO=64, NEG=8, KCOL=4, P15F=4, P15E=4, XEO=8, GCOL=4, GD=4, BC=4, TR=8, ZB=368, HI=4, HJ=4)
-_area(F, **_each(RL=64, RN=64, T2=64, TN=64, M1=32, MN=32, LW=8, LOC=4, KFN=8, KSC=8, LCN=8, OL=8, OB=8, CD=8, CG=8, LF=8, RB=128,
-                 VR=128, KF=32, KL=24, KK=32, G=128, TG=128, V3=24, AB=24, AC=24, DE=24, VA=24, L3=24, X1=8, LO=8, TB=32, EC=32,
-                 LT=8, AA=8, W=640, WD=128, TW=128, LS=4, M16=16, MM=8, EQ=32, KEY=32, K16=16, KM=8, TB2=32, EC2=32, SV=8, NW=8,
-                 NP=8, BP=8, VAL=24, BK=72, SA=24, SB=8, KS=8, CA=8, CO=8, CH=8, XC=8, A2=32, TA=32, XT=16, KQ=32, PP=32, P16=16,
-                 PA=8))
+_area(I, PI=1, PJ=4, DUPI=8)
+_area(F, ZERO=64, NEG=8, KCOL=4, P15F=4, SL=4, XEO=8, GCOL=4, GD=4, BC=4, TR=8, ZB=368)
+_area(F, **_each(CUT=64, HW=32, RL=32, RN=64, T2=32, TN=64, M1=8, MN=32, LOC=4, KFN=8, KSC=8, LCN=8, OL=8, OB=8, CD=8, CG=8, LF=8,
+                 RB=128, VR=128, KF=32, KL=24, KK=32, G=128, TG=128, V3=24, AB=24, AC=24, DE=24, VA=24, L3=24, X1=8, LO=8, TB=32,
+                 EC=32, LT=8, AA=8, W=1552, WD=128, TW=128, PF=16, M16=16, MM=8, EQ=32, KEY=32, K16=16, KM=8, TB2=32, EC2=32, SV=8,
+                 NW=8, NP=8, BP=8, VAL=24, BK=72, SA=24, SB=8, KS=8, CA=8, CO=8, CH=8, XC=8, A2=32, TA=32, XT=16, KQ=32, PP=32,
+                 P16=16, PA=8))
 _area(I, **_each(TI=64, TJ=64, WN=8, KN=8, CL=4, LI=8, KC=8, KD=32, LN=8))
 _area(H, **_each(LU=8, OF=8, PO=12, XO=16))
-NDMA = 36
+NDMA = 48
 SEMAPHORES = ["qv", "qa", "qt", "qg", "m3", "lm3"] + ["d%d" % i for i in range(NDMA)] + [
     x + str(t) for t in (1, 2) for x in ("m", "lm", "v", "lv", "c", "lc", "s", "ls")]
 
@@ -58,7 +58,7 @@ def rank_program(g, core, T, topo):
     slot_at = [(me - d) % 4 - 1 for d in others]
     qs = {"v": g.vector, "a": g.scalar, "t": g.tensor, "g": g, "s": g.sync}
     hist, know, cnt, total = {}, {q: {} for q in qs}, {}, {}
-    nodes, past, last = [], {}, {}
+    nodes, past, last, hold = [], {}, {}, [()]
 
     def V(name, c0=0, c1=None, st=1, p0=0, p1=128):
         return (name, p0, p1, c0, PLACE[name][2] if c1 is None else c1, st)
@@ -90,7 +90,7 @@ def rank_program(g, core, T, topo):
             deps |= {j for (o, ow, j) in past.get(r[0], []) if (w or ow) and clash(r, o)}
         for r, w in regions(reads, writes):
             past.setdefault(r[0], []).append((r, w, i))
-        prev = last.get("g") if "g" in opts else None
+        prev = list(hold[0]) + ([last["g"]] if "g" in opts and "g" in last else [])
         if "g" in opts:
             last["g"] = i
         nodes.append({"opts": opts, "rd": reads, "wr": writes, "cost": cost, "dur": cost if dur is None else dur,
@@ -144,10 +144,9 @@ def rank_program(g, core, T, topo):
                 succ[j].append(i)
         high = [0.0] * n
         for i in range(n - 1, -1, -1):
-            high[i] = nodes[i]["dur"] + max([WAIT + high[j] for j in succ[i]] + [0.0])
-            p = nodes[i]["prev"]
-            if p is not None:
-                high[p] = max(high[p], nodes[p]["cost"] + high[i])
+            high[i] = nodes[i]["dur"] + max([WAIT + high[j] for j in succ[i]] + [high[i]])
+            for p in nodes[i]["prev"]:
+                high[p] = max(high[p], nodes[p]["cost"] + high[i] - nodes[p]["dur"])
         left = [len(nd["deps"]) for nd in nodes]
         ready = {i for i in range(n) if left[i] == 0}
         free, fin, done = {}, [0.0] * n, set()
@@ -155,7 +154,7 @@ def rank_program(g, core, T, topo):
             cand = []
             for i in ready:
                 nd = nodes[i]
-                if nd["prev"] is not None and nd["prev"] not in done:
+                if any(p not in done for p in nd["prev"]):
                     continue
                 s = max([fin[j] + WAIT for j in nd["deps"]] + [0.0])
                 start, q = min((max(s, free.get(q, 0.0)) if q != "x" else s, "vatgsx".index(q)) for q in nd["opts"])
@@ -221,6 +220,10 @@ def rank_program(g, core, T, topo):
     def ms(o, c):
         op("v", lambda: g.vector.memset(ap(o), c), [], [o], width(o))
 
+    def fill(o, base, step=0, rise=0):
+        n = width(o)
+        op("g", lambda: g.iota(ap(o), [[step, n]], base, rise, allow_small_or_imprecise_dtypes=True), [], [o], 130 + 2 * n)
+
     def gat(o, w, off):
         op("v", lambda: g.vector.tensor_copy(ap(o), ap(w).indirect(ap(off))), [w, off], [o], 50 + 1.5 * width(o))
 
@@ -230,7 +233,7 @@ def rank_program(g, core, T, topo):
         op("a", lambda: g.scalar.activation(ap(so), ap(sw).indirect(ap(off)), AF.Copy), [sw, off], [so], 70 + 1.5 * width(qo))
 
     def qz(q, s, a):
-        op("v", lambda: g.vector.quantize_mx(ap(q), ap(s), ap(a)), [a], [q, s], 0.25 * width(a))
+        return op("v", lambda: g.vector.quantize_mx(ap(q), ap(s), ap(a)), [a], [q, s], 0.25 * width(a))
 
     def act(o, a, scale=1.0):
         op("a", lambda: g.scalar.activation(ap(o), ap(a), AF.Copy, scale=scale), [a], [o], width(a))
@@ -281,55 +284,53 @@ def rank_program(g, core, T, topo):
     def bufs(t):
         return lambda name, *a: V(name + str(t), *a)
 
-    load("s", V("RAW1", p0=0, p1=16), T.p1[:], LOCAL)
-    load("a", V("RAW1", p0=16, p1=32), T.p1[:], LOCAL)
+    for i in range(8):
+        load("sa"[i % 2], V("RAW1", p0=16 * i, p1=16 * i + 16), T.p1[:], LOCAL)
     load("s", V("E0", 0, 512), T.e0[:, 0:512], FIRST)
     load("a", V("UT", 0, 4), T.u[:, 0:4], FIRST)
     load("a", V("E0", 512, 1024), T.e0[:, 512:1024], FIRST)
-    load("s", V("RAW2", p0=0, p1=16), T.p2[:], FIRST)
-    load("s", V("RAW2", p0=16, p1=32), T.p2[:], FIRST)
+    for i in range(8):
+        load("s", V("RAW2", p0=16 * i, p1=16 * i + 16), T.p2[:], FIRST)
     op("g", lambda: g.iota(ap(V("PI")), [[0, 1]], 0, 1), [], [V("PI")], 100)
     op("g", lambda: g.iota(ap(V("DUPI")), [[16, 4], [0, 2]], 0, 0), [], [V("DUPI")], 100)
-    op("g", lambda: g.iota(ap(V("TRI")), [[1, 8]], 257, 0), [], [V("TRI")], 100)
-    ms(V("ZERO"), 0.0)
+    fill(V("ZERO"), 0)
+    fill(V("TR"), 257, 1, 8)
+    fill(V("NEG"), -1)
+    fill(V("ZB"), 0)
+    for t in (1, 2):
+        fill(V("W%d" % t, 0, 64), 0)
     for j, m in enumerate((15, 3, 1, 96)):
         ts(V("PJ", j, j + 1), V("PI"), m, A.bitwise_and)
     p15, kcol = V("P15F", 0, 1), V("KCOL", 0, 1)
     tc(p15, V("PJ", 0, 1))
     tc(kcol, V("PJ", 1, 2))
-    ts(V("HJ", 0, 1), p15, 8.0, A.is_ge, 255.0, A.mult)
     tc(V("XEO", 4, 5), V("PJ", 2, 3))
     ts(V("GCOL", 0, 1), V("PJ", 3, 4), 8.0, A.mult)
+    lin(V("SL", 0, 1), V("GCOL", 0, 1), bias=-1.0)
+    lin(V("SL", 1, 2), V("GCOL", 0, 1), bias=float(P))
+    ts(V("SL", 2, 3), V("GCOL", 0, 1), 257 * (3 * P - 1) / P, A.mult, float(257 * 3 * P), A.add)
+    lin(V("SL", 3, 4), V("GCOL", 0, 1), -1.0, 1024.0)
     lin(V("GD", 0, 1), V("GCOL", 0, 1), bias=float(-P * me))
-    lin(V("HI", 0, 1), V("HJ", 0, 1), bias=1.0)
-    lin(V("P15E", 0, 1), p15, scale=8.0)
     lin(V("XEO", 0, 1), V("XEO", 4, 5), -1.0, 1.0)
     ts(V("DUP"), V("DUPI"), p15, A.add)
-    ts(V("TR"), V("TRI"), V("P15E", 0, 1), A.add)
-    ms(V("NEG"), -1.0)
     for k in range(4):
         ms(blk(k, "BC", 0, 1), float(255 + 64 * others.index(k)) if k != me else 0.0)
-    ms(V("ZB"), 0.0)
-    for t in (1, 2):
-        ms(V("W%d" % t, 0, 64), 0.0)
 
     def prep_lists(t, pk):
         b = bufs(t)
-        for s in range(4):
-            ts(blk(s, "TI%d" % t), V("RAW%d" % t, p0=0, p1=32), 1024 - 256 * s, A.add)
-        ts(b("TJ"), b("TI"), 1023, A.bitwise_and)
-        for gg in range(2):
-            for h in range(2):
-                ts(b("RL", 32 * gg + 16 * h, 32 * gg + 16 * h + 16), b("TJ", 32 * gg + h, 32 * gg + 32, 2), V("HI", 0, 1), A.mult)
+        ts(b("CUT"), V("RAW%d" % t), V("SL", 0, 1), A.max, V("SL", 1, 2), A.min)
+        lin(b("HW"), b("CUT", 32, 64), 256.0)
+        for h in range(2):
+            tt(b("RL", 16 * h, 16 * h + 16), b("CUT", h, 32, 2), b("HW", h, 32, 2), A.add)
         tr(b("T2"), b("RL"))
-        tt(b("M1"), b("T2", 0, 64, 2), b("T2", 1, 64, 2), A.min)
-        for gg in range(2):
-            tt(b("LW", gg, 8, 2), b("M1", 16 * gg, 16 * gg + 8, 2), b("M1", 16 * gg + 1, 16 * gg + 8, 2), A.min)
-        tt(b("LOC"), b("LW", 0, 4), b("LW", 4, 8), A.add)
-        tc(pk, b("LOC"))
+        tt(b("M1"), b("T2", 0, 16, 2), b("T2", 1, 16, 2), A.add)
+        tt(b("LOC"), b("M1", 0, 8, 2), b("M1", 1, 8, 2), A.add)
+        ts(pk, b("LOC"), V("SL", 2, 3), A.subtract)
 
     def prep_nodes(t, kcols):
         b = bufs(t)
+        ts(b("TI"), V("RAW%d" % t), V("SL", 3, 4), A.add)
+        ts(b("TJ"), b("TI"), 1023, A.bitwise_and)
         for h in range(2):
             ts(b("RN", 32 * h, 32 * h + 32), b("TJ", h, 64, 2), 4.0, A.mult, kcol, A.add)
         tr(b("TN"), b("RN"))
@@ -361,18 +362,12 @@ def rank_program(g, core, T, topo):
         i = others.index(d)
         return blk(me, "LM1", 4 * i, 4 * i + 4) if t == 1 else blk(me, "LM3", 6 * i, 6 * i + 4)
 
-    def ties(t, d):
-        if d == me:
-            return V("MSG2") if t == 1 else V("MSG3", 4, 6)
-        i = others.index(d)
-        return V("LM2", 2 * i, 2 * i + 2) if t == 1 else V("LM3", 6 * i + 4, 6 * i + 6)
-
     def decode_lists(t):
         b = bufs(t)
         for d in [me] + others:
             tc(blk(d, "CL%d" % t), packed(t, d))
-        ts(b("LI", 0, 4), b("CL"), 255, A.bitwise_and)
-        ts(b("LI", 4, 8), b("CL"), 8, A.logical_shift_right)
+        ts(b("LI", 0, 8, 2), b("CL"), 255, A.bitwise_and)
+        ts(b("LI", 1, 8, 2), b("CL"), 8, A.logical_shift_right)
         tc(b("LU"), b("LI"))
 
     def value_rows(t):
@@ -387,8 +382,14 @@ def rank_program(g, core, T, topo):
 
     def decode_ties(t):
         b = bufs(t)
-        for d in range(4):
-            tc(b("KC", 2 * d, 2 * d + 2), ties(t, d))
+        slot = {d: i for i, d in enumerate(others + [me])}
+        if t == 1:
+            tc(b("KC", 0, 6), V("LM2"))
+            tc(b("KC", 6, 8), V("MSG2"))
+        else:
+            for i in range(3):
+                tc(b("KC", 2 * i, 2 * i + 2), V("LM3", 6 * i + 4, 6 * i + 6))
+            tc(b("KC", 6, 8), V("MSG3", 4, 6))
         for i in range(4):
             ts(b("KD", i, 32, 4), b("KC"), 2 * (3 - i), A.logical_shift_right, 3, A.bitwise_and)
         tc(b("KF"), b("KD"))
@@ -397,7 +398,7 @@ def rank_program(g, core, T, topo):
             for s in range(4):
                 if s != d:
                     i = (s - me) % 4
-                    lin(sub(ka, 8 * i, 8 * i + 8, d), blk(s, "KF%d" % t, 8 * d, 8 * d + 8))
+                    lin(sub(ka, 8 * i, 8 * i + 8, d), blk(s, "KF%d" % t, 8 * slot[d], 8 * slot[d] + 8))
         for i in range(3):
             tt(b("KL", 8 * i, 8 * i + 8), sub(ka, 8 * i + 8, 8 * i + 16), sub(ka, 0, 8), A.is_lt)
         lin(b("KK"), ka, -1.0, 4.0)
@@ -427,23 +428,27 @@ def rank_program(g, core, T, topo):
         ni = zb(t, 0, 32)
         prefix(b("LO"), V("NEG"), ni, zb(t, 64, 40), b("TB"), b("EC"))
         tt(b("LT"), b("LO"), V("TR"), A.mult)
-        tt(b("AA"), b("LT"), sub(ni, 0, 8), A.subtract)
         for h in range(2):
-            ts(b("OF", h, 8, 2), b("AA", 4 * h, 4 * h + 4), b("EC", 7, 8), A.subtract, -1.0, A.add)
+            tt(b("AA", h, 8, 2), b("LT", 4 * h, 4 * h + 4), sub(ni, 4 * h, 4 * h + 4), A.subtract)
+        ts(b("OF"), b("AA"), b("EC", 7, 8), A.subtract, -1.0, A.add)
         op("v", lambda: g.vector.tensor_copy(ap(b("W")).indirect(ap(b("OF"))), ap(b("VR"))), [b("VR"), b("OF")], [b("W")], 450)
         gat(b("WD"), b("W", 0, 64), V("DUP"))
         tr(b("TW"), b("WD"))
-        tt(b("LS"), b("TW", 0, 128, 32), b("TW", 16, 128, 32), A.add)
         cols = {d: (4 * i, 4 * i + 4) for i, d in enumerate(others)}
+        pf = "PF%d" % t
         for d in others:
-            for k in (d // 2 * 2, d // 2 * 2 + 1):
-                tc(blk(k, "PO%d" % t, *cols[d]), blk(d, "LS%d" % t))
+            lo, hi = cols[d]
+            tt(blk(d, pf, lo, hi), blk(d, "TW%d" % t, 0, 128, 32), blk(d, "TW%d" % t, 16, 128, 32), A.add)
+            k = d // 2 * 2 + 1 - d % 2
+            if d == others[2]:
+                tt(blk(k, pf, lo, hi), blk(d, "TW%d" % t, 0, 128, 32), blk(d, "TW%d" % t, 16, 128, 32), A.add)
+            else:
+                lin(blk(k, pf, lo, hi), blk(d, pf, lo, hi))
         for half in range(2):
-            runs = sorted(cols[d] for d in others if d // 2 == half)
-            if len(runs) == 2 and runs[0][1] == runs[1][0]:
-                runs = [(runs[0][0], runs[1][1])]
-            for lo, hi in runs:
-                tc(V("PO%d" % t, lo, hi, 1, 64 - 64 * half, 128 - 64 * half), V("PO%d" % t, lo, hi, 1, 64 * half, 64 * half + 64))
+            own = [cols[d] for d in others if d // 2 == half]
+            lo, hi = min(own)[0], max(own)[1]
+            lin(V(pf, lo, hi, 1, 64 - 64 * half, 128 - 64 * half), V(pf, lo, hi, 1, 64 * half, 64 * half + 64))
+        tc(b("PO"), b("PF", 0, 12))
         pick(b("SQ"), b("SS"), V("QO%d" % (t - 1)), V("QS%d" % (t - 1)), b("PO"))
         for src, land, sem, turn in (("SQ", "QW", "c", 0), ("SS", "QP", "s", 3)):
             trs = []
@@ -520,9 +525,12 @@ def rank_program(g, core, T, topo):
         for f in range(2):
             lo, hi = 128 * f, 128 * f + 128
             for i in range(4):
+                if t == 2 and f == 1 and i == 1:
+                    hold[0] = (first,)
                 tt(b("HT", 512 * f + i, 512 * f + 512, 4), b("Z", 512 * f + 128 * i, 512 * f + 128 * i + 128),
                    V("E%d" % t, 512 * f + i, 512 * f + 512, 4), A.add)
-            qz(V("QO%d" % t, lo, hi), V("QS%d" % t, lo, hi), b("HT", 512 * f, 512 * f + 512))
+            first = qz(V("QO%d" % t, lo, hi), V("QS%d" % t, lo, hi), b("HT", 512 * f, 512 * f + 512))
+            hold[0] = ()
             rs[f] = mm(f, 128, V("UQ"), V("UP"), V("QO%d" % t, lo, hi), V("QS%d" % t, lo, hi))
             tt(V("S%d" % t, lo, hi), rs[f], b("PB", lo, hi), A.add)
             if t == 2:
@@ -530,17 +538,16 @@ def rank_program(g, core, T, topo):
                 dma("s", T.oc[:, 4 * lo:4 * hi], ap(V("QO2", lo, hi)).bitcast(dt.uint8), [V("QO2", lo, hi)], [])
                 for k in range(4):
                     sc = V("QS2", lo, hi, 1, 32 * k, 32 * k + 4)
-                    dma("s" if f == 0 or k < 2 else "a", T.osc[4 * k:4 * k + 4, lo:hi], ap(sc), [sc], [])
-                act(V("YB", lo, hi), yp)
-                dma("a", T.y[:, lo:hi], ap(V("YB", lo, hi)), [V("YB", lo, hi)], [])
+                    dma("s", T.osc[4 * k:4 * k + 4, lo:hi], ap(sc), [sc], [])
+                lin(V("YB", lo, hi), yp)
+                dma("a", T.y[:, lo:hi], ap(V("YB", lo, hi)), [V("YB", lo, hi)], [], dur=LOCAL + 0.6)
         if t == 2:
             row = V("S2", 0, 256, 1, 0, 1)
             dma("s", T.g[:], ap(row), [row], [])
 
     prep_lists(1, V("MSG1"))
     sent = spread(V("MSG1"), lambda s: V("LM1", 4 * s, 4 * s + 4), "m1", "lm1", V("LM1"))
-    for i in (0, 1):
-        load("s", V("AT", 1024 * i, 1024 * i + 1024), T.a[:, 1024 * i:1024 * i + 1024], LONG, [sent])
+    load("s", V("AT", 0, 1024), T.a[:, 0:1024], LONG, [sent])
     w = 4
     while w < 512:
         act(V("UT", w, 2 * w), V("UT", 0, w))
@@ -552,29 +559,38 @@ def rank_program(g, core, T, topo):
     spread(V("MSG2"), lambda s: V("LM2", 2 * s, 2 * s + 2), "m2", "lm2", V("LM2"))
     prep_lists(2, V("MSG3", 0, 4))
     decode_lists(1)
-    sent = scores_out(1)
-    load("s", V("E1"), T.e1[:], LONG, [sent])
+    scores = scores_out(1)
+    load("s", V("AT", 1024, 2048), T.a[:, 1024:2048], LONG, [scores])
+    load("s", V("E1"), T.e1[:], LONG, [scores])
     prep_nodes(2, V("MSG3", 4, 6))
     spread(V("MSG3"), lambda s: V("LM3", 6 * s, 6 * s + 6), "m3", "lm3", V("LM3"))
+    hold[0] = (scores - 1,)
     value_rows(1)
+    hold[0] = ()
     decode_ties(1)
     own_columns(1)
     qz(V("QW0", 0, 256), V("QP0", 0, 256), V("E0"))
+    sent = choose_and_send(1)
+    hold[0] = (sent,)
     for i in range(4):
         qz(V("AQ", 128 * i, 128 * i + 128), V("AP", 128 * i, 128 * i + 128), V("AT", 512 * i, 512 * i + 512))
-    sent = choose_and_send(1)
-    load("s", V("E2"), T.e2[:], LONG, [sent])
-    load("s", V("WT"), T.w[:], LONG, [sent])
+    hold[0] = ()
     own_list(1)
     new_columns(1)
     decode_lists(2)
-    scores_out(2)
+    scores = scores_out(2)
+    load("s", V("WT"), T.w[:], LONG, [scores])
+    load("s", V("E2"), T.e2[:], LONG, [scores])
+    hold[0] = (scores - 1,)
     value_rows(2)
     decode_ties(2)
-    own_columns(2)
     qz(V("QW1", 0, 256), V("QP1", 0, 256), V("HT1"))
+    hold[0] = ()
+    own_columns(2)
+    sent = choose_and_send(2)
+    hold[0] = (sent,)
     qz(V("WQ"), V("WP"), V("WT"))
-    choose_and_send(2)
+    hold[0] = ()
     own_list(2)
     new_columns(2)
     lay()

@@ -4,7 +4,7 @@ from concourse.mybir import dt, AluOpType as A, ActivationFunctionType as AF
 P, CAPP = 256, 64
 TINY = 2.0 ** -100
 STEP = 2.0 ** -24 * (1 + 2.0 ** -10)
-WAIT, LEAST, ISSUE, WAY = 0.12, 0.08, 0.8, 3.5
+WAIT, LEAST, ISSUE, WAY, ONCE = 0.13, 0.09, 0.8, 2.9, 1.5
 LOCAL, FIRST, LONG = 2.3, 3.8, 5.5
 F, B, I, H, C, S8 = "float32", "bfloat16", "int32", "uint16", "float8_e4m3fn_x4", "uint8"
 SCRATCH = {"PS": ("psum", [128, 4096], F)}
@@ -30,24 +30,24 @@ def _each(**names):
 
 
 _buf(B, UT=512, E0=1024, AT=2048, WT=512, E1=1024, E2=1024, HT1=1024, HT2=1024)
-_buf(C, UQ=128, AQ=512, WQ=128, QO0=256, QO1=256, QO2=256, QW0=448, QW1=448, SQ1=192, SQ2=192, XQ1=256, XQ2=256)
-_buf(S8, UP=128, AP=512, WP=128, QS0=256, QS1=256, QS2=256, QP0=448, QP1=448, SS1=192, SS2=192, XS1=256, XS2=256)
-_buf(H, MSG1=4, MSG2=2, MSG3=6, LM1=12, LM2=6, LM3=18)
-_buf(F, U1=32, U2=32, Z1=1024, Z2=1024, YB=256, S0=256, S1=256, S2=256, PR1=256, PR2=256, PB1=256, PB2=256)
+_buf(C, UQ=128, AQ=512, WQ=128, QO0=256, QO1=256, QO2=256, QW0=192, QW1=192, SQ1=192, SQ2=192)
+_buf(S8, UP=128, AP=512, WP=128, QS0=256, QS1=256, QS2=256, QP0=192, QP1=192, SS1=192, SS2=192)
+_buf(H, MSG1=8, MSG2=2, LM1=24, LM2=6, LS2=8, ST2=6, LC2=6, LU1=8, LU2=8)
+_buf(F, U1=32, U2=32, Z1=1792, Z2=1792, YB=256, S0=256, S1=256, S2=256, PR1=256, PR2=256, PB1=256, PB2=256)
 _buf(I, RAW1=64, RAW2=64)
-_area(H, DUP=8)
-_area(I, PI=1, PJ=4, DUPI=8)
-_area(F, ZERO=64, NEG=8, KCOL=4, P15F=4, SL=4, XEO=8, GCOL=4, GD=4, BC=4, TR=8, ZB=368)
-_area(F, **_each(CUT=64, HW=32, RL=32, RN=64, T2=32, TN=64, M1=8, MN=32, LOC=4, KFN=8, KSC=8, LCN=8, OL=8, OB=8, CD=8, CG=8, LF=8,
-                 RB=128, VR=128, KF=32, KL=24, KK=32, G=128, TG=128, V3=24, AB=24, AC=24, DE=24, VA=24, L3=24, X1=8, LO=8, TB=32,
-                 EC=32, LT=8, AA=8, W=1552, WD=128, TW=128, PF=16, M16=16, MM=8, EQ=32, KEY=32, K16=16, KM=8, TB2=32, EC2=32, SV=8,
+_area(H, DUP=8, PERM=2, PV=2)
+_area(I, PI=1, PJ=8, DUPI=8, PERMI=2, KC=8, KD=64)
+_area(F, ZERO=64, NEG=40, KCOL=4, SL=4, XEO=8, GD=4, BC=4, TR=8, ZB=608, PF32=8, J4=64, SEG4=64, J16=128, MASK=128,
+      SEG16=128, SUF=32, J32=32, IDT=256, PKC=16, KF=64)
+_area(F, **_each(RL=64, T2=64, SCL=64, EQN=64, KQN=64, TK=64, SK=64, PK=16, LCN=8, OL=8, OB=8, CD=8, CG=8,
+                 VR=128, KK=32, G=128, SG=128, V4=32, AB=32, AC=32, DE=32, VA=32, L4=32, NI=40, RT=40, TJ=40, TA1=1, SFX=32, LT=8,
+                 AA=8, W=1552, WD=128, TW=128, PF=16, M16=16, MM=8, EQ=32, KEY=32, K16=16, KM=8, TB2=32, EC2=32, SV=8,
                  NW=8, NP=8, BP=8, VAL=24, BK=72, SA=24, SB=8, KS=8, CA=8, CO=8, CH=8, XC=8, A2=32, TA=32, XT=16, KQ=32, PP=32,
                  P16=16, PA=8))
-_area(I, **_each(TI=64, TJ=64, WN=8, KN=8, CL=4, LI=8, KC=8, KD=32, LN=8))
-_area(H, **_each(LU=8, OF=8, PO=12, XO=16))
-NDMA = 48
-SEMAPHORES = ["qv", "qa", "qt", "qg", "m3", "lm3"] + ["d%d" % i for i in range(NDMA)] + [
-    x + str(t) for t in (1, 2) for x in ("m", "lm", "v", "lv", "c", "lc", "s", "ls")]
+_area(H, **_each(OF=8, PO=12, XO=16))
+NDMA = 60
+SEMAPHORES = ["qv", "qa", "qt", "qg", "m1", "lm1", "m2", "lm2", "m3", "lm3"] + ["d%d" % i for i in range(NDMA)] + [
+    x + str(t) for t in (1, 2) for x in ("v", "lv", "c", "lc", "s", "ls")]
 
 
 def rank_program(g, core, T, topo):
@@ -189,6 +189,9 @@ def rank_program(g, core, T, topo):
     def tt(o, a, b, f):
         op("v", lambda: g.vector.tensor_tensor(ap(o), ap(a), ap(b), f), [a, b], [o], width(a) * (1 if a[0] == "PS" else 2))
 
+    def tti(o, w, off, b, f):
+        op("v", lambda: g.vector.tensor_tensor(ap(o), ap(w).indirect(ap(off)), ap(b), f), [w, off, b], [o], 50 + 1.5 * width(b))
+
     def ts(o, a, s1, f1, s2=None, f2=None):
         if f2 is None:
             op("v", lambda: g.vector.tensor_scalar(ap(o), ap(a), sv(s1), None, f1), [a] + cols_of(s1), [o], width(a))
@@ -211,8 +214,8 @@ def rank_program(g, core, T, topo):
             return g.scalar.activation(ap(o), ap(a), AF.Identity, scale=sv(scale), bias=sv(bias))
         push({"v": ("op", on_v), "a": ("op", on_a)}, [a] + cols_of(scale, bias), [o], us(width(a)))
 
-    def scan(o, a, b):
-        op("v", lambda: g.vector.tensor_tensor_scan(ap(o), ap(a), ap(b), 0.0, A.add, A.add), [a, b], [o], width(a))
+    def scan(o, a, b, f0=A.add, f1=A.add):
+        op("v", lambda: g.vector.tensor_tensor_scan(ap(o), ap(a), ap(b), 0.0, f0, f1), [a, b], [o], width(a))
 
     def tr(o, a):
         op("v", lambda: g.vector.transpose(ap(o), ap(a)), [a], [o], width(a))
@@ -220,26 +223,26 @@ def rank_program(g, core, T, topo):
     def ms(o, c):
         op("v", lambda: g.vector.memset(ap(o), c), [], [o], width(o))
 
-    def fill(o, base, step=0, rise=0):
+    def fill(o, base, step=0, rise=0, pattern=None):
         n = width(o)
-        op("g", lambda: g.iota(ap(o), [[step, n]], base, rise, allow_small_or_imprecise_dtypes=True), [], [o], 130 + 2 * n)
+        op("g", lambda: g.iota(ap(o), pattern or [[step, n]], base, rise, allow_small_or_imprecise_dtypes=True), [], [o], 130 + 2 * n)
 
     def gat(o, w, off):
         op("v", lambda: g.vector.tensor_copy(ap(o), ap(w).indirect(ap(off))), [w, off], [o], 50 + 1.5 * width(o))
 
+    def gata(o, w, off):
+        op("a", lambda: g.scalar.activation(ap(o), ap(w).indirect(ap(off)), AF.Copy), [w, off], [o], 70 + 1.5 * width(o))
+
     def pick(qo, so, qw, sw, off):
         op("v", lambda: g.vector.tensor_copy(ap(qo).bitcast(dt.uint32), ap(qw).bitcast(dt.uint32).indirect(ap(off))), [qw, off], [qo],
            50 + 1.5 * width(qo))
-        op("a", lambda: g.scalar.activation(ap(so), ap(sw).indirect(ap(off)), AF.Copy), [sw, off], [so], 70 + 1.5 * width(qo))
+        gata(so, sw, off)
 
     def qz(q, s, a):
         return op("v", lambda: g.vector.quantize_mx(ap(q), ap(s), ap(a)), [a], [q, s], 0.25 * width(a))
 
     def act(o, a, scale=1.0):
         op("a", lambda: g.scalar.activation(ap(o), ap(a), AF.Copy, scale=scale), [a], [o], width(a))
-
-    def plus(o, a, bias):
-        op("a", lambda: g.scalar.activation(ap(o), ap(a), AF.Identity, bias=ap(bias)), [a, bias], [o], width(a))
 
     def mm(b, n, wq, ws, xq, xs):
         o = V("PS", 512 * b, 512 * b + n)
@@ -263,8 +266,10 @@ def rank_program(g, core, T, topo):
         def call():
             g.remote_dma_fused(transfers, local_sem=T.sem[lsem])
             return lsem, count
-        i = push({"g": ("remote", call)}, [src], [], ISSUE, ISSUE + 1.0)
-        push({"x": None}, [], [landing], 0.0, WAY - 1.0, [i])
+        more = 0.0 if cnt.get("remote") else ONCE
+        cnt["remote"] = 1
+        i = push({"g": ("remote", call)}, [src], [], ISSUE + more, ISSUE + 0.5 + more)
+        push({"x": None}, [], [landing], 0.0, WAY - ISSUE - 0.5, [i])
         total[sem] = arrivals
         hist.setdefault(landing[0], []).append((landing, True, (sem, arrivals, {sem: arrivals})))
         return i
@@ -275,11 +280,24 @@ def rank_program(g, core, T, topo):
             dst_ids=[dst(d) for d in others], dma_engine_mask=mask_of(e), remote_sem=T.sem[sem], srcs=[ap(src)],
             dsts=[ap(land(s)) for s in slot_at])], src, lsem, len(e), sem, 3 * len(e), landing)
 
-    def zb(t, o, n):
-        return V("ZB", 184 * (t - 1) + o, 184 * (t - 1) + o + n)
+    def each(src, w, land, sem, lsem, turn=0):
+        trs = []
+        for i, d in enumerate(others):
+            e = topo.engines(core, T.cores[d])
+            j = 4 * ((i + turn) % 4)
+            a, z = V(src, w * i, w * i + w), V(land, w * slot_at[i], w * slot_at[i] + w)
+            code = SCRATCH[src][2] == C
+            trs.append(RemoteDMATransfer(
+                dst_ids=[dst(d)], dma_engine_mask=mask_of(e[j:j + 4]), remote_sem=T.sem[sem],
+                srcs=[ap(a).bitcast(dt.uint8) if code else ap(a)], dsts=[ap(z).bitcast(dt.uint8) if code else ap(z)]))
+        return remote(trs, V(src), lsem, 12, sem, 12, V(land))
 
-    def sub(v, a, b, k=None):
-        return (v[0], v[1] if k is None else 32 * k, v[2] if k is None else 32 * k + 32, v[3] + a, v[3] + b, 1)
+    def zb(t, o, n):
+        o = o if t == 0 else 64 + 272 * (t - 1) + o
+        return V("ZB", o, o + n)
+
+    def sub(v, a, b, k=None, st=1):
+        return (v[0], v[1] if k is None else 32 * k, v[2] if k is None else 32 * k + 32, v[3] + a, v[3] + b, st)
 
     def bufs(t):
         return lambda name, *a: V(name + str(t), *a)
@@ -292,63 +310,71 @@ def rank_program(g, core, T, topo):
     for i in range(8):
         load("s", V("RAW2", p0=16 * i, p1=16 * i + 16), T.p2[:], FIRST)
     op("g", lambda: g.iota(ap(V("PI")), [[0, 1]], 0, 1), [], [V("PI")], 100)
-    op("g", lambda: g.iota(ap(V("DUPI")), [[16, 4], [0, 2]], 0, 0), [], [V("DUPI")], 100)
-    fill(V("ZERO"), 0)
-    fill(V("TR"), 257, 1, 8)
-    fill(V("NEG"), -1)
-    fill(V("ZB"), 0)
-    for t in (1, 2):
-        fill(V("W%d" % t, 0, 64), 0)
-    for j, m in enumerate((15, 3, 1, 96)):
+    fill(V("J4"), 0, pattern=[[0, 16], [1, 4]])
+    fill(V("J16"), 0, pattern=[[0, 8], [1, 16]])
+    for j, m in enumerate((15, 3, 1, 96, 31, 16)):
         ts(V("PJ", j, j + 1), V("PI"), m, A.bitwise_and)
-    p15, kcol = V("P15F", 0, 1), V("KCOL", 0, 1)
-    tc(p15, V("PJ", 0, 1))
-    tc(kcol, V("PJ", 1, 2))
-    tc(V("XEO", 4, 5), V("PJ", 2, 3))
-    ts(V("GCOL", 0, 1), V("PJ", 3, 4), 8.0, A.mult)
-    lin(V("SL", 0, 1), V("GCOL", 0, 1), bias=-1.0)
-    lin(V("SL", 1, 2), V("GCOL", 0, 1), bias=float(P))
-    ts(V("SL", 2, 3), V("GCOL", 0, 1), 257 * (3 * P - 1) / P, A.mult, float(257 * 3 * P), A.add)
-    lin(V("SL", 3, 4), V("GCOL", 0, 1), -1.0, 1024.0)
-    lin(V("GD", 0, 1), V("GCOL", 0, 1), bias=float(-P * me))
-    lin(V("XEO", 0, 1), V("XEO", 4, 5), -1.0, 1.0)
-    ts(V("DUP"), V("DUPI"), p15, A.add)
-    for k in range(4):
-        ms(blk(k, "BC", 0, 1), float(255 + 64 * others.index(k)) if k != me else 0.0)
+    ts(V("PJ", 6, 7), V("PI"), 2, A.logical_shift_right, 3, A.bitwise_and)
+    tc(V("PF32", 0, 7), V("PJ", 0, 7))
+    p15, kcol, p31, p4 = V("PF32", 0, 1), V("PF32", 1, 2), V("PF32", 4, 5), V("PF32", 6, 7)
+    ts(V("SL", 0, 1), V("PF32", 3, 4), 8.0, A.mult, -0.5, A.add)
+    ts(V("SL", 1, 2), V("PF32", 3, 4), 8.0, A.mult, P - 0.5, A.add)
+    ts(V("SL", 2, 3), V("PF32", 3, 4), 24.0, A.mult, 3 * (P - 0.5), A.add)
+    ts(V("SEG4"), V("J4"), 1.0, A.min)
+    fill(V("PKC"), 4, pattern=[[0, 2], [-3, 2], [0, 4]])
+    op("g", lambda: g.iota(ap(V("DUPI")), [[16, 4], [0, 2]], 0, 0), [], [V("DUPI")], 100)
+    op("g", lambda: g.iota(ap(V("PERMI")), [[4, 2]], 0, 0), [], [V("PERMI")], 100)
+    fill(V("J32"), 0, 1)
+    fill(V("TR"), 257, 1, 8)
 
-    def prep_lists(t, pk):
+    def fills():
+        fill(V("IDT"), 0, 1)
+        fill(V("NEG", 8, 40), 0)
+        fill(V("NEG", 0, 8), -1)
+        for t in (1, 2):
+            fill(V("RT%d" % t, 32, 40), 1)
+
+    def constants():
+        for c in range(0, 608, 152):
+            ms(V("ZB", c, c + 152), 0.0)
+        ms(V("ZERO"), 0.0)
+        for t in (1, 2):
+            ms(V("W%d" % t, 0, 64), 0.0)
+        ts(V("MASK"), V("J16"), p15, A.is_equal)
+        ts(V("SEG16"), V("J16"), 1.0, A.min)
+        ts(V("SUF"), V("J32"), p31, A.is_ge)
+        ts(V("KCOL", 1, 2), kcol, 8.0, A.mult, p4, A.add)
+        ts(V("DUP"), V("DUPI"), p15, A.add)
+        ts(V("PERM"), V("PERMI"), V("KCOL", 1, 2), A.add)
+        ts(V("PV"), V("PERMI"), p4, A.add)
+        ts(V("XEO", 4, 5), V("PF32", 2, 3), 1.0, A.mult)
+        lin(V("XEO", 0, 1), V("PF32", 2, 3), -1.0, 1.0)
+        ts(V("GD", 0, 1), V("PF32", 3, 4), 8.0, A.mult, float(-P * me), A.add)
+        for k in range(4):
+            ms(blk(k, "BC", 0, 1), float(255 + 64 * others.index(k)) if k != me else 0.0)
+
+    def prep_lists(t, out):
         b = bufs(t)
-        ts(b("CUT"), V("RAW%d" % t), V("SL", 0, 1), A.max, V("SL", 1, 2), A.min)
-        lin(b("HW"), b("CUT", 32, 64), 256.0)
         for h in range(2):
-            tt(b("RL", 16 * h, 16 * h + 16), b("CUT", h, 32, 2), b("HW", h, 32, 2), A.add)
+            ts(b("RL", 32 * h, 32 * h + 32), V("RAW%d" % t, h, 64, 2), V("SL", 0, 1), A.max, V("SL", 1, 2), A.min)
         tr(b("T2"), b("RL"))
-        tt(b("M1"), b("T2", 0, 16, 2), b("T2", 1, 16, 2), A.add)
-        tt(b("LOC"), b("M1", 0, 8, 2), b("M1", 1, 8, 2), A.add)
-        ts(pk, b("LOC"), V("SL", 2, 3), A.subtract)
+        scan(b("SCL"), V("SEG4"), b("T2"), A.mult, A.add)
+        for h in range(2):
+            ts(V(out, 4 * h, 4 * h + 4), b("SCL", 32 * h + 3, 32 * h + 16, 4), V("SL", 2, 3), A.subtract)
 
-    def prep_nodes(t, kcols):
+    def prep_ties(t):
         b = bufs(t)
-        ts(b("TI"), V("RAW%d" % t), V("SL", 3, 4), A.add)
-        ts(b("TJ"), b("TI"), 1023, A.bitwise_and)
         for h in range(2):
-            ts(b("RN", 32 * h, 32 * h + 32), b("TJ", h, 64, 2), 4.0, A.mult, kcol, A.add)
-        tr(b("TN"), b("RN"))
-        tt(b("MN"), b("TN", 0, 64, 2), b("TN", 1, 64, 2), A.min)
-        for h in range(2):
-            tt(b("WN", 4 * h, 4 * h + 4), b("MN", 16 * h, 16 * h + 8, 2), b("MN", 16 * h + 1, 16 * h + 8, 2), A.min)
-        ts(b("KN"), b("WN"), 3, A.bitwise_and)
-        ts(b("KSC", 0, 2), b("KN", 0, 8, 4), 4.0, A.mult)
-        for i in (1, 2, 3):
-            tt(b("KFN", 2 * i, 2 * i + 2), b("KSC", 2 * i - 2, 2 * i), b("KN", i, 8, 4), A.add)
-            if i < 3:
-                lin(b("KSC", 2 * i, 2 * i + 2), b("KFN", 2 * i, 2 * i + 2), scale=4.0)
-        tc(kcols, b("KFN", 6, 8))
+            tt(b("EQN", 32 * h, 32 * h + 32), b("RL", 32 * h, 32 * h + 32), V("RAW%d" % t, h, 64, 2), A.is_equal)
+        lin(b("KQN"), b("EQN"), scale=V("KCOL", 0, 1))
+        tr(b("TK"), b("KQN"))
+        scan(b("SK"), V("SEG4"), b("TK"), A.mult, A.add)
+        scan(b("PK"), V("PKC"), b("SK", 3, 64, 4), A.mult, A.add)
+        tc(V("MSG2", t - 1, t), b("PK", 15, 16))
 
     def own_columns(t):
         b = bufs(t)
-        ts(b("LN"), b("WN"), 2, A.logical_shift_right)
-        tc(b("LCN"), b("LN"))
+        tc(b("LCN"), V("MSG1") if t == 1 else V("LS2"))
         for k in [me] + others:
             act(blk(k, "OL%d" % t), blk(me, "LCN%d" % t))
         lin(blk(me, "CO%d" % t), blk(me, "LCN%d" % t), bias=float(P * me))
@@ -356,62 +382,43 @@ def rank_program(g, core, T, topo):
         tt(b("CD"), b("LCN"), b("OL"), A.subtract)
         lin(b("CG"), b("CD"), bias=V("GD", 0, 1))
 
-    def packed(t, d):
-        if d == me:
-            return blk(me, "MSG1") if t == 1 else blk(me, "MSG3", 0, 4)
-        i = others.index(d)
-        return blk(me, "LM1", 4 * i, 4 * i + 4) if t == 1 else blk(me, "LM3", 6 * i, 6 * i + 4)
-
-    def decode_lists(t):
-        b = bufs(t)
-        for d in [me] + others:
-            tc(blk(d, "CL%d" % t), packed(t, d))
-        ts(b("LI", 0, 8, 2), b("CL"), 255, A.bitwise_and)
-        ts(b("LI", 1, 8, 2), b("CL"), 8, A.logical_shift_right)
-        tc(b("LU"), b("LI"))
-
-    def value_rows(t):
-        b = bufs(t)
-        tc(b("LF"), b("LI"))
-        for i in range(3):
-            act(b("V3", 8 * i, 8 * i + 8), b("U", 0, 8))
-        op("a", lambda: g.scalar.activation(ap(b("AB")), ap(b("V3")), AF.Abs, scale=STEP), [b("V3")], [b("AB")], 24)
-        for c in range(8):
-            plus(b("RB", 16 * c, 16 * c + 16), V("ZERO", 0, 16), b("LF", c, c + 1))
-        tr(b("VR"), b("RB"))
-
-    def decode_ties(t):
-        b = bufs(t)
+    def decode_ties():
         slot = {d: i for i, d in enumerate(others + [me])}
-        if t == 1:
-            tc(b("KC", 0, 6), V("LM2"))
-            tc(b("KC", 6, 8), V("MSG2"))
-        else:
-            for i in range(3):
-                tc(b("KC", 2 * i, 2 * i + 2), V("LM3", 6 * i + 4, 6 * i + 6))
-            tc(b("KC", 6, 8), V("MSG3", 4, 6))
-        for i in range(4):
-            ts(b("KD", i, 32, 4), b("KC"), 2 * (3 - i), A.logical_shift_right, 3, A.bitwise_and)
-        tc(b("KF"), b("KD"))
-        ka = zb(t, 144, 32)
+        tc(V("KC", 0, 6), V("LM2"))
+        tc(V("KC", 6, 8), V("MSG2"))
+        for c in range(8):
+            ts(V("KD", c, 64, 8), V("KC"), 2 * (7 - c), A.logical_shift_right, 3, A.bitwise_and)
+        tc(V("KF"), V("KD"))
+        ka = zb(0, 0, 64)
         for d in range(4):
             for s in range(4):
                 if s != d:
                     i = (s - me) % 4
-                    lin(sub(ka, 8 * i, 8 * i + 8, d), blk(s, "KF%d" % t, 8 * slot[d], 8 * slot[d] + 8))
-        for i in range(3):
-            tt(b("KL", 8 * i, 8 * i + 8), sub(ka, 8 * i + 8, 8 * i + 16), sub(ka, 0, 8), A.is_lt)
-        lin(b("KK"), ka, -1.0, 4.0)
+                    lin(sub(ka, 16 * i, 16 * i + 16, d), blk(s, "KF", 16 * slot[d], 16 * slot[d] + 16))
+        for t in (1, 2):
+            o = 8 * (t - 1)
+            for i in range(4):
+                if i:
+                    tt(sub(zb(t, 80, 32), i, 32, None, 4), sub(ka, 16 * i + o, 16 * i + o + 8), sub(ka, o, o + 8), A.is_lt)
+                lin(V("KK%d" % t, 8 * i, 8 * i + 8), sub(ka, 16 * i + o, 16 * i + o + 8), -1.0, 4.0)
+
+    def value_rows(t):
+        b = bufs(t)
+        gata(b("V4"), b("U", 0, 8), V("PV"))
+        op("a", lambda: g.scalar.activation(ap(b("AB")), ap(b("V4")), AF.Abs, scale=STEP), [b("V4")], [b("AB")], 32)
+        gata(b("VR"), V("IDT"), b("LU"))
+
+    def thresholds(t):
+        b = bufs(t)
         ts(b("AC"), b("AB"), TINY, A.add)
-        tt(b("DE"), b("AC"), b("KL"), A.mult)
-        tt(b("VA"), b("V3"), b("DE"), A.subtract)
+        tt(b("DE"), b("AC"), zb(t, 80, 32), A.mult)
+        tt(b("VA"), b("V4"), b("DE"), A.subtract)
 
     def scores_out(t):
         b = bufs(t)
-        gat(b("G"), V("S%d" % (t - 1)), b("LU"))
-        tr(b("TG"), b("G"))
-        lin(b("U", 0, 4), b("TG", 0, 128, 32))
-        lin(b("U", 4, 8), b("TG", 16, 128, 32))
+        tti(b("G"), V("S%d" % (t - 1)), b("LU"), V("MASK"), A.mult)
+        scan(b("SG"), V("SEG16"), b("G"), A.mult, A.add)
+        lin(b("U", 0, 8), b("SG", 15, 128, 16))
         return spread(b("U", 0, 8), lambda s: b("U", 8 + 8 * s, 16 + 8 * s), "v%d" % t, "lv%d" % t, b("U", 8, 32))
 
     def prefix(x, add, ni, eb, tb, ec):
@@ -422,15 +429,17 @@ def rank_program(g, core, T, topo):
 
     def choose_and_send(t):
         b = bufs(t)
-        tt(b("L3"), b("U", 8, 32), b("VA"), A.is_gt)
-        tt(b("X1"), b("L3", 0, 8), b("L3", 8, 16), A.max)
-        tt(b("LO"), b("X1"), b("L3", 16, 24), A.max)
-        ni = zb(t, 0, 32)
-        prefix(b("LO"), V("NEG"), ni, zb(t, 64, 40), b("TB"), b("EC"))
-        tt(b("LT"), b("LO"), V("TR"), A.mult)
-        for h in range(2):
-            tt(b("AA", h, 8, 2), b("LT", 4 * h, 4 * h + 4), sub(ni, 4 * h, 4 * h + 4), A.subtract)
-        ts(b("OF"), b("AA"), b("EC", 7, 8), A.subtract, -1.0, A.add)
+        better = zb(t, 112, 160)
+        tti(b("L4"), b("U"), V("PERM"), b("VA"), A.is_gt)
+        scan(sub(better, 0, 32), V("SEG4", 0, 32), b("L4"), A.mult, A.max)
+        scan(b("NI"), sub(better, 3, 160, None, 4), V("NEG"))
+        tr(b("RT", 0, 32), b("NI", 8, 40))
+        op("a", lambda: g.scalar.activation(ap(b("TJ", 0, 33)), ap(b("RT", 0, 33)), AF.Copy, accum_out=ap(b("TA1"))),
+           [b("RT", 0, 33)], [b("TJ", 0, 33), b("TA1")], 50)
+        scan(b("SFX"), b("RT", 0, 32), V("SUF"), A.add, A.mult)
+        tt(b("LT"), sub(better, 3, 32, None, 4), V("TR"), A.mult)
+        tt(b("AA"), b("LT"), b("NI", 0, 8), A.subtract)
+        ts(b("OF"), b("AA"), b("TA1"), A.subtract, b("SFX", 31, 32), A.add)
         op("v", lambda: g.vector.tensor_copy(ap(b("W")).indirect(ap(b("OF"))), ap(b("VR"))), [b("VR"), b("OF")], [b("W")], 450)
         gat(b("WD"), b("W", 0, 64), V("DUP"))
         tr(b("TW"), b("WD"))
@@ -443,24 +452,15 @@ def rank_program(g, core, T, topo):
             if d == others[2]:
                 tt(blk(k, pf, lo, hi), blk(d, "TW%d" % t, 0, 128, 32), blk(d, "TW%d" % t, 16, 128, 32), A.add)
             else:
-                lin(blk(k, pf, lo, hi), blk(d, pf, lo, hi))
+                act(blk(k, pf, lo, hi), blk(d, pf, lo, hi))
         for half in range(2):
             own = [cols[d] for d in others if d // 2 == half]
             lo, hi = min(own)[0], max(own)[1]
             lin(V(pf, lo, hi, 1, 64 - 64 * half, 128 - 64 * half), V(pf, lo, hi, 1, 64 * half, 64 * half + 64))
         tc(b("PO"), b("PF", 0, 12))
         pick(b("SQ"), b("SS"), V("QO%d" % (t - 1)), V("QS%d" % (t - 1)), b("PO"))
-        for src, land, sem, turn in (("SQ", "QW", "c", 0), ("SS", "QP", "s", 3)):
-            trs = []
-            for i, d in enumerate(others):
-                e = topo.engines(core, T.cores[d])
-                j = 4 * ((i + turn) % 4)
-                a, z = b(src, 64 * i, 64 * i + 64), V(land + str(t - 1), 256 + 64 * slot_at[i], 320 + 64 * slot_at[i])
-                trs.append(RemoteDMATransfer(
-                    dst_ids=[dst(d)], dma_engine_mask=mask_of(e[j:j + 4]), remote_sem=T.sem[sem + str(t)],
-                    srcs=[ap(a).bitcast(dt.uint8) if src == "SQ" else ap(a)], dsts=[ap(z).bitcast(dt.uint8) if src == "SQ" else ap(z)]))
-            i = remote(trs, b(src), "l" + sem + str(t), 12, sem + str(t), 12, V(land + str(t - 1), 256, 448))
-        return i
+        each("SQ%d" % t, 64, "QW%d" % (t - 1), "c%d" % t, "lc%d" % t)
+        return each("SS%d" % t, 64, "QP%d" % (t - 1), "s%d" % t, "ls%d" % t, 3)
 
     def own_list(t):
         b = bufs(t)
@@ -472,10 +472,10 @@ def rank_program(g, core, T, topo):
         tt(b("KEY"), b("EQ"), b("KK"), A.mult)
         tt(b("K16"), b("KEY", 0, 16), b("KEY", 16, 32), A.max)
         tt(b("KM"), b("K16", 0, 8), b("K16", 8, 16), A.max)
-        wb, i2 = zb(t, 176, 8), zb(t, 32, 32)
+        wb, i2 = zb(t, 72, 8), zb(t, 0, 32)
         for i, s in enumerate(others):
             tt(sub(wb, 0, 8, s), mk("KEY", 8 * i + 8, 8 * i + 16), mk("KM"), A.is_equal)
-        prefix(wb, V("ZERO", 0, 8), i2, zb(t, 104, 40), b("TB2"), b("EC2"))
+        prefix(wb, V("ZERO", 0, 8), i2, zb(t, 32, 40), b("TB2"), b("EC2"))
         lin(b("NW"), wb, -1000.0, 1000.0)
         tt(b("NP"), sub(i2, 0, 8), b("NW"), A.add)
         tt(b("BP"), sub(i2, 0, 8), b("OB"), A.add)
@@ -511,43 +511,44 @@ def rank_program(g, core, T, topo):
         tt(mk("CH"), mk("SA", 8, 16), mk("CA"), A.add)
         dma("s", T.ch[t - 1:t, :], ap(mk("CH")), [mk("CH")], [])
 
+    def products(t, i, arrived):
+        q, s, n, o = ("QW", "QP", 192, 256) if arrived else ("QO", "QS", 256, 0)
+        r = mm(i if arrived else 4 + i, n, V("AQ", 128 * i, 128 * i + 128), V("AP", 128 * i, 128 * i + 128), V(q + str(t - 1)), V(s + str(t - 1)))
+        act(V("Z%d" % t, 448 * i + o, 448 * i + o + n), r, 0.05)
+
     def new_columns(t):
         b = bufs(t)
-        for f in range(2):
-            lo, hi = 128 * f, 128 * f + 128
-            pick(b("XQ", lo, hi), b("XS", lo, hi), V("QW%d" % (t - 1)), V("QP%d" % (t - 1)), b("XO", 8 * f, 8 * f + 8))
+        for i in range(4):
+            products(t, i, True)
         rs = {}
         for f in range(2):
-            for i in range(4):
-                rs[f, i] = mm(4 * f + i, 128, V("AQ", 128 * i, 128 * i + 128), V("AP", 128 * i, 128 * i + 128),
-                              b("XQ", 128 * f, 128 * f + 128), b("XS", 128 * f, 128 * f + 128))
-                act(b("Z", 512 * f + 128 * i, 512 * f + 128 * i + 128), rs[f, i], 0.05)
-        for f in range(2):
             lo, hi = 128 * f, 128 * f + 128
             for i in range(4):
-                if t == 2 and f == 1 and i == 1:
+                if f == 1 and i == 2:
                     hold[0] = (first,)
-                tt(b("HT", 512 * f + i, 512 * f + 512, 4), b("Z", 512 * f + 128 * i, 512 * f + 128 * i + 128),
-                   V("E%d" % t, 512 * f + i, 512 * f + 512, 4), A.add)
+                tti(b("HT", 512 * f + i, 512 * f + 512, 4), b("Z", 448 * i, 448 * i + 448), b("XO", 8 * f, 8 * f + 8),
+                    V("E%d" % t, 512 * f + i, 512 * f + 512, 4), A.add)
             first = qz(V("QO%d" % t, lo, hi), V("QS%d" % t, lo, hi), b("HT", 512 * f, 512 * f + 512))
             hold[0] = ()
-            rs[f] = mm(f, 128, V("UQ"), V("UP"), V("QO%d" % t, lo, hi), V("QS%d" % t, lo, hi))
-            tt(V("S%d" % t, lo, hi), rs[f], b("PB", lo, hi), A.add)
+            rs[f] = mm(4 + f, 128, V("UQ"), V("UP"), V("QO%d" % t, lo, hi), V("QS%d" % t, lo, hi))
             if t == 2:
-                yp = mm(2 + f, 128, V("WQ"), V("WP"), V("QO2", lo, hi), V("QS2", lo, hi))
+                yp = mm(6 + f, 128, V("WQ"), V("WP"), V("QO2", lo, hi), V("QS2", lo, hi))
                 dma("s", T.oc[:, 4 * lo:4 * hi], ap(V("QO2", lo, hi)).bitcast(dt.uint8), [V("QO2", lo, hi)], [])
                 for k in range(4):
                     sc = V("QS2", lo, hi, 1, 32 * k, 32 * k + 4)
                     dma("s", T.osc[4 * k:4 * k + 4, lo:hi], ap(sc), [sc], [])
                 lin(V("YB", lo, hi), yp)
                 dma("a", T.y[:, lo:hi], ap(V("YB", lo, hi)), [V("YB", lo, hi)], [], dur=LOCAL + 0.6)
+        hold[0] = (first,)
+        for f in range(2):
+            tt(V("S%d" % t, 128 * f, 128 * f + 128), rs[f], b("PB", 128 * f, 128 * f + 128), A.add)
+        hold[0] = ()
         if t == 2:
             row = V("S2", 0, 256, 1, 0, 1)
             dma("s", T.g[:], ap(row), [row], [])
 
-    prep_lists(1, V("MSG1"))
-    sent = spread(V("MSG1"), lambda s: V("LM1", 4 * s, 4 * s + 4), "m1", "lm1", V("LM1"))
-    load("s", V("AT", 0, 1024), T.a[:, 0:1024], LONG, [sent])
+    prep_lists(1, "MSG1")
+    sent = spread(V("MSG1"), lambda s: V("LM1", 8 * s, 8 * s + 8), "m1", "lm1", V("LM1"))
     w = 4
     while w < 512:
         act(V("UT", w, 2 * w), V("UT", 0, w))
@@ -555,36 +556,49 @@ def rank_program(g, core, T, topo):
     qz(V("UQ"), V("UP"), V("UT"))
     qz(V("QO0"), V("QS0"), V("E0"))
     act(V("S0"), mm(0, 256, V("UQ"), V("UP"), V("QO0"), V("QS0")))
-    prep_nodes(1, V("MSG2"))
-    spread(V("MSG2"), lambda s: V("LM2", 2 * s, 2 * s + 2), "m2", "lm2", V("LM2"))
-    prep_lists(2, V("MSG3", 0, 4))
-    decode_lists(1)
+    prep_lists(2, "LS2")
+    hold[0] = (sent,)
+    ts(V("KCOL", 0, 1), V("PF32", 5, 6), 0.0, A.is_equal, kcol, A.mult)
+    prep_ties(1)
+    prep_ties(2)
+    ties = spread(V("MSG2"), lambda s: V("LM2", 2 * s, 2 * s + 2), "m2", "lm2", V("LM2"))
+    load("s", V("AT", 0, 1024), T.a[:, 0:1024], LONG, [ties])
+    fills()
+    constants()
+    hold[0] = ()
+    for d in [me] + others:
+        tc(blk(d, "LU1"), blk(me, "MSG1") if d == me else blk(me, "LM1", 8 * others.index(d), 8 * others.index(d) + 8))
+    tc(blk(me, "LU2"), blk(me, "LS2"))
     scores = scores_out(1)
     load("s", V("AT", 1024, 2048), T.a[:, 1024:2048], LONG, [scores])
     load("s", V("E1"), T.e1[:], LONG, [scores])
-    prep_nodes(2, V("MSG3", 4, 6))
-    spread(V("MSG3"), lambda s: V("LM3", 6 * s, 6 * s + 6), "m3", "lm3", V("LM3"))
+    own_columns(1)
+    for i, d in enumerate(others):
+        dma("s", ap(V("ST2", 2 * i, 2 * i + 2)), ap(blk(d, "LS2")), [blk(d, "LS2")], [V("ST2", 2 * i, 2 * i + 2)])
     hold[0] = (scores - 1,)
     value_rows(1)
     hold[0] = ()
-    decode_ties(1)
-    own_columns(1)
-    qz(V("QW0", 0, 256), V("QP0", 0, 256), V("E0"))
+    decode_ties()
+    thresholds(1)
     sent = choose_and_send(1)
+    each("ST2", 2, "LC2", "m3", "lm3")
+    for i, d in enumerate(others):
+        dma("s", ap(blk(d, "LU2")), ap(V("LC2", 2 * i, 2 * i + 2)), [V("LC2", 2 * i, 2 * i + 2)], [blk(d, "LU2")])
     hold[0] = (sent,)
     for i in range(4):
         qz(V("AQ", 128 * i, 128 * i + 128), V("AP", 128 * i, 128 * i + 128), V("AT", 512 * i, 512 * i + 512))
+        products(1, i, False)
     hold[0] = ()
     own_list(1)
     new_columns(1)
-    decode_lists(2)
     scores = scores_out(2)
     load("s", V("WT"), T.w[:], LONG, [scores])
     load("s", V("E2"), T.e2[:], LONG, [scores])
     hold[0] = (scores - 1,)
     value_rows(2)
-    decode_ties(2)
-    qz(V("QW1", 0, 256), V("QP1", 0, 256), V("HT1"))
+    thresholds(2)
+    for i in range(4):
+        products(2, i, False)
     hold[0] = ()
     own_columns(2)
     sent = choose_and_send(2)

@@ -4,6 +4,7 @@ from concourse.mybir import dt, AluOpType as A, ActivationFunctionType as AF
 P, CAPP = 256, 64
 TINY = 2.0 ** -100
 STEP = 2.0 ** -24 * (1 + 2.0 ** -10)
+BIG = 1.5 * 2.0 ** 25
 WAIT, LEAST, ISSUE, WAY, ONCE = 0.13, 0.09, 0.8, 2.9, 1.5
 LOCAL, FIRST, LONG = 2.3, 3.8, 5.5
 F, B, I, H, C, S8 = "float32", "bfloat16", "int32", "uint16", "float8_e4m3fn_x4", "uint8"
@@ -37,11 +38,11 @@ _buf(F, U1=32, U2=32, Z1=1792, Z2=1792, YB=256, S0=256, S1=256, S2=256, PR1=256,
 _buf(I, RAW1=64, RAW2=64)
 _area(H, DUP=8, PERM=2, PV=2)
 _area(I, PI=1, PJ=8, DUPI=8, PERMI=2, KC=8, KD=64)
-_area(F, ZERO=64, NEG=40, KCOL=4, SL=4, XEO=8, GD=4, BC=4, TR=8, ZB=608, PF32=8, J4=64, SEG4=64, J16=128, MASK=128,
+_area(F, ZERO=64, BAR=64, SEGT=40, KCOL=4, SL=4, XEO=8, GD=4, BC=4, TR=8, ZB=416, PF32=8, J4=64, SEG4=64, J16=128, MASK=128,
       SEG16=128, SUF=32, J32=32, IDT=256, PKC=16, KF=64)
 _area(F, **_each(RL=64, T2=64, SCL=64, EQN=64, KQN=64, TK=64, SK=64, PK=16, LCN=8, OL=8, OB=8, CD=8, CG=8,
-                 VR=128, KK=32, G=128, SG=128, V4=32, AB=32, AC=32, DE=32, VA=32, L4=32, NI=40, RT=40, TJ=40, TA1=1, SFX=32, LT=8,
-                 AA=8, W=1552, WD=128, TW=128, PF=16, M16=16, MM=8, EQ=32, KEY=32, K16=16, KM=8, TB2=32, EC2=32, SV=8,
+                 VR=128, KK=32, G=128, SG=128, V4=32, AB=32, AC=32, DE=32, VA=32, BT=40, NI=64, RT=40, TJ=40, TA1=1, SFX=32,
+                 AA=8, W=6208, WD=128, TW=128, PF=16, M16=16, MM=8, EQ=32, KEY=32, K16=16, KM=8, TB2=32, EC2=32, SV=8,
                  NW=8, NP=8, BP=8, VAL=24, BK=72, SA=24, SB=8, KS=8, CA=8, CO=8, CH=8, XC=8, A2=32, TA=32, XT=16, KQ=32, PP=32,
                  P16=16, PA=8))
 _area(H, **_each(OF=8, PO=12, XO=16))
@@ -293,7 +294,7 @@ def rank_program(g, core, T, topo):
         return remote(trs, V(src), lsem, 12, sem, 12, V(land))
 
     def zb(t, o, n):
-        o = o if t == 0 else 64 + 272 * (t - 1) + o
+        o = o if t == 0 else 64 + 176 * (t - 1) + o
         return V("ZB", o, o + n)
 
     def sub(v, a, b, k=None, st=1):
@@ -322,29 +323,33 @@ def rank_program(g, core, T, topo):
     ts(V("SL", 2, 3), V("PF32", 3, 4), 24.0, A.mult, 3 * (P - 0.5), A.add)
     ts(V("SEG4"), V("J4"), 1.0, A.min)
     fill(V("PKC"), 4, pattern=[[0, 2], [-3, 2], [0, 4]])
-    op("g", lambda: g.iota(ap(V("DUPI")), [[16, 4], [0, 2]], 0, 0), [], [V("DUPI")], 100)
+    op("g", lambda: g.iota(ap(V("DUPI")), [[64, 4], [0, 2]], 0, 0), [], [V("DUPI")], 100)
     op("g", lambda: g.iota(ap(V("PERMI")), [[4, 2]], 0, 0), [], [V("PERMI")], 100)
     fill(V("J32"), 0, 1)
-    fill(V("TR"), 257, 1, 8)
+    fill(V("TR"), 1028, 4, 32)
 
     def fills():
         fill(V("IDT"), 0, 1)
-        fill(V("NEG", 8, 40), 0)
-        fill(V("NEG", 0, 8), -1)
         for t in (1, 2):
-            fill(V("RT%d" % t, 32, 40), 1)
+            fill(V("RT%d" % t, 32, 40), 4)
 
     def constants():
-        for c in range(0, 608, 152):
-            ms(V("ZB", c, c + 152), 0.0)
+        for c in range(0, 416, 104):
+            ms(V("ZB", c, c + 104), 0.0)
         ms(V("ZERO"), 0.0)
-        for t in (1, 2):
-            ms(V("W%d" % t, 0, 64), 0.0)
+        ms(V("W1", 0, 256), 0.0)
+        ms(V("BAR"), 0.0)
+        ms(V("BAR", 4, 33, 4), -BIG - 4.0)
+        ms(V("BAR", 1, 32, 4), 1.5)
+        ms(V("BAR", 3, 32, 4), BIG)
+        ts(V("SEGT"), V("J4", 0, 40), 1.5, A.is_gt)
+        lin(V("SEGT", 4, 33, 4), V("TR"))
         ts(V("MASK"), V("J16"), p15, A.is_equal)
         ts(V("SEG16"), V("J16"), 1.0, A.min)
         ts(V("SUF"), V("J32"), p31, A.is_ge)
         ts(V("KCOL", 1, 2), kcol, 8.0, A.mult, p4, A.add)
-        ts(V("DUP"), V("DUPI"), p15, A.add)
+        ts(V("KCOL", 2, 3), p15, 4.0, A.mult)
+        ts(V("DUP"), V("DUPI"), V("KCOL", 2, 3), A.add)
         ts(V("PERM"), V("PERMI"), V("KCOL", 1, 2), A.add)
         ts(V("PV"), V("PERMI"), p4, A.add)
         ts(V("XEO", 4, 5), V("PF32", 2, 3), 1.0, A.mult)
@@ -357,8 +362,10 @@ def rank_program(g, core, T, topo):
         b = bufs(t)
         for h in range(2):
             ts(b("RL", 32 * h, 32 * h + 32), V("RAW%d" % t, h, 64, 2), V("SL", 0, 1), A.max, V("SL", 1, 2), A.min)
-        tr(b("T2"), b("RL"))
-        scan(b("SCL"), V("SEG4"), b("T2"), A.mult, A.add)
+        for h in range(2):
+            tr(b("T2", 32 * h, 32 * h + 32), b("RL", 32 * h, 32 * h + 32))
+        for h in range(2):
+            scan(b("SCL", 32 * h, 32 * h + 32), V("SEG4", 0, 32), b("T2", 32 * h, 32 * h + 32), A.mult, A.add)
         for h in range(2):
             ts(V(out, 4 * h, 4 * h + 4), b("SCL", 32 * h + 3, 32 * h + 16, 4), V("SL", 2, 3), A.subtract)
 
@@ -395,12 +402,13 @@ def rank_program(g, core, T, topo):
                 if s != d:
                     i = (s - me) % 4
                     lin(sub(ka, 16 * i, 16 * i + 16, d), blk(s, "KF", 16 * slot[d], 16 * slot[d] + 16))
-        for t in (1, 2):
-            o = 8 * (t - 1)
-            for i in range(4):
-                if i:
-                    tt(sub(zb(t, 80, 32), i, 32, None, 4), sub(ka, 16 * i + o, 16 * i + o + 8), sub(ka, o, o + 8), A.is_lt)
-                lin(V("KK%d" % t, 8 * i, 8 * i + 8), sub(ka, 16 * i + o, 16 * i + o + 8), -1.0, 4.0)
+
+    def tie_flags(t):
+        ka, o = zb(0, 0, 64), 8 * (t - 1)
+        for i in range(4):
+            if i:
+                tt(sub(zb(t, 80, 32), i, 32, None, 4), sub(ka, 16 * i + o, 16 * i + o + 8), sub(ka, o, o + 8), A.is_lt)
+            lin(V("KK%d" % t, 8 * i, 8 * i + 8), sub(ka, 16 * i + o, 16 * i + o + 8), -1.0, 4.0)
 
     def value_rows(t):
         b = bufs(t)
@@ -429,35 +437,36 @@ def rank_program(g, core, T, topo):
 
     def choose_and_send(t):
         b = bufs(t)
-        better = zb(t, 112, 160)
-        tti(b("L4"), b("U"), V("PERM"), b("VA"), A.is_gt)
-        scan(sub(better, 0, 32), V("SEG4", 0, 32), b("L4"), A.mult, A.max)
-        scan(b("NI"), sub(better, 3, 160, None, 4), V("NEG"))
-        tr(b("RT", 0, 32), b("NI", 8, 40))
+        worse = zb(t, 112, 64)
+        tti(sub(worse, 0, 32), b("U"), V("PERM"), b("VA"), A.is_gt)
+        scan(b("NI"), worse, V("BAR"))
+        scan(b("BT", 0, 33), V("SEGT", 0, 33), sub(worse, 0, 33), A.mult, A.max)
+        tr(b("RT", 0, 32), b("NI", 32, 64))
         op("a", lambda: g.scalar.activation(ap(b("TJ", 0, 33)), ap(b("RT", 0, 33)), AF.Copy, accum_out=ap(b("TA1"))),
            [b("RT", 0, 33)], [b("TJ", 0, 33), b("TA1")], 50)
+        tt(b("AA"), b("BT", 4, 33, 4), b("NI", 4, 33, 4), A.subtract)
         scan(b("SFX"), b("RT", 0, 32), V("SUF"), A.add, A.mult)
-        tt(b("LT"), sub(better, 3, 32, None, 4), V("TR"), A.mult)
-        tt(b("AA"), b("LT"), b("NI", 0, 8), A.subtract)
         ts(b("OF"), b("AA"), b("TA1"), A.subtract, b("SFX", 31, 32), A.add)
         op("v", lambda: g.vector.tensor_copy(ap(b("W")).indirect(ap(b("OF"))), ap(b("VR"))), [b("VR"), b("OF")], [b("W")], 450)
-        gat(b("WD"), b("W", 0, 64), V("DUP"))
+        gat(b("WD", 0, 64), b("W", 0, 256), V("DUP", 0, 4))
+        gata(b("WD", 64, 128), b("W", 0, 256), V("DUP", 4, 8))
         tr(b("TW"), b("WD"))
         cols = {d: (4 * i, 4 * i + 4) for i, d in enumerate(others)}
         pf = "PF%d" % t
-        for d in others:
+        alone = me // 2 * 2 + 1 - me % 2
+        for d in [d for d in others if d != alone] + [alone]:
             lo, hi = cols[d]
             tt(blk(d, pf, lo, hi), blk(d, "TW%d" % t, 0, 128, 32), blk(d, "TW%d" % t, 16, 128, 32), A.add)
             k = d // 2 * 2 + 1 - d % 2
-            if d == others[2]:
+            if d == alone:
                 tt(blk(k, pf, lo, hi), blk(d, "TW%d" % t, 0, 128, 32), blk(d, "TW%d" % t, 16, 128, 32), A.add)
             else:
                 act(blk(k, pf, lo, hi), blk(d, pf, lo, hi))
-        for half in range(2):
+        for half in (me // 2, 1 - me // 2):
             own = [cols[d] for d in others if d // 2 == half]
             lo, hi = min(own)[0], max(own)[1]
-            lin(V(pf, lo, hi, 1, 64 - 64 * half, 128 - 64 * half), V(pf, lo, hi, 1, 64 * half, 64 * half + 64))
-        tc(b("PO"), b("PF", 0, 12))
+            for h in (half, 1 - half):
+                tc(V("PO%d" % t, lo, hi, 1, 64 * h, 64 * h + 64), V(pf, lo, hi, 1, 64 * half, 64 * half + 64))
         pick(b("SQ"), b("SS"), V("QO%d" % (t - 1)), V("QS%d" % (t - 1)), b("PO"))
         each("SQ%d" % t, 64, "QW%d" % (t - 1), "c%d" % t, "lc%d" % t)
         return each("SS%d" % t, 64, "QP%d" % (t - 1), "s%d" % t, "ls%d" % t, 3)
@@ -492,9 +501,8 @@ def rank_program(g, core, T, topo):
         tt(mk("KS"), mk("SA", 16, 24), mk("BK", 64, 72), A.add)
         tt(mk("XC"), mk("SA", 0, 8), mk("SB"), A.add)
         lin(mk("KQ", 0, 8), mk("KS"), -1.0, 1.0)
-        for j in range(2):
-            lin(mk("A2", 8 * j, 8 * j + 8), mk("XC"), scale=blk(me, "XEO", 4 * j, 4 * j + 1))
-        lin(mk("A2", 16, 32), mk("A2", 0, 16))
+        for j in range(4):
+            lin(mk("A2", 8 * j, 8 * j + 8), mk("XC"), scale=blk(me, "XEO", 4 * (j % 2), 4 * (j % 2) + 1))
         tr(mk("TA"), mk("A2"))
         tt(mk("XT"), mk("TA", 0, 32, 2), mk("TA", 1, 32, 2), A.add)
         half = me // 2
@@ -507,6 +515,9 @@ def rank_program(g, core, T, topo):
         pr = V("PR%d" % t, 0, 256, 1, 0, 1)
         dma("s", ap(pr), ap(mk("PA")), [mk("PA")], [pr])
         op("g", lambda: g.partition_broadcast(ap(b("PB")), ap(pr), 128), [pr], [b("PB")], 1024)
+
+    def own_choice(t):
+        mk = lambda name, *a: blk(me, name + str(t), *a)
         tt(mk("CA"), mk("BK", 56, 64), mk("CO"), A.add)
         tt(mk("CH"), mk("SA", 8, 16), mk("CA"), A.add)
         dma("s", T.ch[t - 1:t, :], ap(mk("CH")), [mk("CH")], [])
@@ -520,16 +531,19 @@ def rank_program(g, core, T, topo):
         b = bufs(t)
         for i in range(4):
             products(t, i, True)
-        rs = {}
+        rs, first, wide = {}, None, 3
+
+        def choose(i, lo, hi):
+            tti(b("HT", 4 * lo + i, 4 * hi, 4), b("Z", 448 * i, 448 * i + 448), b("XO", lo // 16, hi // 16),
+                V("E%d" % t, 4 * lo + i, 4 * hi, 4), A.add)
+        for i in range(wide):
+            choose(i, 0, P)
+        for i in range(wide, 4):
+            choose(i, 0, 128)
+            choose(i, 128, P)
         for f in range(2):
             lo, hi = 128 * f, 128 * f + 128
-            for i in range(4):
-                if f == 1 and i == 2:
-                    hold[0] = (first,)
-                tti(b("HT", 512 * f + i, 512 * f + 512, 4), b("Z", 448 * i, 448 * i + 448), b("XO", 8 * f, 8 * f + 8),
-                    V("E%d" % t, 512 * f + i, 512 * f + 512, 4), A.add)
             first = qz(V("QO%d" % t, lo, hi), V("QS%d" % t, lo, hi), b("HT", 512 * f, 512 * f + 512))
-            hold[0] = ()
             rs[f] = mm(4 + f, 128, V("UQ"), V("UP"), V("QO%d" % t, lo, hi), V("QS%d" % t, lo, hi))
             if t == 2:
                 yp = mm(6 + f, 128, V("WQ"), V("WP"), V("QO2", lo, hi), V("QS2", lo, hi))
@@ -579,6 +593,7 @@ def rank_program(g, core, T, topo):
     value_rows(1)
     hold[0] = ()
     decode_ties()
+    tie_flags(1)
     thresholds(1)
     sent = choose_and_send(1)
     each("ST2", 2, "LC2", "m3", "lm3")
@@ -595,17 +610,21 @@ def rank_program(g, core, T, topo):
     load("s", V("WT"), T.w[:], LONG, [scores])
     load("s", V("E2"), T.e2[:], LONG, [scores])
     hold[0] = (scores - 1,)
+    tie_flags(2)
     value_rows(2)
     thresholds(2)
     for i in range(4):
         products(2, i, False)
-    hold[0] = ()
+    ms(V("W2", 0, 256), 0.0)
     own_columns(2)
+    own_choice(1)
+    hold[0] = ()
     sent = choose_and_send(2)
     hold[0] = (sent,)
     qz(V("WQ"), V("WP"), V("WT"))
     hold[0] = ()
     own_list(2)
+    own_choice(2)
     new_columns(2)
     lay()
     for sem in sorted(total):

from concourse.bass import DstId, RemoteDMATransfer
from concourse.mybir import dt, AluOpType as A, ActivationFunctionType as AF

P, CAPP = 256, 64
TINY = 2.0 ** -100
STEP = 2.0 ** -24 * (1 + 2.0 ** -10)
BIG = 1.5 * 2.0 ** 25
WAIT, LEAST, ISSUE, WAY, ONCE = 0.13, 0.09, 0.8, 2.9, 1.5
LOCAL, FIRST, LONG = 2.3, 3.8, 5.5
F, B, I, H, C, S8 = "float32", "bfloat16", "int32", "uint16", "float8_e4m3fn_x4", "uint8"
SCRATCH = {"PS": ("psum", [128, 4096], F)}
PLACE = {"PS": ("PS", 0, 4096)}


def _buf(dtype, **names):
    for k, n in names.items():
        SCRATCH[k] = ("sbuf", [128, n], dtype)
        PLACE[k] = (k, 0, n)


def _area(dtype, **names):
    k = "W" + dtype
    for name, n in names.items():
        at = SCRATCH[k][1][1] if k in SCRATCH else 0
        PLACE[name] = (k, at, n)
        SCRATCH[k] = ("sbuf", [128, at + (n + 15) // 16 * 16], dtype)


def _each(**names):
    return {n + str(t): w for t in (1, 2) for n, w in names.items()}


_buf(B, UT=512, E0=1024, AT=2048, WT=512, E1=1024, E2=1024, HT1=1024, HT2=1024)
_buf(C, UQ=128, AQ=512, WQ=128, QO0=256, QO1=256, QO2=256, QW0=192, QW1=192, SQ1=192, SQ2=192)
_buf(S8, UP=128, AP=512, WP=128, QS0=256, QS1=256, QS2=256, QP0=192, QP1=192, SS1=192, SS2=192)
_buf(H, MSG1=8, MSG2=2, LM1=24, LM2=6, LS2=8, ST2=6, LC2=6, LU1=8, LU2=8)
_buf(F, U1=32, U2=32, Z1=1792, Z2=1792, YB=256, S0=256, S1=256, S2=256, PR1=256, PR2=256, PB1=256, PB2=256)
_buf(I, RAW1=64, RAW2=64)
_area(H, DUP=8, PERM=2, PV=2)
_area(I, PI=1, PJ=8, DUPI=8, PERMI=2, KC=8, KD=64)
_area(F, ZERO=64, BAR=64, SEGT=40, KCOL=4, SL=4, XEO=8, GD=4, BC=4, TR=8, ZB=416, PF32=8, J4=64, SEG4=64, J16=128, MASK=128,
      SEG16=128, SUF=32, J32=32, IDT=256, PKC=16, KF=64)
_area(F, **_each(RL=64, T2=64, SCL=64, EQN=64, KQN=64, TK=64, SK=64, PK=16, LCN=8, OL=8, OB=8, CD=8, CG=8,
                 VR=128, KK=32, G=128, SG=128, V4=32, AB=32, AC=32, DE=32, VA=32, BT=40, NI=64, RT=40, TJ=40, TA1=1, SFX=32,
                 AA=8, W=6208, WD=128, TW=128, PF=16, M16=16, MM=8, EQ=32, KEY=32, K16=16, KM=8, TB2=32, EC2=32, SV=8,
                 NW=8, NP=8, BP=8, VAL=24, BK=72, SA=24, SB=8, KS=8, CA=8, CO=8, CH=8, XC=8, A2=32, TA=32, XT=16, KQ=32, PP=32,
                 P16=16, PA=8))
_area(H, **_each(OF=8, PO=12, XO=16))
NDMA = 60
SEMAPHORES = ["qv", "qa", "qt", "qg", "m1", "lm1", "m2", "lm2", "m3", "lm3"] + ["d%d" % i for i in range(NDMA)] + [
    x + str(t) for t in (1, 2) for x in ("v", "lv", "c", "lc", "s", "ls")]


def rank_program(g, core, T, topo):
    me = T.rank_of(core)
    if me is None:
        return
    others = [(me + 1 + i) % 4 for i in range(3)]
    slot_at = [(me - d) % 4 - 1 for d in others]
    qs = {"v": g.vector, "a": g.scalar, "t": g.tensor, "g": g, "s": g.sync}
    hist, know, cnt, total = {}, {q: {} for q in qs}, {}, {}
    nodes, past, last, hold = [], {}, {}, [()]

    def V(name, c0=0, c1=None, st=1, p0=0, p1=128):
        return (name, p0, p1, c0, PLACE[name][2] if c1 is None else c1, st)

    def blk(k, name, c0=0, c1=None, st=1):
        return V(name, c0, c1, st, 32 * k, 32 * k + 32)

    def ap(v):
        name, o, _ = PLACE[v[0]]
        return T[name][v[1]:v[2], o + v[3]:o + v[4]] if v[5] == 1 else T[name][v[1]:v[2], o + v[3]:o + v[4]:v[5]]

    def width(v):
        return (v[4] - v[3] + v[5] - 1) // v[5]

    def clash(a, b):
        if a[2] <= b[1] or b[2] <= a[1] or a[4] <= b[3] or b[4] <= a[3]:
            return False
        return not (a[5] == b[5] and a[5] > 1 and (a[3] - b[3]) % a[5])

    def bank(v):
        return (v[0], 0, 128, v[3] // 512 * 512, v[3] // 512 * 512 + 512, 1) if v[0] == "PS" else v

    def regions(reads, writes):
        return [(bank(v), False) for v in reads] + [(bank(v), True) for v in writes]

    def push(opts, reads, writes, cost, dur=None, after=()):
        i, deps = len(nodes), set(after)
        for r, w in regions(reads, writes):
            deps |= {j for (o, ow, j) in past.get(r[0], []) if (w or ow) and clash(r, o)}
        for r, w in regions(reads, writes):
            past.setdefault(r[0], []).append((r, w, i))
        prev = list(hold[0]) + ([last["g"]] if "g" in opts and "g" in last else [])
        if "g" in opts:
            last["g"] = i
        nodes.append({"opts": opts, "rd": reads, "wr": writes, "cost": cost, "dur": cost if dur is None else dur,
                      "deps": deps - {i}, "prev": prev, "gate": [j for j in after]})
        return i

    def wait(q, evs):
        need = {}
        for sem, val, clock in evs:
            if know[q].get(sem, 0) < val and need.get(sem, (0, 0))[0] < val:
                need[sem] = (val, clock)
        for sem in sorted(need):
            val, clock = need[sem]
            if know[q].get(sem, 0) >= val or any(o != sem and need[o][1].get(sem, 0) >= val for o in need):
                continue
            qs[q].wait_ge(T.sem[sem], val)
        for sem in need:
            for k, n in list(need[sem][1].items()) + [(sem, need[sem][0])]:
                know[q][k] = max(know[q].get(k, 0), n)

    def issue(node, q):
        if q == "x":
            return
        evs = [nodes[j]["ev"] for j in node["gate"]]
        for r, w in regions(node["rd"], node["wr"]):
            evs += [ev for (o, ow, ev) in hist.get(r[0], []) if (w or ow) and clash(r, o)]
        wait(q, evs)
        kind, call = node["opts"][q]
        if kind == "op":
            sem, val = "q" + q, cnt.get(q, 0) + 1
            cnt[q] = val
            call().then_inc(T.sem[sem], 1)
        elif kind == "dma":
            sem, val = "d%d" % cnt.get("dma", 0), 16
            cnt["dma"] = cnt.get("dma", 0) + 1
            call().then_inc(T.sem[sem], 16)
        else:
            sem, val = call()
        clock = dict(know[q])
        clock[sem] = val
        total[sem] = max(total.get(sem, 0), val)
        node["ev"] = (sem, val, clock)
        for r, w in regions(node["rd"], node["wr"]):
            hist.setdefault(r[0], []).append((r, w, node["ev"]))

    def lay():
        n = len(nodes)
        succ = [[] for _ in range(n)]
        for i, nd in enumerate(nodes):
            for j in nd["deps"]:
                succ[j].append(i)
        high = [0.0] * n
        for i in range(n - 1, -1, -1):
            high[i] = nodes[i]["dur"] + max([WAIT + high[j] for j in succ[i]] + [high[i]])
            for p in nodes[i]["prev"]:
                high[p] = max(high[p], nodes[p]["cost"] + high[i] - nodes[p]["dur"])
        left = [len(nd["deps"]) for nd in nodes]
        ready = {i for i in range(n) if left[i] == 0}
        free, fin, done = {}, [0.0] * n, set()
        while ready:
            cand = []
            for i in ready:
                nd = nodes[i]
                if any(p not in done for p in nd["prev"]):
                    continue
                s = max([fin[j] + WAIT for j in nd["deps"]] + [0.0])
                start, q = min((max(s, free.get(q, 0.0)) if q != "x" else s, "vatgsx".index(q)) for q in nd["opts"])
                cand.append((start, -high[i], i, "vatgsx"[q]))
            first = min(cand)[0]
            start, _, i, q = min((c for c in cand if c[0] <= first + 0.05), key=lambda c: c[1:])
            issue(nodes[i], q)
            free[q] = start + nodes[i]["cost"]
            fin[i] = start + nodes[i]["dur"]
            ready.discard(i)
            done.add(i)
            for j in succ[i]:
                left[j] -= 1
                if left[j] == 0:
                    ready.add(j)

    def us(cycles):
        return max(LEAST, 0.02 + 0.001 * cycles)

    def op(q, call, reads, writes, cycles):
        return push({q: ("op", call)}, reads, writes, us(cycles))

    def sv(s):
        return ap(s) if isinstance(s, tuple) else s

    def cols_of(*ss):
        return [s for s in ss if isinstance(s, tuple)]

    def tc(o, a):
        op("v", lambda: g.vector.tensor_copy(ap(o), ap(a)), [a], [o], width(a))

    def tt(o, a, b, f):
        op("v", lambda: g.vector.tensor_tensor(ap(o), ap(a), ap(b), f), [a, b], [o], width(a) * (1 if a[0] == "PS" else 2))

    def tti(o, w, off, b, f):
        op("v", lambda: g.vector.tensor_tensor(ap(o), ap(w).indirect(ap(off)), ap(b), f), [w, off, b], [o], 50 + 1.5 * width(b))

    def ts(o, a, s1, f1, s2=None, f2=None):
        if f2 is None:
            op("v", lambda: g.vector.tensor_scalar(ap(o), ap(a), sv(s1), None, f1), [a] + cols_of(s1), [o], width(a))
        else:
            op("v", lambda: g.vector.tensor_scalar(ap(o), ap(a), sv(s1), sv(s2), f1, f2), [a] + cols_of(s1, s2), [o], width(a))

    def lin(o, a, scale=1.0, bias=0.0):
        def on_v():
            if scale == 1.0 and bias == 0.0:
                return g.vector.tensor_copy(ap(o), ap(a))
            if bias == 0.0:
                return g.vector.tensor_scalar(ap(o), ap(a), sv(scale), None, A.mult)
            if scale == 1.0:
                return g.vector.tensor_scalar(ap(o), ap(a), sv(bias), None, A.add)
            return g.vector.tensor_scalar(ap(o), ap(a), sv(scale), sv(bias), A.mult, A.add)

        def on_a():
            if bias == 0.0:
                return g.scalar.activation(ap(o), ap(a), AF.Copy, scale=sv(scale))
            return g.scalar.activation(ap(o), ap(a), AF.Identity, scale=sv(scale), bias=sv(bias))
        push({"v": ("op", on_v), "a": ("op", on_a)}, [a] + cols_of(scale, bias), [o], us(width(a)))

    def scan(o, a, b, f0=A.add, f1=A.add):
        op("v", lambda: g.vector.tensor_tensor_scan(ap(o), ap(a), ap(b), 0.0, f0, f1), [a, b], [o], width(a))

    def tr(o, a):
        op("v", lambda: g.vector.transpose(ap(o), ap(a)), [a], [o], width(a))

    def ms(o, c):
        op("v", lambda: g.vector.memset(ap(o), c), [], [o], width(o))

    def fill(o, base, step=0, rise=0, pattern=None):
        n = width(o)
        op("g", lambda: g.iota(ap(o), pattern or [[step, n]], base, rise, allow_small_or_imprecise_dtypes=True), [], [o], 130 + 2 * n)

    def gat(o, w, off):
        op("v", lambda: g.vector.tensor_copy(ap(o), ap(w).indirect(ap(off))), [w, off], [o], 50 + 1.5 * width(o))

    def gata(o, w, off):
        op("a", lambda: g.scalar.activation(ap(o), ap(w).indirect(ap(off)), AF.Copy), [w, off], [o], 70 + 1.5 * width(o))

    def pick(qo, so, qw, sw, off):
        op("v", lambda: g.vector.tensor_copy(ap(qo).bitcast(dt.uint32), ap(qw).bitcast(dt.uint32).indirect(ap(off))), [qw, off], [qo],
           50 + 1.5 * width(qo))
        gata(so, sw, off)

    def qz(q, s, a):
        return op("v", lambda: g.vector.quantize_mx(ap(q), ap(s), ap(a)), [a], [q, s], 0.25 * width(a))

    def act(o, a, scale=1.0):
        op("a", lambda: g.scalar.activation(ap(o), ap(a), AF.Copy, scale=scale), [a], [o], width(a))

    def mm(b, n, wq, ws, xq, xs):
        o = V("PS", 512 * b, 512 * b + n)
        op("t", lambda: g.tensor.matmul_mx(ap(o), ap(wq), ap(ws), ap(xq), ap(xs), True, True), [wq, ws, xq, xs], [o], n + 16)
        return o

    def dma(q, out, in_, reads, writes, after=(), dur=LOCAL):
        return push({q: ("dma", lambda: qs[q].dma_start(out, in_))}, reads, writes, 0.08, dur, after)

    def load(q, v, src, dur, after=()):
        return dma(q, ap(v), src, [], [v], after, dur)

    def mask_of(engines):
        return sum(1 << e for e in engines)

    def dst(d):
        rid, pid, _ = topo.addr(T.cores[d])
        return DstId(rid=rid, pnc=pid)

    def remote(transfers, src, lsem, count, sem, arrivals, landing):
        def call():
            g.remote_dma_fused(transfers, local_sem=T.sem[lsem])
            return lsem, count
        more = 0.0 if cnt.get("remote") else ONCE
        cnt["remote"] = 1
        i = push({"g": ("remote", call)}, [src], [], ISSUE + more, ISSUE + 0.5 + more)
        push({"x": None}, [], [landing], 0.0, WAY - ISSUE - 0.5, [i])
        total[sem] = arrivals
        hist.setdefault(landing[0], []).append((landing, True, (sem, arrivals, {sem: arrivals})))
        return i

    def spread(src, land, sem, lsem, landing):
        e = topo.engines(core, T.cores[others[0]])[:16]
        return remote([RemoteDMATransfer(
            dst_ids=[dst(d) for d in others], dma_engine_mask=mask_of(e), remote_sem=T.sem[sem], srcs=[ap(src)],
            dsts=[ap(land(s)) for s in slot_at])], src, lsem, len(e), sem, 3 * len(e), landing)

    def each(src, w, land, sem, lsem, turn=0):
        trs = []
        for i, d in enumerate(others):
            e = topo.engines(core, T.cores[d])
            j = 4 * ((i + turn) % 4)
            a, z = V(src, w * i, w * i + w), V(land, w * slot_at[i], w * slot_at[i] + w)
            code = SCRATCH[src][2] == C
            trs.append(RemoteDMATransfer(
                dst_ids=[dst(d)], dma_engine_mask=mask_of(e[j:j + 4]), remote_sem=T.sem[sem],
                srcs=[ap(a).bitcast(dt.uint8) if code else ap(a)], dsts=[ap(z).bitcast(dt.uint8) if code else ap(z)]))
        return remote(trs, V(src), lsem, 12, sem, 12, V(land))

    def zb(t, o, n):
        o = o if t == 0 else 64 + 176 * (t - 1) + o
        return V("ZB", o, o + n)

    def sub(v, a, b, k=None, st=1):
        return (v[0], v[1] if k is None else 32 * k, v[2] if k is None else 32 * k + 32, v[3] + a, v[3] + b, st)

    def bufs(t):
        return lambda name, *a: V(name + str(t), *a)

    for i in range(8):
        load("sa"[i % 2], V("RAW1", p0=16 * i, p1=16 * i + 16), T.p1[:], LOCAL)
    load("s", V("E0", 0, 512), T.e0[:, 0:512], FIRST)
    load("a", V("UT", 0, 4), T.u[:, 0:4], FIRST)
    load("a", V("E0", 512, 1024), T.e0[:, 512:1024], FIRST)
    for i in range(8):
        load("s", V("RAW2", p0=16 * i, p1=16 * i + 16), T.p2[:], FIRST)
    op("g", lambda: g.iota(ap(V("PI")), [[0, 1]], 0, 1), [], [V("PI")], 100)
    fill(V("J4"), 0, pattern=[[0, 16], [1, 4]])
    fill(V("J16"), 0, pattern=[[0, 8], [1, 16]])
    for j, m in enumerate((15, 3, 1, 96, 31, 16)):
        ts(V("PJ", j, j + 1), V("PI"), m, A.bitwise_and)
    ts(V("PJ", 6, 7), V("PI"), 2, A.logical_shift_right, 3, A.bitwise_and)
    tc(V("PF32", 0, 7), V("PJ", 0, 7))
    p15, kcol, p31, p4 = V("PF32", 0, 1), V("PF32", 1, 2), V("PF32", 4, 5), V("PF32", 6, 7)
    ts(V("SL", 0, 1), V("PF32", 3, 4), 8.0, A.mult, -0.5, A.add)
    ts(V("SL", 1, 2), V("PF32", 3, 4), 8.0, A.mult, P - 0.5, A.add)
    ts(V("SL", 2, 3), V("PF32", 3, 4), 24.0, A.mult, 3 * (P - 0.5), A.add)
    ts(V("SEG4"), V("J4"), 1.0, A.min)
    fill(V("PKC"), 4, pattern=[[0, 2], [-3, 2], [0, 4]])
    op("g", lambda: g.iota(ap(V("DUPI")), [[64, 4], [0, 2]], 0, 0), [], [V("DUPI")], 100)
    op("g", lambda: g.iota(ap(V("PERMI")), [[4, 2]], 0, 0), [], [V("PERMI")], 100)
    fill(V("J32"), 0, 1)
    fill(V("TR"), 1028, 4, 32)

    def fills():
        fill(V("IDT"), 0, 1)
        for t in (1, 2):
            fill(V("RT%d" % t, 32, 40), 4)

    def constants():
        for c in range(0, 416, 104):
            ms(V("ZB", c, c + 104), 0.0)
        ms(V("ZERO"), 0.0)
        ms(V("W1", 0, 256), 0.0)
        ms(V("BAR"), 0.0)
        ms(V("BAR", 4, 33, 4), -BIG - 4.0)
        ms(V("BAR", 1, 32, 4), 1.5)
        ms(V("BAR", 3, 32, 4), BIG)
        ts(V("SEGT"), V("J4", 0, 40), 1.5, A.is_gt)
        lin(V("SEGT", 4, 33, 4), V("TR"))
        ts(V("MASK"), V("J16"), p15, A.is_equal)
        ts(V("SEG16"), V("J16"), 1.0, A.min)
        ts(V("SUF"), V("J32"), p31, A.is_ge)
        ts(V("KCOL", 1, 2), kcol, 8.0, A.mult, p4, A.add)
        ts(V("KCOL", 2, 3), p15, 4.0, A.mult)
        ts(V("DUP"), V("DUPI"), V("KCOL", 2, 3), A.add)
        ts(V("PERM"), V("PERMI"), V("KCOL", 1, 2), A.add)
        ts(V("PV"), V("PERMI"), p4, A.add)
        ts(V("XEO", 4, 5), V("PF32", 2, 3), 1.0, A.mult)
        lin(V("XEO", 0, 1), V("PF32", 2, 3), -1.0, 1.0)
        ts(V("GD", 0, 1), V("PF32", 3, 4), 8.0, A.mult, float(-P * me), A.add)
        for k in range(4):
            ms(blk(k, "BC", 0, 1), float(255 + 64 * others.index(k)) if k != me else 0.0)

    def prep_lists(t, out):
        b = bufs(t)
        for h in range(2):
            ts(b("RL", 32 * h, 32 * h + 32), V("RAW%d" % t, h, 64, 2), V("SL", 0, 1), A.max, V("SL", 1, 2), A.min)
        for h in range(2):
            tr(b("T2", 32 * h, 32 * h + 32), b("RL", 32 * h, 32 * h + 32))
        for h in range(2):
            scan(b("SCL", 32 * h, 32 * h + 32), V("SEG4", 0, 32), b("T2", 32 * h, 32 * h + 32), A.mult, A.add)
        for h in range(2):
            ts(V(out, 4 * h, 4 * h + 4), b("SCL", 32 * h + 3, 32 * h + 16, 4), V("SL", 2, 3), A.subtract)

    def prep_ties(t):
        b = bufs(t)
        for h in range(2):
            tt(b("EQN", 32 * h, 32 * h + 32), b("RL", 32 * h, 32 * h + 32), V("RAW%d" % t, h, 64, 2), A.is_equal)
        lin(b("KQN"), b("EQN"), scale=V("KCOL", 0, 1))
        tr(b("TK"), b("KQN"))
        scan(b("SK"), V("SEG4"), b("TK"), A.mult, A.add)
        scan(b("PK"), V("PKC"), b("SK", 3, 64, 4), A.mult, A.add)
        tc(V("MSG2", t - 1, t), b("PK", 15, 16))

    def own_columns(t):
        b = bufs(t)
        tc(b("LCN"), V("MSG1") if t == 1 else V("LS2"))
        for k in [me] + others:
            act(blk(k, "OL%d" % t), blk(me, "LCN%d" % t))
        lin(blk(me, "CO%d" % t), blk(me, "LCN%d" % t), bias=float(P * me))
        lin(b("OB"), b("OL"), -1.0, V("BC", 0, 1))
        tt(b("CD"), b("LCN"), b("OL"), A.subtract)
        lin(b("CG"), b("CD"), bias=V("GD", 0, 1))

    def decode_ties():
        slot = {d: i for i, d in enumerate(others + [me])}
        tc(V("KC", 0, 6), V("LM2"))
        tc(V("KC", 6, 8), V("MSG2"))
        for c in range(8):
            ts(V("KD", c, 64, 8), V("KC"), 2 * (7 - c), A.logical_shift_right, 3, A.bitwise_and)
        tc(V("KF"), V("KD"))
        ka = zb(0, 0, 64)
        for d in range(4):
            for s in range(4):
                if s != d:
                    i = (s - me) % 4
                    lin(sub(ka, 16 * i, 16 * i + 16, d), blk(s, "KF", 16 * slot[d], 16 * slot[d] + 16))

    def tie_flags(t):
        ka, o = zb(0, 0, 64), 8 * (t - 1)
        for i in range(4):
            if i:
                tt(sub(zb(t, 80, 32), i, 32, None, 4), sub(ka, 16 * i + o, 16 * i + o + 8), sub(ka, o, o + 8), A.is_lt)
            lin(V("KK%d" % t, 8 * i, 8 * i + 8), sub(ka, 16 * i + o, 16 * i + o + 8), -1.0, 4.0)

    def value_rows(t):
        b = bufs(t)
        gata(b("V4"), b("U", 0, 8), V("PV"))
        op("a", lambda: g.scalar.activation(ap(b("AB")), ap(b("V4")), AF.Abs, scale=STEP), [b("V4")], [b("AB")], 32)
        gata(b("VR"), V("IDT"), b("LU"))

    def thresholds(t):
        b = bufs(t)
        ts(b("AC"), b("AB"), TINY, A.add)
        tt(b("DE"), b("AC"), zb(t, 80, 32), A.mult)
        tt(b("VA"), b("V4"), b("DE"), A.subtract)

    def scores_out(t):
        b = bufs(t)
        tti(b("G"), V("S%d" % (t - 1)), b("LU"), V("MASK"), A.mult)
        scan(b("SG"), V("SEG16"), b("G"), A.mult, A.add)
        lin(b("U", 0, 8), b("SG", 15, 128, 16))
        return spread(b("U", 0, 8), lambda s: b("U", 8 + 8 * s, 16 + 8 * s), "v%d" % t, "lv%d" % t, b("U", 8, 32))

    def prefix(x, add, ni, eb, tb, ec):
        scan(sub(ni, 0, 8), x, add)
        tr(tb, ni)
        scan(sub(eb, 1, 33), tb, V("ZERO", 0, 32))
        tr(ec, sub(eb, 0, 32))

    def choose_and_send(t):
        b = bufs(t)
        worse = zb(t, 112, 64)
        tti(sub(worse, 0, 32), b("U"), V("PERM"), b("VA"), A.is_gt)
        scan(b("NI"), worse, V("BAR"))
        scan(b("BT", 0, 33), V("SEGT", 0, 33), sub(worse, 0, 33), A.mult, A.max)
        tr(b("RT", 0, 32), b("NI", 32, 64))
        op("a", lambda: g.scalar.activation(ap(b("TJ", 0, 33)), ap(b("RT", 0, 33)), AF.Copy, accum_out=ap(b("TA1"))),
           [b("RT", 0, 33)], [b("TJ", 0, 33), b("TA1")], 50)
        tt(b("AA"), b("BT", 4, 33, 4), b("NI", 4, 33, 4), A.subtract)
        scan(b("SFX"), b("RT", 0, 32), V("SUF"), A.add, A.mult)
        ts(b("OF"), b("AA"), b("TA1"), A.subtract, b("SFX", 31, 32), A.add)
        op("v", lambda: g.vector.tensor_copy(ap(b("W")).indirect(ap(b("OF"))), ap(b("VR"))), [b("VR"), b("OF")], [b("W")], 450)
        gat(b("WD", 0, 64), b("W", 0, 256), V("DUP", 0, 4))
        gata(b("WD", 64, 128), b("W", 0, 256), V("DUP", 4, 8))
        tr(b("TW"), b("WD"))
        cols = {d: (4 * i, 4 * i + 4) for i, d in enumerate(others)}
        pf = "PF%d" % t
        alone = me // 2 * 2 + 1 - me % 2
        for d in [d for d in others if d != alone] + [alone]:
            lo, hi = cols[d]
            tt(blk(d, pf, lo, hi), blk(d, "TW%d" % t, 0, 128, 32), blk(d, "TW%d" % t, 16, 128, 32), A.add)
            k = d // 2 * 2 + 1 - d % 2
            if d == alone:
                tt(blk(k, pf, lo, hi), blk(d, "TW%d" % t, 0, 128, 32), blk(d, "TW%d" % t, 16, 128, 32), A.add)
            else:
                act(blk(k, pf, lo, hi), blk(d, pf, lo, hi))
        for half in (me // 2, 1 - me // 2):
            own = [cols[d] for d in others if d // 2 == half]
            lo, hi = min(own)[0], max(own)[1]
            for h in (half, 1 - half):
                tc(V("PO%d" % t, lo, hi, 1, 64 * h, 64 * h + 64), V(pf, lo, hi, 1, 64 * half, 64 * half + 64))
        pick(b("SQ"), b("SS"), V("QO%d" % (t - 1)), V("QS%d" % (t - 1)), b("PO"))
        each("SQ%d" % t, 64, "QW%d" % (t - 1), "c%d" % t, "lc%d" % t)
        return each("SS%d" % t, 64, "QP%d" % (t - 1), "s%d" % t, "ls%d" % t, 3)

    def own_list(t):
        b = bufs(t)
        mk = lambda name, *a: blk(me, name + str(t), *a)
        tt(b("M16"), b("U", 0, 16), b("U", 16, 32), A.max)
        tt(b("MM"), b("M16", 0, 8), b("M16", 8, 16), A.max)
        for i in range(4):
            tt(b("EQ", 8 * i, 8 * i + 8), b("U", 8 * i, 8 * i + 8), b("MM"), A.is_equal)
        tt(b("KEY"), b("EQ"), b("KK"), A.mult)
        tt(b("K16"), b("KEY", 0, 16), b("KEY", 16, 32), A.max)
        tt(b("KM"), b("K16", 0, 8), b("K16", 8, 16), A.max)
        wb, i2 = zb(t, 72, 8), zb(t, 0, 32)
        for i, s in enumerate(others):
            tt(sub(wb, 0, 8, s), mk("KEY", 8 * i + 8, 8 * i + 16), mk("KM"), A.is_equal)
        prefix(wb, V("ZERO", 0, 8), i2, zb(t, 32, 40), b("TB2"), b("EC2"))
        lin(b("NW"), wb, -1000.0, 1000.0)
        tt(b("NP"), sub(i2, 0, 8), b("NW"), A.add)
        tt(b("BP"), sub(i2, 0, 8), b("OB"), A.add)
        keep = b("VAL", 16, 24)
        ts(keep, b("NP"), b("EC2", 7, 8), A.add, float(CAPP), A.is_le)
        ts(b("SV"), b("BP"), b("EC2", 7, 8), A.add)
        tt(b("VAL", 8, 16), keep, b("CG"), A.mult)
        tt(b("VAL", 0, 8), keep, b("SV"), A.mult)
        for i, s in enumerate(others):
            lin(mk("BK", 24 * i, 24 * i + 24), blk(s, "VAL%d" % t))
            lin(mk("KQ", 8 * i + 8, 8 * i + 16), mk("BK", 24 * i + 16, 24 * i + 24))
        tt(mk("SA"), mk("BK", 0, 24), mk("BK", 24, 48), A.add)
        tt(mk("SB"), mk("BK", 48, 56), mk("LCN"), A.add)
        tt(mk("KS"), mk("SA", 16, 24), mk("BK", 64, 72), A.add)
        tt(mk("XC"), mk("SA", 0, 8), mk("SB"), A.add)
        lin(mk("KQ", 0, 8), mk("KS"), -1.0, 1.0)
        for j in range(4):
            lin(mk("A2", 8 * j, 8 * j + 8), mk("XC"), scale=blk(me, "XEO", 4 * (j % 2), 4 * (j % 2) + 1))
        tr(mk("TA"), mk("A2"))
        tt(mk("XT"), mk("TA", 0, 32, 2), mk("TA", 1, 32, 2), A.add)
        half = me // 2
        for k in (2 * half, 2 * half + 1):
            tc(blk(k, "XO%d" % t), mk("XT"))
        tc(V("XO%d" % t, p0=64 - 64 * half, p1=128 - 64 * half), V("XO%d" % t, p0=64 * half, p1=64 * half + 64))
        tt(mk("PP"), mk("KQ"), mk("U"), A.mult)
        tt(mk("P16"), mk("PP", 0, 16), mk("PP", 16, 32), A.add)
        tt(mk("PA"), mk("P16", 0, 8), mk("P16", 8, 16), A.add)
        pr = V("PR%d" % t, 0, 256, 1, 0, 1)
        dma("s", ap(pr), ap(mk("PA")), [mk("PA")], [pr])
        op("g", lambda: g.partition_broadcast(ap(b("PB")), ap(pr), 128), [pr], [b("PB")], 1024)

    def own_choice(t):
        mk = lambda name, *a: blk(me, name + str(t), *a)
        tt(mk("CA"), mk("BK", 56, 64), mk("CO"), A.add)
        tt(mk("CH"), mk("SA", 8, 16), mk("CA"), A.add)
        dma("s", T.ch[t - 1:t, :], ap(mk("CH")), [mk("CH")], [])

    def products(t, i, arrived):
        q, s, n, o = ("QW", "QP", 192, 256) if arrived else ("QO", "QS", 256, 0)
        r = mm(i if arrived else 4 + i, n, V("AQ", 128 * i, 128 * i + 128), V("AP", 128 * i, 128 * i + 128), V(q + str(t - 1)), V(s + str(t - 1)))
        act(V("Z%d" % t, 448 * i + o, 448 * i + o + n), r, 0.05)

    def new_columns(t):
        b = bufs(t)
        for i in range(4):
            products(t, i, True)
        rs, first, wide = {}, None, 3

        def choose(i, lo, hi):
            tti(b("HT", 4 * lo + i, 4 * hi, 4), b("Z", 448 * i, 448 * i + 448), b("XO", lo // 16, hi // 16),
                V("E%d" % t, 4 * lo + i, 4 * hi, 4), A.add)
        for i in range(wide):
            choose(i, 0, P)
        for i in range(wide, 4):
            choose(i, 0, 128)
            choose(i, 128, P)
        for f in range(2):
            lo, hi = 128 * f, 128 * f + 128
            first = qz(V("QO%d" % t, lo, hi), V("QS%d" % t, lo, hi), b("HT", 512 * f, 512 * f + 512))
            rs[f] = mm(4 + f, 128, V("UQ"), V("UP"), V("QO%d" % t, lo, hi), V("QS%d" % t, lo, hi))
            if t == 2:
                yp = mm(6 + f, 128, V("WQ"), V("WP"), V("QO2", lo, hi), V("QS2", lo, hi))
                dma("s", T.oc[:, 4 * lo:4 * hi], ap(V("QO2", lo, hi)).bitcast(dt.uint8), [V("QO2", lo, hi)], [])
                for k in range(4):
                    sc = V("QS2", lo, hi, 1, 32 * k, 32 * k + 4)
                    dma("s", T.osc[4 * k:4 * k + 4, lo:hi], ap(sc), [sc], [])
                lin(V("YB", lo, hi), yp)
                dma("a", T.y[:, lo:hi], ap(V("YB", lo, hi)), [V("YB", lo, hi)], [], dur=LOCAL + 0.6)
        hold[0] = (first,)
        for f in range(2):
            tt(V("S%d" % t, 128 * f, 128 * f + 128), rs[f], b("PB", 128 * f, 128 * f + 128), A.add)
        hold[0] = ()
        if t == 2:
            row = V("S2", 0, 256, 1, 0, 1)
            dma("s", T.g[:], ap(row), [row], [])

    prep_lists(1, "MSG1")
    sent = spread(V("MSG1"), lambda s: V("LM1", 8 * s, 8 * s + 8), "m1", "lm1", V("LM1"))
    w = 4
    while w < 512:
        act(V("UT", w, 2 * w), V("UT", 0, w))
        w *= 2
    qz(V("UQ"), V("UP"), V("UT"))
    qz(V("QO0"), V("QS0"), V("E0"))
    act(V("S0"), mm(0, 256, V("UQ"), V("UP"), V("QO0"), V("QS0")))
    prep_lists(2, "LS2")
    hold[0] = (sent,)
    ts(V("KCOL", 0, 1), V("PF32", 5, 6), 0.0, A.is_equal, kcol, A.mult)
    prep_ties(1)
    prep_ties(2)
    ties = spread(V("MSG2"), lambda s: V("LM2", 2 * s, 2 * s + 2), "m2", "lm2", V("LM2"))
    load("s", V("AT", 0, 1024), T.a[:, 0:1024], LONG, [ties])
    fills()
    constants()
    hold[0] = ()
    for d in [me] + others:
        tc(blk(d, "LU1"), blk(me, "MSG1") if d == me else blk(me, "LM1", 8 * others.index(d), 8 * others.index(d) + 8))
    tc(blk(me, "LU2"), blk(me, "LS2"))
    scores = scores_out(1)
    load("s", V("AT", 1024, 2048), T.a[:, 1024:2048], LONG, [scores])
    load("s", V("E1"), T.e1[:], LONG, [scores])
    own_columns(1)
    for i, d in enumerate(others):
        dma("s", ap(V("ST2", 2 * i, 2 * i + 2)), ap(blk(d, "LS2")), [blk(d, "LS2")], [V("ST2", 2 * i, 2 * i + 2)])
    hold[0] = (scores - 1,)
    value_rows(1)
    hold[0] = ()
    decode_ties()
    tie_flags(1)
    thresholds(1)
    sent = choose_and_send(1)
    each("ST2", 2, "LC2", "m3", "lm3")
    for i, d in enumerate(others):
        dma("s", ap(blk(d, "LU2")), ap(V("LC2", 2 * i, 2 * i + 2)), [V("LC2", 2 * i, 2 * i + 2)], [blk(d, "LU2")])
    hold[0] = (sent,)
    for i in range(4):
        qz(V("AQ", 128 * i, 128 * i + 128), V("AP", 128 * i, 128 * i + 128), V("AT", 512 * i, 512 * i + 512))
        products(1, i, False)
    hold[0] = ()
    own_list(1)
    new_columns(1)
    scores = scores_out(2)
    load("s", V("WT"), T.w[:], LONG, [scores])
    load("s", V("E2"), T.e2[:], LONG, [scores])
    hold[0] = (scores - 1,)
    tie_flags(2)
    value_rows(2)
    thresholds(2)
    for i in range(4):
        products(2, i, False)
    ms(V("W2", 0, 256), 0.0)
    own_columns(2)
    own_choice(1)
    hold[0] = ()
    sent = choose_and_send(2)
    hold[0] = (sent,)
    qz(V("WQ"), V("WP"), V("WT"))
    hold[0] = ()
    own_list(2)
    own_choice(2)
    new_columns(2)
    lay()
    for sem in sorted(total):
        wait("s", [(sem, total[sem], {})])
